import numpy as np
CORES = [22,38,54,62,70,110,23,39,55,63,71,111]
N = 12
T, KB = 2048, 16
CAPP = 512
def entries(a): return a.T.reshape(-1)
def pack(v, P): return np.ascontiguousarray(np.asarray(v, np.int32).reshape(-1, P).T)
def order(K):
    return np.argsort(K, kind="stable")
def most(K):
    o = order(K); return int(np.bincount(o // T * N + np.arange(N * T) // T, minlength=N * N).max())
def lists(rng, how):
    i, G = np.arange(N), T // CAPP
    if how == "uniform":
        for again in range(50):
            K = rng.integers(0, KB, (N, T))
            if most(K.reshape(-1)) <= CAPP: break
        else: K = np.broadcast_to(np.arange(T) % KB, (N, T)).copy()
    else:
        if how == "uneven":
            t = rng.integers(0, CAPP + 1, N)
            if t.sum() < T: t = CAPP - t
            t[0] = CAPP; w = np.diff(np.minimum(np.cumsum(t), T), prepend=0); L = w[(rng.permutation(N)[:, None] - rng.permutation(N)) % N]
        else:
            w = np.zeros(N, int); w[(G * (ord(how[-1]) - 97) + np.arange(G)) % N] = CAPP; L = w[(i[:, None] - i) % N]
        a = N - 1 - np.argmax(L[::-1] > 0, axis=0)
        m = np.minimum(rng.integers(1, CAPP, N - 1), L[a[:-1], i[1:]])
        v = np.nonzero((L[a[:-1], i[:-1]] == CAPP) & (L[a[:-1], i[1:]] == CAPP) & (a[:-1] != np.append(-1, a[:-2])))[0]
        if len(v): m[rng.choice(v)] = CAPP
        C = L.copy(); C[a[:-1], i[:-1]] += m; C[a[:-1], i[1:]] -= m
        kv = np.sort(rng.permutation(KB)[:N]); K = np.stack([rng.permutation(np.repeat(kv, c)) for c in C]); K[::3] = np.sort(K[::3], axis=1)
    return {"key": np.stack([pack(k, 16) for k in K])}
def setup_inputs(rng):
    return dict({"x": rng.standard_normal((N, 128, T), dtype=np.float32)}, **lists(rng, "uniform"))
def setup_inputs_fulla(rng):
    d = setup_inputs(rng); d.update(lists(rng, "fulla"))
    for k in ("x",): d[k] = (d[k].astype(np.float32) * 1048576.0).astype(d[k].dtype)
    return d
def setup_inputs_fullb(rng):
    d = setup_inputs(rng); d.update(lists(rng, "fullb"))
    for k in ("x",): d[k] = (d[k].astype(np.float32) * (1 / 1024.0)).astype(d[k].dtype)
    return d
def setup_inputs_fullc(rng):
    d = setup_inputs(rng); d.update(lists(rng, "fullc"))
    return d
def setup_inputs_uneven(rng):
    d = setup_inputs(rng); d.update(lists(rng, "uneven"))
    return d
def check_inputs(x):
    bad = []
    if x["key"].min() < 0 or x["key"].max() >= KB: bad.append("key out of range")
    if most(np.concatenate([entries(a) for a in x["key"]])) > CAPP: bad.append("more than CAPP columns go from one rank to one rank")
    return bad
def reference(x, key):
    X = np.concatenate(list(x), axis=1); K = np.concatenate([entries(a) for a in key])
    Y = X[:, order(K)]
    return {"y": np.stack([Y[:, T * r:T * r + T] for r in range(N)])}

@@ -1,0 +1,394 @@
+from concourse.bass import DstId, RemoteDMATransfer
+from concourse.mybir import AluOpType as OP, AxisListType, ActivationFunctionType
+
+N, W, CAP = 12, 2048, 512
+F32, F16, I32, U16 = "float32", "float16", "int32", "uint16"
+SCRATCH = {
+    "land": ("sbuf", [128, N * CAP], F32), "slots": ("sbuf", [128, (N - 1) * CAP], F32),
+    "xin": ("sbuf", [128, W], F32), "xs": ("sbuf", [128, W + CAP], F32), "yb": ("sbuf", [128, W], F32),
+    "ki": ("sbuf", [128, 128], I32), "erow": ("sbuf", [128, 256], F16), "el": ("sbuf", [128, 256], F16),
+    "gl": ("sbuf", [128, 128], U16), "sl": ("sbuf", [128, N * 32], U16), "ol": ("sbuf", [128, 128], U16),
+    "ed": ("dram", [N, 128, 2], F16),
+}
+for _i in range(8):
+    SCRATCH["b%d" % _i] = ("psum", [128, 512], F32)
+_TILES = {
+    F16: (("kh", 128), ("oh", 256), ("fs", 256), ("mk", 256), ("sbase", 32), ("lq", 2048), ("rq", 2048), ("z2", N),
+          ("selv", 128), ("c16h", 128), ("cch", 128), ("bo", 128), ("gt", 128), ("le", 128), ("lb", 128), ("te0", 256),
+          ("te1", 256), ("onh", 128), ("on8", 128), ("r1", 36), ("r2", 36), ("zd", 2)),
+    F32: (("lhf", 32), ("z1", N), ("pf", 1), ("vcol", 1), ("kcol", 2), ("kc", 128), ("c16", 128), ("cc", 128),
+          ("jcol", 16), ("dcon", N), ("qb", 128), ("qpat", 128), ("rm", N), ("rcol", 36), ("mka", 36), ("mkb", 36),
+          ("rb", 2), ("onf", 128), ("ngf", 128), ("pa", 36), ("pb", 36), ("cols", 6), ("u", 2), ("zm", 2), ("lr", 4),
+          ("lxf", 8), ("t1", 2), ("t2", 2), ("dl", 2), ("rg", 1024), ("lg", 512), ("off", 128)),
+    I32: (("posi", 16), ("lh", 32), ("cmp", 128), ("cma", 128), ("pi", 1), ("pk", 2), ("li", 4), ("lx", 8)),
+}
+_AT = {}
+for _dt, _ts in _TILES.items():
+    _o = 0
+    for _n, _w in _ts:
+        _AT[_n] = ("m_" + _dt, _o, _w, _dt)
+        _o += (_w + 31) // 32 * 32
+    SCRATCH["m_" + _dt] = ("sbuf", [128, _o], _dt)
+NSEM = 110
+SEMAPHORES = ["earr", "arr", "sent", "esent"] + ["fw%d" % i for i in range(5)] + ["s%d" % i for i in range(NSEM)]
+
+
+def _layout(core, T, topo):
+    chips = sorted(set(topo.chip(c) for c in T.cores))
+    rk = dict((h, sorted(c for c in T.cores if topo.chip(c) == h)) for h in chips)
+    hp = {}
+    for h in chips:
+        far = [t for t in T.cores if topo.chip(t) != h]
+        cand = []
+        for c in range(112):
+            if topo.chip(c) == h and T.rank_of(c) is None and topo.die(c) != topo.die(rk[h][0]):
+                if all(topo.may_write(c, t) for t in far):
+                    cand.append(c)
+        hp[h] = cand
+    return chips, rk, hp
+
+
+def _order(core_chip, k, chips, rk):
+    ci = chips.index(core_chip)
+    out = []
+    for o in range(1, len(chips)):
+        h = chips[(ci + o) % len(chips)]
+        out.append((rk[h][k], rk[h][1 - k]))
+    return out
+
+
+def _helper(g, core, T, topo, chips, rk, hp):
+    h = topo.chip(core)
+    if h not in hp or core not in hp[h][:2]:
+        return
+    k = hp[h].index(core)
+    src = T.rank_of(rk[h][k])
+    pairs = _order(h, k, chips, rk)
+    for i, (_, dst) in enumerate(pairs):
+        rid, pid, _e = topo.addr(dst)
+        g.wait_ge(T.sem["fw%d" % i], 8)
+        g.remote_dma(T.land[:, src * CAP:(src + 1) * CAP], T.land[:, i * CAP:(i + 1) * CAP], T.sem.arr, T.sem.sent,
+                     pid, rid, topo.mask(core, dst))
+    g.wait_ge(T.sem.sent, 8 * len(pairs))
+
+
+def rank_program(g, core, T, topo):
+    chips, rk, hp = _layout(core, T, topo)
+    r = T.rank_of(core)
+    if r is None:
+        return _helper(g, core, T, topo, chips, rk, hp)
+    chip = topo.chip(core)
+    kk = rk[chip].index(core)
+    mate = rk[chip][1 - kk]
+    helper = hp[chip][kk]
+    pairs = _order(chip, kk, chips, rk)
+    lo = topo.mask(core, pairs[0][0])
+    hi = topo.mask(core, helper) & ~lo
+
+    V, S, P, Y = g.vector, g.scalar, g.tensor, g.sync
+    q = {"v": V, "s": S, "t": P, "g": g, "y": Y}
+    seen = dict((n, {}) for n in q)
+    toks = []
+
+    def B(name, a=0, b=None, p=128):
+        buf, o, w, _ = _AT[name]
+        return T[buf][0:p, o + a:o + (w if b is None else b)]
+
+    def new():
+        t = {"s": "s%d" % len(toks), "n": 0, "w": False}
+        toks.append(t)
+        return t
+
+    def need(n, deps):
+        for t in deps:
+            if seen[n].get(t["s"], 0) < t["n"]:
+                q[n].wait_ge(T.sem[t["s"]], t["n"])
+                seen[n][t["s"]] = t["n"]
+                t["w"] = True
+
+    def inc(inst, t, k=1):
+        inst.then_inc(T.sem[t["s"]], k)
+        t["n"] += k
+        return t
+
+    def ts(out, in0, s1, op0, t, s2=None, op1=None):
+        if op1 is None:
+            return inc(V.tensor_scalar(out, in0, s1, None, op0), t)
+        return inc(V.tensor_scalar(out, in0, s1, s2, op0, op1), t)
+
+    tk, tx = new(), new()
+    inc(Y.dma_start(T.ki[0:16, :], T.key[:]), tk, 16)
+    inc(Y.dma_start(T.xin[:], T.x[:]), tx, 16)
+
+    def iota(name, pat, base, cm):
+        if _AT[name][3] == I32:
+            return inc(g.iota(B(name), pat, base, cm), new())
+        return inc(g.iota(B(name), pat, base, cm, allow_small_or_imprecise_dtypes=True), new())
+    i_pi = iota("pi", [[0, 1]], 0, 1)
+    i_cmp = iota("cmp", [[1, 128]], 0, -1)
+    i_kc = iota("kc", [[1, 8], [0, 16]], 0, 0)
+    i_c16 = iota("c16", [[0, 8], [1, 16]], 0, 0)
+    i_cc = iota("cc", [[1, 128]], 0, 0)
+    i_j = iota("jcol", [[1, 16]], 0, 16)
+    i_rm = iota("rm", [[1, N]], 0, -1)
+    i_dc = iota("dcon", [[2048, N]], 0, 0)
+    i_qb = iota("qb", [[16, 128]], 0, 0)
+    i_rc = iota("rcol", [[0, 3], [1, N]], 0, 0)
+
+    need("v", [i_pi])
+    c1 = new()
+    ts(B("pk", 0, 1), B("pi"), 4, OP.arith_shift_right, c1)
+    ts(B("pk", 1, 2), B("pi"), 15, OP.bitwise_and, c1)
+    inc(V.tensor_copy(B("pf"), B("pi")), c1)
+    need("v", [i_cmp])
+    ts(B("cma"), B("cmp"), 15, OP.bitwise_and, c1)
+    need("v", [c1])
+    c2 = new()
+    ts(B("selv"), B("cma"), 0, OP.is_equal, c2)
+    ts(B("kcol", 0, 1), B("pk", 0, 1), 0, OP.add, c2)
+    ts(B("kcol", 1, 2), B("pk", 0, 1), 8, OP.add, c2)
+    inc(V.tensor_copy(B("vcol"), B("pk", 1, 2)), c2)
+    need("v", [c2, i_c16])
+    c3 = new()
+    for h, te in enumerate(("te0", "te1")):
+        ts(B(te, 0, 128), B("c16"), B("kcol", h, h + 1), OP.is_ge, c3)
+        ts(B(te, 128, 256), B("c16"), B("kcol", h, h + 1), OP.is_gt, c3)
+    c5 = new()
+    need("v", [i_kc])
+    ts(B("bo"), B("kc"), B("kcol", 0, 1), OP.is_equal, c5)
+
+    need("v", [tk])
+    a1 = inc(V.tensor_copy(B("kh", p=16), T.ki[0:16, :]), new())
+    need("t", [c2, a1])
+    a2 = inc(P.matmul(T.b0[:, 0:128], B("selv", p=16), B("kh", p=16), True, True), new())
+    need("v", [i_cc, c5])
+    ts(B("gt"), B("kc"), B("kcol", 0, 1), OP.is_gt, c5)
+    ts(B("le"), B("cc"), B("pf"), OP.is_le, c5, -1.0, OP.mult)
+    need("v", [a2])
+    a3, a4 = new(), new()
+    for h in range(2):
+        ts(B("oh", h * 128, h * 128 + 128), T.b0[:, 0:128], B("kcol", h, h + 1), OP.is_equal, a3)
+    need("v", [a3])
+    for h in range(2):
+        o = B("oh", h * 128, h * 128 + 128)
+        inc(V.tensor_tensor_scan(B("fs", h * 128, h * 128 + 128), o, o, 0.0, OP.add, OP.max), a4)
+    cnt = [B("fs", 127, 128), B("fs", 255, 256)]
+    need("t", [a4, c3])
+    P.matmul(T.b5[0:1, 0:256], cnt[0], B("te0"), True, False)
+    a5 = inc(P.matmul(T.b5[0:1, 0:256], cnt[1], B("te1"), False, True), new())
+    need("v", [c5])
+    c6 = new()
+    inc(V.tensor_tensor(B("lb"), B("le"), B("bo"), OP.mult), c6)
+    ts(B("onh"), B("cc"), 0.0, OP.is_ge, c6)
+    need("v", [a5])
+    a6 = inc(V.tensor_copy(T.erow[0:1, :], T.b5[0:1, 0:256]), new())
+    need("y", [a6])
+    a7 = inc(Y.dma_start(T.ed[r], T.erow[0:1, :]), new(), 16)
+    need("g", [a7])
+    far = [t for p in pairs for t in p]
+
+    def did(c):
+        rid, pid, _e = topo.addr(c)
+        return DstId(rid=rid, pnc=pid)
+    g.remote_dma_fused([
+        RemoteDMATransfer(srcs=[T.ed[r]], dsts=[T.ed[r] for _ in far], dst_ids=[did(c) for c in far],
+                          dma_engine_mask=lo, remote_sem=T.sem.earr),
+        RemoteDMATransfer(srcs=[T.ed[r]], dsts=[T.ed[r]], dst_ids=[did(mate)], dma_engine_mask=hi,
+                          remote_sem=T.sem.earr)], local_sem=T.sem.esent)
+    Y.wait_ge(T.sem.earr, 8 * (N - 1))
+    need("y", [a7])
+    e1 = inc(Y.dma_start(T.el[0:N, :], T.ed[:]), new(), 16)
+
+    need("t", [c6])
+    P.matmul(T.b1[:, 0:256], B("bo"), B("fs"), True, False)
+    d1 = inc(P.matmul(T.b1[:, 0:256], B("lb"), B("oh"), False, True), new())
+    P.matmul(T.b2[:, 0:1], B("gt"), cnt[0], True, True)
+    P.matmul(T.b2[:, 1:2], B("onh"), cnt[0], True, False)
+    d2 = inc(P.matmul(T.b2[:, 1:2], B("gt"), cnt[1], False, True), new())
+    need("v", [d1])
+    d3 = inc(V.tensor_tensor(B("mk"), T.b1[:, 0:256], B("oh"), OP.mult), new())
+    need("v", [d2])
+    s16 = B("selv", 0, 16)
+    for h in range(2):
+        ts(B("sbase", h * 16, h * 16 + 16), s16, T.b2[:, h:h + 1], OP.mult, d3)
+    need("t", [d3])
+    P.matmul(T.b3[:, 0:16], B("mk", 0, 128), s16, True, False)
+    P.matmul(T.b3[:, 0:16], B("mk", 128, 256), s16, False, False)
+    P.matmul(T.b3[:, 0:16], B("oh", 0, 128), B("sbase", 0, 16), False, False)
+    d4 = inc(P.matmul(T.b3[:, 0:16], B("oh", 128, 256), B("sbase", 16, 32), False, True), new())
+    c7 = new()
+    inc(V.tensor_copy(B("c16h"), B("c16")), c7)
+    inc(V.tensor_copy(B("cch"), B("cc")), c7)
+    need("v", [d4])
+    d5 = inc(V.tensor_copy(B("posi"), T.b3[:, 0:16]), new())
+    need("v", [d5])
+    d6 = new()
+    ts(B("lh", 0, 16), B("posi"), 15, OP.bitwise_and, d6)
+    ts(B("lh", 16, 32), B("posi"), 4, OP.arith_shift_right, d6)
+    need("v", [d6])
+    d7 = inc(V.tensor_copy(B("lhf"), B("lh")), new())
+    need("v", [d7, c7, i_j])
+    for b in range(4):
+        d8 = new()
+        for v in range(4 * b, 4 * b + 4):
+            ts(B("lq", v * 128, v * 128 + 128), B("c16h"), B("lhf", v, v + 1), OP.is_equal, d8)
+            ts(B("rq", v * 128, v * 128 + 128), B("cch"), B("lhf", 16 + v, 17 + v), OP.is_equal, d8,
+               B("jcol", v, v + 1), OP.mult)
+        need("t", [d8])
+        for v in range(4 * b, 4 * b + 4):
+            m = P.matmul(T.b4[:, 0:128], B("lq", v * 128, v * 128 + 128), B("rq", v * 128, v * 128 + 128), v == 0,
+                         v == 15)
+    d9 = inc(m, new())
+    c8 = new()
+    need("v", [i_rm, i_qb])
+    for a, dst, op, mul in ((0, "r1", OP.is_gt, 1.0), (12, "r1", OP.is_equal, 0.0), (24, "r1", OP.is_equal, 1.0),
+                            (0, "r2", OP.is_le, 1.0), (12, "r2", OP.is_equal, 1.0), (24, "r2", OP.is_equal, -1.0)):
+        ts(B(dst, a, a + N), B("rm"), 0.0, op, c8, mul, OP.mult)
+    ts(B("on8"), B("cc"), 0.0, OP.is_ge, c8, 0.125, OP.mult)
+    ts(B("qpat"), B("qb"), B("vcol"), OP.add, c8)
+    inc(V.memset(T.xs[:, W:W + CAP], 0.0), c8)
+    need("v", [d9])
+    f1 = inc(V.tensor_copy(T.gl[:], T.b4[:, 0:128]), new())
+    f2 = new()
+    f3 = new()
+    need("v", [f1, tx])
+    inc(V.tensor_copy(T.xs[:, 0:W // 2], T.xin[:, 0:W].indirect(T.gl[:, 0:64])), f2)
+    need("s", [f1, tx])
+    inc(S.activation(T.xs[:, W // 2:W], T.xin[:, 0:W].indirect(T.gl[:, 64:128]), ActivationFunctionType.Copy), f3)
+
+    need("t", [e1, c8])
+    P.matmul(T.b5[:, 0:36], T.el[0:N, 0:128], B("r1", p=N), True, False)
+    h1 = inc(P.matmul(T.b5[:, 0:36], T.el[0:N, 128:256], B("r2", p=N), False, True), new())
+    need("v", [h1, i_dc])
+    h2 = new()
+    ts(B("z1"), B("dcon"), T.b5[:, r:r + 1], OP.subtract, h2, T.b5[:, 24 + r:25 + r], OP.min)
+    need("v", [h2])
+    h3 = new()
+    ts(B("z2"), B("z1"), 0.0, OP.max, h3)
+    need("t", [h3])
+    h4 = inc(P.matmul(T.b6[:, 0:N], B("on8"), B("z2"), True, True), new())
+    need("v", [h4])
+    tl = {}
+
+    def mklist(d):
+        tl[d] = new()
+        ts(T.sl[:, d * 32:d * 32 + 32], B("qpat", 0, 32), T.b6[:, d:d + 1], OP.add, tl[d])
+
+    def piece(n, d, out):
+        need(n, [tl[d], f2, f3, c8])
+        src = T.xs[:, 0:W + CAP].indirect(T.sl[:, d * 32:d * 32 + 32])
+        t = new()
+        if n == "v":
+            return inc(V.tensor_copy(out, src), t)
+        return inc(S.activation(out, src, ActivationFunctionType.Copy), t)
+
+    def slot(i):
+        return T.slots[:, i * CAP:(i + 1) * CAP]
+    rd = [(T.rank_of(a), T.rank_of(b)) for a, b in pairs]
+    mr = T.rank_of(mate)
+    mine = T.land[:, r * CAP:(r + 1) * CAP]
+    mklist(rd[0][0])
+    for i in range(5):
+        mklist(rd[i][1])
+        mklist(rd[i + 1][0] if i < 4 else mr)
+        ta = piece("s", rd[i][0], slot(2 * i))
+        tb = piece("v", rd[i][1], slot(2 * i + 1))
+        need("g", [ta, tb])
+        g.remote_dma_fused([
+            RemoteDMATransfer(srcs=[slot(2 * i + 1)], dsts=[T.land[:, i * CAP:(i + 1) * CAP]], dst_ids=[did(helper)],
+                              dma_engine_mask=hi, remote_sem=T.sem["fw%d" % i]),
+            RemoteDMATransfer(srcs=[slot(2 * i)], dsts=[mine], dst_ids=[did(pairs[i][0])],
+                              dma_engine_mask=lo, remote_sem=T.sem.arr)], local_sem=T.sem.sent)
+    tm = piece("s", mr, slot(10))
+    need("g", [tm])
+    rid, pid, _e = topo.addr(mate)
+    g.remote_dma(mine, slot(10), T.sem.arr, T.sem.sent, pid, rid, hi)
+    mklist(r)
+    town = piece("v", r, mine)
+
+    k1 = new()
+    need("v", [i_rc])
+    ts(B("mka"), B("rcol"), B("kcol", 0, 1), OP.is_equal, k1)
+    ts(B("mkb"), B("rcol"), B("kcol", 1, 2), OP.is_equal, k1)
+    ts(B("rb"), B("kcol"), float(CAP), OP.mult, k1)
+    inc(V.memset(B("onf"), 1.0), k1)
+    inc(V.memset(B("ngf"), -1.0), k1)
+    need("v", [k1])
+    k2 = new()
+    inc(V.tensor_tensor(B("pa"), T.b5[:, 0:36], B("mka"), OP.mult), k2)
+    inc(V.tensor_tensor(B("pb"), T.b5[:, 0:36], B("mkb"), OP.mult), k2)
+    need("v", [k2])
+    k3 = new()
+    for j in range(3):
+        for x, p in enumerate(("pa", "pb")):
+            inc(V.tensor_reduce(B("cols", 2 * j + x, 2 * j + x + 1), B(p, 12 * j, 12 * j + 12), AxisListType.X, OP.add),
+                k3)
+    need("v", [k3])
+    k4 = new()
+    ts(B("u"), B("cols", 0, 2), -1.0, OP.mult, k4, float(W * r), OP.add)
+    need("v", [k4])
+    k5 = new()
+    inc(V.tensor_tensor(B("zm"), B("u"), B("cols", 4, 6), OP.min), k5)
+    ts(B("lr", 0, 2), B("u"), -1.0, OP.mult, k5)
+    inc(V.tensor_tensor(B("lr", 2, 4), B("cols", 4, 6), B("u"), OP.subtract), k5)
+    inc(V.tensor_tensor(B("t1"), B("u"), B("cols", 2, 4), OP.add), k5)
+    need("v", [k5])
+    k6 = new()
+    ts(B("zd"), B("zm"), 0.0, OP.max, k6)
+    need("t", [k6])
+    k7 = inc(P.matmul(T.b7[:, 0:2], B("bo"), B("zd"), True, True), new())
+    k8 = new()
+    ts(B("li"), B("lr"), 0.0, OP.max, k8, float(W), OP.min)
+    inc(V.tensor_tensor(B("t2"), B("t1"), B("rb"), OP.add), k8)
+    need("v", [k8])
+    k9 = new()
+    ts(B("lx", 0, 4), B("li"), 4, OP.arith_shift_right, k9)
+    ts(B("lx", 4, 8), B("li"), 15, OP.bitwise_and, k9)
+    need("v", [k9])
+    k10 = inc(V.tensor_copy(B("lxf"), B("lx")), new())
+    need("v", [k7])
+    inc(V.tensor_tensor(B("dl"), B("t2"), T.b7[:, 0:2], OP.subtract), k10)
+    need("v", [k10])
+    k11 = new()
+    for x in range(2):
+        dl = B("dl", x, x + 1)
+        for e in range(2):
+            o = x * 512 + e * 256
+            hs, ls = 2 * e + x, 4 + 2 * e + x
+            ts(B("rg", o, o + 128), B("cc"), B("lxf", hs, hs + 1), OP.is_gt, k11, dl, OP.mult)
+            ts(B("rg", o + 128, o + 256), B("cc"), B("lxf", hs, hs + 1), OP.is_equal, k11, dl, OP.mult)
+            o = x * 256 + e * 128
+            ts(B("lg", o, o + 128), B("c16"), B("lxf", ls, ls + 1), OP.is_ge, k11, 1.0 - 2.0 * e, OP.mult)
+    need("t", [k11])
+    for x in range(2):
+        for e in range(2):
+            o = x * 512 + e * 256
+            P.matmul(T.b7[:, 128:256], B("ngf" if e else "onf"), B("rg", o, o + 128), x + e == 0, False)
+            m = P.matmul(T.b7[:, 128:256], B("lg", x * 256 + e * 128, x * 256 + e * 128 + 128),
+                         B("rg", o + 128, o + 256), False, x + e == 2)
+    k12 = inc(m, new())
+    need("v", [k12])
+    k13 = inc(V.tensor_tensor(B("off"), T.b7[:, 128:256], B("qpat"), OP.add), new())
+    need("v", [k13])
+    k14 = inc(V.tensor_copy(T.ol[:], B("off")), new())
+
+    V.wait_ge(T.sem.arr, 8 * (N - 1))
+    S.wait_ge(T.sem.arr, 8 * (N - 1))
+    ty = new()
+    for b in range(4):
+        n = "s" if b % 2 else "v"
+        need(n, [k14, town])
+        src = T.land[:, 0:N * CAP].indirect(T.ol[:, b * 32:b * 32 + 32])
+        out = T.yb[:, b * 512:b * 512 + 512]
+        if n == "v":
+            t = inc(V.tensor_copy(out, src), new())
+        else:
+            t = inc(S.activation(out, src, ActivationFunctionType.Copy), new())
+        need("y", [t])
+        inc(Y.dma_start(T.y[:, b * 512:b * 512 + 512], out), ty, 16)
+    need("y", [ty])
+    g.wait_ge(T.sem.esent, 16)
+    g.wait_ge(T.sem.sent, 16 * 5 + 8)
+    for t in toks:
+        if not t["w"]:
+            need("g", [t])

@@ -1,13 +1,16 @@
 from concourse.bass import DstId, RemoteDMATransfer
 from concourse.mybir import AluOpType as OP, AxisListType, ActivationFunctionType
 
-N, W, CAP = 12, 2048, 512
+N, W, CAP, SIM = 12, 2048, 512, 112
+NEXT = ((3, 4, 1, 2, 5), (5, 2, 3, 4, 0), (0, 5, 4, 1, 3), (4, 0, 5, 2, 1), (1, 5, 0, 3, 2), (1, 4, 2, 0, 3))
+FAR = ((1, 5), (2, 5), (3, 0), (3, 4), (5, 1), (5, 4))
 F32, F16, I32, U16 = "float32", "float16", "int32", "uint16"
 SCRATCH = {
-    "land": ("sbuf", [128, N * CAP], F32), "slots": ("sbuf", [128, (N - 1) * CAP], F32),
+    "land": ("sbuf", [128, N * CAP], F32), "slots": ("sbuf", [128, N * CAP], F32),
     "xin": ("sbuf", [128, W], F32), "xs": ("sbuf", [128, W + CAP], F32), "yb": ("sbuf", [128, W], F32),
     "ki": ("sbuf", [128, 128], I32), "erow": ("sbuf", [128, 256], F16), "el": ("sbuf", [128, 256], F16),
     "gl": ("sbuf", [128, 128], U16), "sl": ("sbuf", [128, N * 32], U16), "ol": ("sbuf", [128, 128], U16),
+    "tq": ("sbuf", [128, 128], F32), "tr": ("sbuf", [128, 212], F16), "th": ("sbuf", [128, 330], F32),
     "ed": ("dram", [N, 128, 2], F16),
 }
 for _i in range(8):
@@ -15,12 +18,12 @@ for _i in range(8):
 _TILES = {
     F16: (("kh", 128), ("oh", 256), ("fs", 256), ("mk", 256), ("sbase", 32), ("lq", 2048), ("rq", 2048), ("z2", N),
           ("selv", 128), ("c16h", 128), ("cch", 128), ("bo", 128), ("gt", 128), ("le", 128), ("lb", 128), ("te0", 256),
-          ("te1", 256), ("onh", 128), ("on8", 128), ("r1", 36), ("r2", 36), ("zd", 2)),
-    F32: (("lhf", 32), ("z1", N), ("pf", 1), ("vcol", 1), ("kcol", 2), ("kc", 128), ("c16", 128), ("cc", 128),
-          ("jcol", 16), ("dcon", N), ("qb", 128), ("qpat", 128), ("rm", N), ("rcol", 36), ("mka", 36), ("mkb", 36),
-          ("rb", 2), ("onf", 128), ("ngf", 128), ("pa", 36), ("pb", 36), ("cols", 6), ("u", 2), ("zm", 2), ("lr", 4),
-          ("lxf", 8), ("t1", 2), ("t2", 2), ("dl", 2), ("rg", 1024), ("lg", 512), ("off", 128)),
-    I32: (("posi", 16), ("lh", 32), ("cmp", 128), ("cma", 128), ("pi", 1), ("pk", 2), ("li", 4), ("lx", 8)),
+          ("te1", 256), ("onh", 128), ("zd", 2)),
+    F32: (("lhf", 32), ("z1", N), ("pf", 1), ("p16", 1), ("vcol", 1), ("kcol", 2), ("jcol", 16), ("pa", 36),
+          ("pb", 36), ("cols", 6), ("u", 2), ("zm", 2), ("lr", 4), ("lxf", 8), ("t1", 2), ("t2", 2), ("dl", 2),
+          ("rg", 1024), ("lg", 512), ("off", 128)),
+    I32: (("posi", 16), ("lh", 32), ("ci", 128), ("c16", 128), ("kc", 128), ("pi", 1), ("pk", 2), ("li", 4),
+          ("lx", 8)),
 }
 _AT = {}
 for _dt, _ts in _TILES.items():
@@ -29,64 +32,81 @@ for _dt, _ts in _TILES.items():
         _AT[_n] = ("m_" + _dt, _o, _w, _dt)
         _o += (_w + 31) // 32 * 32
     SCRATCH["m_" + _dt] = ("sbuf", [128, _o], _dt)
-NSEM = 110
-SEMAPHORES = ["earr", "arr", "sent", "esent"] + ["fw%d" % i for i in range(5)] + ["s%d" % i for i in range(NSEM)]
+NSEM = 120
+SEMAPHORES = (["earr", "arr", "sent", "esent", "tabm", "tabh", "tsent"] + ["fw%d" % i for i in range(8)]
+              + ["s%d" % i for i in range(NSEM)])
 
 
-def _layout(core, T, topo):
+def _plan(T, topo):
     chips = sorted(set(topo.chip(c) for c in T.cores))
     rk = dict((h, sorted(c for c in T.cores if topo.chip(c) == h)) for h in chips)
     hp = {}
     for h in chips:
         far = [t for t in T.cores if topo.chip(t) != h]
-        cand = []
-        for c in range(112):
-            if topo.chip(c) == h and T.rank_of(c) is None and topo.die(c) != topo.die(rk[h][0]):
-                if all(topo.may_write(c, t) for t in far):
-                    cand.append(c)
-        hp[h] = cand
-    return chips, rk, hp
+        hp[h] = [c for c in range(SIM) if topo.chip(c) == h and T.rank_of(c) is None
+                 and topo.die(c) != topo.die(rk[h][0]) and all(topo.may_write(c, t) for t in far)]
+
+    def relay(a, k, die, dst):
+        b = topo.chip(dst)
+        if (chips.index(a), chips.index(b)) not in FAR:
+            return []
+        return [[c for c in range(SIM) if topo.mates(topo.chip(c), b) and topo.die(c) == die
+                 and topo.may_write(c, dst)][k]]
+    groups, jobs, mate, helper = {}, {}, {}, {}
+    for a in chips:
+        for k in range(2):
+            me, hc = rk[a][k], hp[a][k]
+            mate[me], helper[me] = rk[a][1 - k], hc
+            own, oth, last = [], [], []
+            for o in NEXT[chips.index(a)]:
+                d0, d1 = rk[chips[o]][k], rk[chips[o]][1 - k]
+                own.append([me] + relay(a, k, topo.die(me), d0) + [d0])
+                oth.append([me, hc] + relay(a, k, topo.die(hc), d1) + [d1])
+                last = [me] + relay(a, k, topo.die(me), d1) + [d1]
+            m, h = [me, rk[a][1 - k]], CAP // 2
+            grp = [[(own[0], 0, h), (oth[0], 0, h)], [(own[0], h, CAP), (oth[0], h, CAP)]]
+            grp += [[(own[i], 0, CAP), (oth[i], 0, CAP)] for i in (1, 2, 3)]
+            grp += [[(own[4], 0, h), (oth[4], 0, h)], [(own[4], h, CAP), (m, 0, h)], [(last, h, CAP), (m, h, CAP)]]
+            groups[me] = grp
+            for pair in grp:
+                for piece in pair:
+                    for c in piece[0][1:-1]:
+                        jobs.setdefault(c, []).append(piece)
+    return groups, jobs, mate, helper
 
 
-def _order(core_chip, k, chips, rk):
-    ci = chips.index(core_chip)
-    out = []
-    for o in range(1, len(chips)):
-        h = chips[(ci + o) % len(chips)]
-        out.append((rk[h][k], rk[h][1 - k]))
-    return out
+def _mask(topo, src, dst):
+    m = topo.mask(src, dst)
+    if topo.chip(src) == topo.chip(dst):
+        off = [topo.mask(src, c) for c in range(SIM) if topo.same_plane(topo.chip(src), topo.chip(c))][0]
+        return m & ~off
+    return m
 
 
-def _helper(g, core, T, topo, chips, rk, hp):
-    h = topo.chip(core)
-    if h not in hp or core not in hp[h][:2]:
-        return
-    k = hp[h].index(core)
-    src = T.rank_of(rk[h][k])
-    pairs = _order(h, k, chips, rk)
-    for i, (_, dst) in enumerate(pairs):
-        rid, pid, _e = topo.addr(dst)
-        g.wait_ge(T.sem["fw%d" % i], 8)
-        g.remote_dma(T.land[:, src * CAP:(src + 1) * CAP], T.land[:, i * CAP:(i + 1) * CAP], T.sem.arr, T.sem.sent,
-                     pid, rid, topo.mask(core, dst))
-    g.wait_ge(T.sem.sent, 8 * len(pairs))
+def _did(topo, c):
+    rid, pid, _e = topo.addr(c)
+    return DstId(rid=rid, pnc=pid)
 
 
-def rank_program(g, core, T, topo):
-    chips, rk, hp = _layout(core, T, topo)
-    r = T.rank_of(core)
-    if r is None:
-        return _helper(g, core, T, topo, chips, rk, hp)
-    chip = topo.chip(core)
-    kk = rk[chip].index(core)
-    mate = rk[chip][1 - kk]
-    helper = hp[chip][kk]
-    pairs = _order(chip, kk, chips, rk)
-    lo = topo.mask(core, pairs[0][0])
-    hi = topo.mask(core, helper) & ~lo
+def _hop(T, topo, jobs, piece, core, src):
+    path, c0, c1 = piece
+    nx = path[path.index(core) + 1]
+    if nx == path[-1]:
+        r = T.rank_of(path[0])
+        dst, sem = T.land[:, r * CAP + c0:r * CAP + c1], T.sem.arr
+    else:
+        j = jobs[nx].index(piece)
+        dst, sem = T.land[:, j * CAP:j * CAP + c1 - c0], T.sem["fw%d" % j]
+    return RemoteDMATransfer(srcs=[src], dsts=[dst], dst_ids=[_did(topo, nx)],
+                             dma_engine_mask=_mask(topo, core, nx), remote_sem=sem)
 
-    V, S, P, Y = g.vector, g.scalar, g.tensor, g.sync
-    q = {"v": V, "s": S, "t": P, "g": g, "y": Y}
+
+def _n(topo, a, b):
+    return bin(_mask(topo, a, b)).count("1")
+
+
+def _tools(g, T):
+    q = {"v": g.vector, "s": g.scalar, "t": g.tensor, "g": g, "y": g.sync}
     seen = dict((n, {}) for n in q)
     toks = []
 
@@ -113,57 +133,117 @@ def rank_program(g, core, T, topo):
 
     def ts(out, in0, s1, op0, t, s2=None, op1=None):
         if op1 is None:
-            return inc(V.tensor_scalar(out, in0, s1, None, op0), t)
-        return inc(V.tensor_scalar(out, in0, s1, s2, op0, op1), t)
+            return inc(g.vector.tensor_scalar(out, in0, s1, None, op0), t)
+        return inc(g.vector.tensor_scalar(out, in0, s1, s2, op0, op1), t)
+
+    def counters():
+        i1 = inc(g.iota(B("pi"), [[0, 1]], 0, 1), new())
+        i2 = inc(g.iota(B("ci"), [[1, 128]], 0, 0), new())
+        c1 = new()
+        need("v", [i1])
+        ts(B("pk", 0, 1), B("pi"), 4, OP.arith_shift_right, c1)
+        ts(B("pk", 1, 2), B("pi"), 15, OP.bitwise_and, c1)
+        inc(g.vector.tensor_copy(B("pf"), B("pi")), c1)
+        ts(B("p16"), B("pi"), 16, OP.mult, c1)
+        need("v", [i2])
+        ts(B("c16"), B("ci"), 15, OP.bitwise_and, c1)
+        ts(B("kc"), B("ci"), 4, OP.arith_shift_right, c1)
+        need("v", [c1])
+        c2 = new()
+        ts(B("kcol", 0, 1), B("pk", 0, 1), 0, OP.add, c2)
+        ts(B("kcol", 1, 2), B("pk", 0, 1), 8, OP.add, c2)
+        inc(g.vector.tensor_copy(B("vcol"), B("pk", 1, 2)), c2)
+        need("v", [c2])
+
+    def close():
+        for t in toks:
+            if not t["w"]:
+                need("g", [t])
+    return B, new, need, inc, ts, counters, close
+
+
+def _pass_on(g, core, T, topo, jobs, helper):
+    mine = jobs.get(core, [])
+    B, new, need, inc, ts, counters, close = _tools(g, T)
+    own = [c for c in T.cores if helper[c] == core]
+    if own:
+        counters()
+        t = new()
+        for j in range(3):
+            for x in range(2):
+                ts(T.th[:, 36 * x + 12 * j:36 * x + 12 * j + 12], B("ci", 0, N), B("kcol", x, x + 1), OP.is_equal, t)
+        ts(T.th[:, 72:74], B("kcol"), float(CAP), OP.mult, t)
+        inc(g.vector.memset(T.th[:, 74:202], 1.0), t)
+        inc(g.vector.memset(T.th[:, 202:330], -1.0), t)
+        need("g", [t])
+        rid, pid, _e = topo.addr(own[0])
+        g.remote_dma(T.th[:], T.th[:], T.sem.tabh, T.sem.tsent, pid, rid,
+                     topo.mask(core, own[0]) & ~_mask(topo, core, own[0]))
+    sent = 0
+    for i, piece in enumerate(mine):
+        path, c0, c1 = piece
+        at = path.index(core)
+        g.wait_ge(T.sem["fw%d" % i], _n(topo, path[at - 1], core))
+        g.remote_dma_fused([_hop(T, topo, jobs, piece, core, T.land[:, i * CAP:i * CAP + c1 - c0])],
+                           local_sem=T.sem.sent)
+        sent += _n(topo, core, path[at + 1])
+    if own:
+        g.wait_ge(T.sem.tsent, 8)
+    if mine:
+        g.wait_ge(T.sem.sent, sent)
+    close()
+
+
+def rank_program(g, core, T, topo):
+    groups, jobs, mates, helper = _plan(T, topo)
+    r = T.rank_of(core)
+    if r is None:
+        return _pass_on(g, core, T, topo, jobs, helper)
+    mate = mates[core]
+    far = [c for c in T.cores if topo.chip(c) != topo.chip(core)]
+    lo = topo.mask(core, far[0])
+    hi = topo.mask(core, mate) & ~lo
+    mid, mpid, _e = topo.addr(mate)
+    first = T.rank_of(core) < T.rank_of(mate)
+
+    V, S, P, Y = g.vector, g.scalar, g.tensor, g.sync
+    B, new, need, inc, ts, counters, close = _tools(g, T)
 
     tk, tx = new(), new()
     inc(Y.dma_start(T.ki[0:16, :], T.key[:]), tk, 16)
     inc(Y.dma_start(T.xin[:], T.x[:]), tx, 16)
 
-    def iota(name, pat, base, cm):
-        if _AT[name][3] == I32:
-            return inc(g.iota(B(name), pat, base, cm), new())
-        return inc(g.iota(B(name), pat, base, cm, allow_small_or_imprecise_dtypes=True), new())
-    i_pi = iota("pi", [[0, 1]], 0, 1)
-    i_cmp = iota("cmp", [[1, 128]], 0, -1)
-    i_kc = iota("kc", [[1, 8], [0, 16]], 0, 0)
-    i_c16 = iota("c16", [[0, 8], [1, 16]], 0, 0)
-    i_cc = iota("cc", [[1, 128]], 0, 0)
-    i_j = iota("jcol", [[1, 16]], 0, 16)
-    i_rm = iota("rm", [[1, N]], 0, -1)
-    i_dc = iota("dcon", [[2048, N]], 0, 0)
-    i_qb = iota("qb", [[16, 128]], 0, 0)
-    i_rc = iota("rcol", [[0, 3], [1, N]], 0, 0)
+    counters()
+    tab = new()
+    if first:
+        ts(T.tq[:], B("ci"), 16.0, OP.mult, tab, B("vcol"), OP.add)
+        mytab = T.tq[:]
+    else:
+        c12 = B("ci", 0, N)
+        for a, op, mul in ((0, OP.is_gt, 1.0), (12, OP.is_equal, 0.0), (24, OP.is_equal, 1.0),
+                           (36, OP.is_le, 1.0), (48, OP.is_equal, 1.0), (60, OP.is_equal, -1.0)):
+            ts(T.tr[:, a:a + N], c12, B("pf"), op, tab, mul, OP.mult)
+        ts(T.tr[:, 72:200], B("ci"), 0.0, OP.is_ge, tab, 0.125, OP.mult)
+        ts(T.tr[:, 200:212], c12, float(W), OP.mult, tab)
+        mytab = T.tr[:]
+    need("g", [tab])
+    g.remote_dma(mytab, mytab, T.sem.tabm, T.sem.tsent, mpid, mid, topo.mask(core, mate))
 
-    need("v", [i_pi])
-    c1 = new()
-    ts(B("pk", 0, 1), B("pi"), 4, OP.arith_shift_right, c1)
-    ts(B("pk", 1, 2), B("pi"), 15, OP.bitwise_and, c1)
-    inc(V.tensor_copy(B("pf"), B("pi")), c1)
-    need("v", [i_cmp])
-    ts(B("cma"), B("cmp"), 15, OP.bitwise_and, c1)
-    need("v", [c1])
     c2 = new()
-    ts(B("selv"), B("cma"), 0, OP.is_equal, c2)
-    ts(B("kcol", 0, 1), B("pk", 0, 1), 0, OP.add, c2)
-    ts(B("kcol", 1, 2), B("pk", 0, 1), 8, OP.add, c2)
-    inc(V.tensor_copy(B("vcol"), B("pk", 1, 2)), c2)
-    need("v", [c2, i_c16])
+    ts(B("selv"), B("c16"), B("vcol"), OP.is_equal, c2)
     c3 = new()
     for h, te in enumerate(("te0", "te1")):
         ts(B(te, 0, 128), B("c16"), B("kcol", h, h + 1), OP.is_ge, c3)
         ts(B(te, 128, 256), B("c16"), B("kcol", h, h + 1), OP.is_gt, c3)
-    c5 = new()
-    need("v", [i_kc])
-    ts(B("bo"), B("kc"), B("kcol", 0, 1), OP.is_equal, c5)
 
     need("v", [tk])
     a1 = inc(V.tensor_copy(B("kh", p=16), T.ki[0:16, :]), new())
     need("t", [c2, a1])
     a2 = inc(P.matmul(T.b0[:, 0:128], B("selv", p=16), B("kh", p=16), True, True), new())
-    need("v", [i_cc, c5])
+    c5 = new()
+    ts(B("bo"), B("kc"), B("kcol", 0, 1), OP.is_equal, c5)
     ts(B("gt"), B("kc"), B("kcol", 0, 1), OP.is_gt, c5)
-    ts(B("le"), B("cc"), B("pf"), OP.is_le, c5, -1.0, OP.mult)
+    ts(B("le"), B("ci"), B("pf"), OP.is_le, c5, -1.0, OP.mult)
     need("v", [a2])
     a3, a4 = new(), new()
     for h in range(2):
@@ -179,21 +259,16 @@ def rank_program(g, core, T, topo):
     need("v", [c5])
     c6 = new()
     inc(V.tensor_tensor(B("lb"), B("le"), B("bo"), OP.mult), c6)
-    ts(B("onh"), B("cc"), 0.0, OP.is_ge, c6)
+    ts(B("onh"), B("ci"), 0.0, OP.is_ge, c6)
     need("v", [a5])
     a6 = inc(V.tensor_copy(T.erow[0:1, :], T.b5[0:1, 0:256]), new())
     need("y", [a6])
     a7 = inc(Y.dma_start(T.ed[r], T.erow[0:1, :]), new(), 16)
     need("g", [a7])
-    far = [t for p in pairs for t in p]
-
-    def did(c):
-        rid, pid, _e = topo.addr(c)
-        return DstId(rid=rid, pnc=pid)
     g.remote_dma_fused([
-        RemoteDMATransfer(srcs=[T.ed[r]], dsts=[T.ed[r] for _ in far], dst_ids=[did(c) for c in far],
+        RemoteDMATransfer(srcs=[T.ed[r]], dsts=[T.ed[r] for _ in far], dst_ids=[_did(topo, c) for c in far],
                           dma_engine_mask=lo, remote_sem=T.sem.earr),
-        RemoteDMATransfer(srcs=[T.ed[r]], dsts=[T.ed[r]], dst_ids=[did(mate)], dma_engine_mask=hi,
+        RemoteDMATransfer(srcs=[T.ed[r]], dsts=[T.ed[r]], dst_ids=[_did(topo, mate)], dma_engine_mask=hi,
                           remote_sem=T.sem.earr)], local_sem=T.sem.esent)
     Y.wait_ge(T.sem.earr, 8 * (N - 1))
     need("y", [a7])
@@ -218,7 +293,9 @@ def rank_program(g, core, T, topo):
     d4 = inc(P.matmul(T.b3[:, 0:16], B("oh", 128, 256), B("sbase", 16, 32), False, True), new())
     c7 = new()
     inc(V.tensor_copy(B("c16h"), B("c16")), c7)
-    inc(V.tensor_copy(B("cch"), B("cc")), c7)
+    inc(V.tensor_copy(B("cch"), B("ci")), c7)
+    ts(B("jcol"), B("ci", 0, 16), B("p16"), OP.add, c7)
+    inc(V.memset(T.xs[:, W:W + CAP], 0.0), c7)
     need("v", [d4])
     d5 = inc(V.tensor_copy(B("posi"), T.b3[:, 0:16]), new())
     need("v", [d5])
@@ -227,7 +304,7 @@ def rank_program(g, core, T, topo):
     ts(B("lh", 16, 32), B("posi"), 4, OP.arith_shift_right, d6)
     need("v", [d6])
     d7 = inc(V.tensor_copy(B("lhf"), B("lh")), new())
-    need("v", [d7, c7, i_j])
+    need("v", [d7, c7])
     for b in range(4):
         d8 = new()
         for v in range(4 * b, 4 * b + 4):
@@ -239,14 +316,6 @@ def rank_program(g, core, T, topo):
             m = P.matmul(T.b4[:, 0:128], B("lq", v * 128, v * 128 + 128), B("rq", v * 128, v * 128 + 128), v == 0,
                          v == 15)
     d9 = inc(m, new())
-    c8 = new()
-    need("v", [i_rm, i_qb])
-    for a, dst, op, mul in ((0, "r1", OP.is_gt, 1.0), (12, "r1", OP.is_equal, 0.0), (24, "r1", OP.is_equal, 1.0),
-                            (0, "r2", OP.is_le, 1.0), (12, "r2", OP.is_equal, 1.0), (24, "r2", OP.is_equal, -1.0)):
-        ts(B(dst, a, a + N), B("rm"), 0.0, op, c8, mul, OP.mult)
-    ts(B("on8"), B("cc"), 0.0, OP.is_ge, c8, 0.125, OP.mult)
-    ts(B("qpat"), B("qb"), B("vcol"), OP.add, c8)
-    inc(V.memset(T.xs[:, W:W + CAP], 0.0), c8)
     need("v", [d9])
     f1 = inc(V.tensor_copy(T.gl[:], T.b4[:, 0:128]), new())
     f2 = new()
@@ -256,67 +325,61 @@ def rank_program(g, core, T, topo):
     need("s", [f1, tx])
     inc(S.activation(T.xs[:, W // 2:W], T.xin[:, 0:W].indirect(T.gl[:, 64:128]), ActivationFunctionType.Copy), f3)
 
-    need("t", [e1, c8])
-    P.matmul(T.b5[:, 0:36], T.el[0:N, 0:128], B("r1", p=N), True, False)
-    h1 = inc(P.matmul(T.b5[:, 0:36], T.el[0:N, 128:256], B("r2", p=N), False, True), new())
-    need("v", [h1, i_dc])
+    if first:
+        P.wait_ge(T.sem.tabm, 16)
+    else:
+        need("t", [tab])
+    V.wait_ge(T.sem.tabm, 16)
+    need("v", [tab])
+    need("t", [e1])
+    P.matmul(T.b5[:, 0:36], T.el[0:N, 0:128], T.tr[0:N, 0:36], True, False)
+    h1 = inc(P.matmul(T.b5[:, 0:36], T.el[0:N, 128:256], T.tr[0:N, 36:72], False, True), new())
+    need("v", [h1])
     h2 = new()
-    ts(B("z1"), B("dcon"), T.b5[:, r:r + 1], OP.subtract, h2, T.b5[:, 24 + r:25 + r], OP.min)
+    ts(B("z1"), T.tr[:, 200:212], T.b5[:, r:r + 1], OP.subtract, h2, T.b5[:, 24 + r:25 + r], OP.min)
     need("v", [h2])
     h3 = new()
     ts(B("z2"), B("z1"), 0.0, OP.max, h3)
     need("t", [h3])
-    h4 = inc(P.matmul(T.b6[:, 0:N], B("on8"), B("z2"), True, True), new())
+    h4 = inc(P.matmul(T.b6[:, 0:N], T.tr[:, 72:200], B("z2"), True, True), new())
     need("v", [h4])
     tl = {}
 
     def mklist(d):
-        tl[d] = new()
-        ts(T.sl[:, d * 32:d * 32 + 32], B("qpat", 0, 32), T.b6[:, d:d + 1], OP.add, tl[d])
+        if d not in tl:
+            tl[d] = new()
+            ts(T.sl[:, d * 32:d * 32 + 32], T.tq[:, 0:32], T.b6[:, d:d + 1], OP.add, tl[d])
 
-    def piece(n, d, out):
-        need(n, [tl[d], f2, f3, c8])
-        src = T.xs[:, 0:W + CAP].indirect(T.sl[:, d * 32:d * 32 + 32])
-        t = new()
+    def gather(n, d, c0, c1, out):
+        need(n, [tl[d], f2, f3, c7])
+        src = T.xs[:, 0:W + CAP].indirect(T.sl[:, d * 32 + c0 // 16:d * 32 + c1 // 16])
         if n == "v":
-            return inc(V.tensor_copy(out, src), t)
-        return inc(S.activation(out, src, ActivationFunctionType.Copy), t)
+            return inc(V.tensor_copy(out, src), new())
+        return inc(S.activation(out, src, ActivationFunctionType.Copy), new())
 
-    def slot(i):
-        return T.slots[:, i * CAP:(i + 1) * CAP]
-    rd = [(T.rank_of(a), T.rank_of(b)) for a, b in pairs]
-    mr = T.rank_of(mate)
-    mine = T.land[:, r * CAP:(r + 1) * CAP]
-    mklist(rd[0][0])
-    for i in range(5):
-        mklist(rd[i][1])
-        mklist(rd[i + 1][0] if i < 4 else mr)
-        ta = piece("s", rd[i][0], slot(2 * i))
-        tb = piece("v", rd[i][1], slot(2 * i + 1))
-        need("g", [ta, tb])
-        g.remote_dma_fused([
-            RemoteDMATransfer(srcs=[slot(2 * i + 1)], dsts=[T.land[:, i * CAP:(i + 1) * CAP]], dst_ids=[did(helper)],
-                              dma_engine_mask=hi, remote_sem=T.sem["fw%d" % i]),
-            RemoteDMATransfer(srcs=[slot(2 * i)], dsts=[mine], dst_ids=[did(pairs[i][0])],
-                              dma_engine_mask=lo, remote_sem=T.sem.arr)], local_sem=T.sem.sent)
-    tm = piece("s", mr, slot(10))
-    need("g", [tm])
-    rid, pid, _e = topo.addr(mate)
-    g.remote_dma(mine, slot(10), T.sem.arr, T.sem.sent, pid, rid, hi)
+    sent = 0
+    grp = groups[core]
+    for i, pair in enumerate(grp):
+        for piece in pair + grp[i + 1][0:1] if i + 1 < len(grp) else pair:
+            mklist(T.rank_of(piece[0][-1]))
+        done, tr = [], []
+        for n, piece in zip("sv", pair):
+            path, c0, c1 = piece
+            d = T.rank_of(path[-1])
+            out = T.slots[:, d * CAP + c0:d * CAP + c1]
+            done.append(gather(n, d, c0, c1, out))
+            tr.append(_hop(T, topo, jobs, piece, core, out))
+            sent += _n(topo, core, path[1])
+        need("g", done)
+        g.remote_dma_fused(tr, local_sem=T.sem.sent)
     mklist(r)
-    town = piece("v", r, mine)
+    town = gather("v", r, 0, CAP, T.land[:, r * CAP:(r + 1) * CAP])
 
-    k1 = new()
-    need("v", [i_rc])
-    ts(B("mka"), B("rcol"), B("kcol", 0, 1), OP.is_equal, k1)
-    ts(B("mkb"), B("rcol"), B("kcol", 1, 2), OP.is_equal, k1)
-    ts(B("rb"), B("kcol"), float(CAP), OP.mult, k1)
-    inc(V.memset(B("onf"), 1.0), k1)
-    inc(V.memset(B("ngf"), -1.0), k1)
-    need("v", [k1])
+    V.wait_ge(T.sem.tabh, 8)
+    P.wait_ge(T.sem.tabh, 8)
     k2 = new()
-    inc(V.tensor_tensor(B("pa"), T.b5[:, 0:36], B("mka"), OP.mult), k2)
-    inc(V.tensor_tensor(B("pb"), T.b5[:, 0:36], B("mkb"), OP.mult), k2)
+    inc(V.tensor_tensor(B("pa"), T.b5[:, 0:36], T.th[:, 0:36], OP.mult), k2)
+    inc(V.tensor_tensor(B("pb"), T.b5[:, 0:36], T.th[:, 36:72], OP.mult), k2)
     need("v", [k2])
     k3 = new()
     for j in range(3):
@@ -339,7 +402,7 @@ def rank_program(g, core, T, topo):
     k7 = inc(P.matmul(T.b7[:, 0:2], B("bo"), B("zd"), True, True), new())
     k8 = new()
     ts(B("li"), B("lr"), 0.0, OP.max, k8, float(W), OP.min)
-    inc(V.tensor_tensor(B("t2"), B("t1"), B("rb"), OP.add), k8)
+    inc(V.tensor_tensor(B("t2"), B("t1"), T.th[:, 72:74], OP.add), k8)
     need("v", [k8])
     k9 = new()
     ts(B("lx", 0, 4), B("li"), 4, OP.arith_shift_right, k9)
@@ -355,25 +418,26 @@ def rank_program(g, core, T, topo):
         for e in range(2):
             o = x * 512 + e * 256
             hs, ls = 2 * e + x, 4 + 2 * e + x
-            ts(B("rg", o, o + 128), B("cc"), B("lxf", hs, hs + 1), OP.is_gt, k11, dl, OP.mult)
-            ts(B("rg", o + 128, o + 256), B("cc"), B("lxf", hs, hs + 1), OP.is_equal, k11, dl, OP.mult)
+            ts(B("rg", o, o + 128), B("ci"), B("lxf", hs, hs + 1), OP.is_gt, k11, dl, OP.mult)
+            ts(B("rg", o + 128, o + 256), B("ci"), B("lxf", hs, hs + 1), OP.is_equal, k11, dl, OP.mult)
             o = x * 256 + e * 128
             ts(B("lg", o, o + 128), B("c16"), B("lxf", ls, ls + 1), OP.is_ge, k11, 1.0 - 2.0 * e, OP.mult)
     need("t", [k11])
     for x in range(2):
         for e in range(2):
             o = x * 512 + e * 256
-            P.matmul(T.b7[:, 128:256], B("ngf" if e else "onf"), B("rg", o, o + 128), x + e == 0, False)
+            P.matmul(T.b7[:, 128:256], T.th[:, 74 + 128 * e:202 + 128 * e], B("rg", o, o + 128), x + e == 0, False)
             m = P.matmul(T.b7[:, 128:256], B("lg", x * 256 + e * 128, x * 256 + e * 128 + 128),
                          B("rg", o + 128, o + 256), False, x + e == 2)
     k12 = inc(m, new())
     need("v", [k12])
-    k13 = inc(V.tensor_tensor(B("off"), T.b7[:, 128:256], B("qpat"), OP.add), new())
+    k13 = inc(V.tensor_tensor(B("off"), T.b7[:, 128:256], T.tq[:], OP.add), new())
     need("v", [k13])
     k14 = inc(V.tensor_copy(T.ol[:], B("off")), new())
 
-    V.wait_ge(T.sem.arr, 8 * (N - 1))
-    S.wait_ge(T.sem.arr, 8 * (N - 1))
+    total = sum(_n(topo, p[0][-2], core) for c in T.cores for pair in groups[c] for p in pair if p[0][-1] == core)
+    V.wait_ge(T.sem.arr, total)
+    S.wait_ge(T.sem.arr, total)
     ty = new()
     for b in range(4):
         n = "s" if b % 2 else "v"
@@ -387,8 +451,7 @@ def rank_program(g, core, T, topo):
         need("y", [t])
         inc(Y.dma_start(T.y[:, b * 512:b * 512 + 512], out), ty, 16)
     need("y", [ty])
+    g.wait_ge(T.sem.tsent, 16)
     g.wait_ge(T.sem.esent, 16)
-    g.wait_ge(T.sem.sent, 16 * 5 + 8)
-    for t in toks:
-        if not t["w"]:
-            need("g", [t])
+    g.wait_ge(T.sem.sent, sent)
+    close()

@@ -1,29 +1,37 @@
 from concourse.bass import DstId, RemoteDMATransfer
-from concourse.mybir import AluOpType as OP, AxisListType, ActivationFunctionType
+from concourse.mybir import AluOpType as OP, AxisListType, ActivationFunctionType as AF
 
-N, W, CAP, SIM = 12, 2048, 512, 112
-NEXT = ((3, 4, 1, 2, 5), (5, 2, 3, 4, 0), (0, 5, 4, 1, 3), (4, 0, 5, 2, 1), (1, 5, 0, 3, 2), (1, 4, 2, 0, 3))
-FAR = ((1, 5), (2, 5), (3, 0), (3, 4), (5, 1), (5, 4))
-F32, F16, I32, U16 = "float32", "float16", "int32", "uint16"
+N, W, SIM = 12, 2048, 112
+S1, S2 = 176, 192
+TW, HALF = 1.0 / 12, 11.0 / 24
+VS = 11
+XP = 4
+F32, F16, BF, I32, U16 = "float32", "float16", "bfloat16", "int32", "uint16"
 SCRATCH = {
-    "land": ("sbuf", [128, N * CAP], F32), "slots": ("sbuf", [128, N * CAP], F32),
-    "xin": ("sbuf", [128, W], F32), "xs": ("sbuf", [128, W + CAP], F32), "yb": ("sbuf", [128, W], F32),
+    "xin": ("sbuf", [128, W], F32), "p1": ("sbuf", [128, N * S1], F32), "xl": ("sbuf", [128, N * S1], F32),
+    "p2": ("sbuf", [128, N * S2], F32), "sb": ("sbuf", [128, 4 * S2], F32), "land": ("sbuf", [128, N * S2], F32),
+    "yb": ("sbuf", [128, W], F32),
     "ki": ("sbuf", [128, 128], I32), "erow": ("sbuf", [128, 256], F16), "el": ("sbuf", [128, 256], F16),
-    "gl": ("sbuf", [128, 128], U16), "sl": ("sbuf", [128, N * 32], U16), "ol": ("sbuf", [128, 128], U16),
-    "tq": ("sbuf", [128, 128], F32), "tr": ("sbuf", [128, 212], F16), "th": ("sbuf", [128, 330], F32),
+    "gl": ("sbuf", [128, 132], U16), "il": ("sbuf", [128, 144], U16), "ol": ("sbuf", [128, 128], U16),
+    "xt": ("sbuf", [128, 664], F16), "th": ("sbuf", [128, 456], F32),
     "ed": ("dram", [N, 128, 2], F16),
 }
 for _i in range(8):
     SCRATCH["b%d" % _i] = ("psum", [128, 512], F32)
 _TILES = {
-    F16: (("kh", 128), ("oh", 256), ("fs", 256), ("mk", 256), ("sbase", 32), ("lq", 2048), ("rq", 2048), ("z2", N),
-          ("selv", 128), ("c16h", 128), ("cch", 128), ("bo", 128), ("gt", 128), ("le", 128), ("lb", 128), ("te0", 256),
-          ("te1", 256), ("onh", 128), ("zd", 2)),
-    F32: (("lhf", 32), ("z1", N), ("pf", 1), ("p16", 1), ("vcol", 1), ("kcol", 2), ("jcol", 16), ("pa", 36),
-          ("pb", 36), ("cols", 6), ("u", 2), ("zm", 2), ("lr", 4), ("lxf", 8), ("t1", 2), ("t2", 2), ("dl", 2),
-          ("rg", 1024), ("lg", 512), ("off", 128)),
-    I32: (("posi", 16), ("lh", 32), ("ci", 128), ("c16", 128), ("kc", 128), ("pi", 1), ("pk", 2), ("li", 4),
-          ("lx", 8)),
+    F16: (("kh", 128), ("oh", 256), ("fs", 256), ("mk", 256), ("sbase", 32), ("lq", 2048), ("rq", 16 * 132),
+          ("selv", 128), ("c16h", 128), ("kch", 128), ("cch", 132), ("bo", 128), ("gt", 128), ("le", 128),
+          ("lb", 128), ("te0", 256), ("te1", 256), ("onh", 128), ("zd", 4), ("n16", 2), ("z2", 288), ("xg", 72),
+          ("xy", 72), ("xz", 72), ("an", 2), ("nn", 2), ("xr", 288), ("xq", 288), ("xlg", 256)),
+    BF: (("c16b", 128), ("lab", 640), ("lqs", 640)),
+    F32: (("lhf", 32), ("qf", 16), ("jf", 16), ("pq", 16), ("pf", 1), ("p16", 1), ("vcol", 1), ("kcol", 2),
+          ("jcol", 16), ("pa", 36), ("pb", 36), ("cols", 6), ("u", 2), ("u2", 2), ("zm", 4), ("lr", 4), ("lxf", 8),
+          ("t1", 2), ("t2", 2), ("dl", 2), ("rf", 4), ("rb", 2), ("ra", 2), ("ov", 2), ("rg", 1024), ("lg", 512),
+          ("off", 128), ("vq", 128), ("v1", 128), ("v2", 128), ("v3", 128), ("z1", 288), ("df", 1), ("dcol", 1),
+          ("sm", 1), ("fq", 4), ("ohl", 4), ("xd", 2), ("xo", 144)),
+    I32: (("posi", 16), ("qi", 16), ("lh", 32), ("ci", 132), ("c16", 128), ("kc", 128), ("pi", 1), ("pk", 2),
+          ("li", 4), ("lx", 8), ("ri", 4), ("vi", 128), ("wd", 24), ("cc", 72), ("cd", 72), ("di", 1), ("qx", 4),
+          ("oi", 2), ("oh2", 4)),
 }
 _AT = {}
 for _dt, _ts in _TILES.items():
@@ -32,55 +40,31 @@ for _dt, _ts in _TILES.items():
         _AT[_n] = ("m_" + _dt, _o, _w, _dt)
         _o += (_w + 31) // 32 * 32
     SCRATCH["m_" + _dt] = ("sbuf", [128, _o], _dt)
-NSEM = 120
-SEMAPHORES = (["earr", "arr", "sent", "esent", "tabm", "tabh", "tsent"] + ["fw%d" % i for i in range(8)]
+_XT = {"tr": 0, "xu": 200, "xb": 272, "xs": 344, "xm": 416, "cc": 488, "base": 560, "wd": 632, "s176": 656}
+NSEM = 110
+SEMAPHORES = (["earr", "arr", "a1", "sent", "esent", "tabh", "tsent", "xa", "la", "ola", "f0", "f1"]
               + ["s%d" % i for i in range(NSEM)])
 
 
-def _plan(T, topo):
+def _places(T, topo):
     chips = sorted(set(topo.chip(c) for c in T.cores))
-    rk = dict((h, sorted(c for c in T.cores if topo.chip(c) == h)) for h in chips)
-    hp = {}
-    for h in chips:
+    rk = [sorted(c for c in T.cores if topo.chip(c) == h) for h in chips]
+    hp = []
+    for i, h in enumerate(chips):
         far = [t for t in T.cores if topo.chip(t) != h]
-        hp[h] = [c for c in range(SIM) if topo.chip(c) == h and T.rank_of(c) is None
-                 and topo.die(c) != topo.die(rk[h][0]) and all(topo.may_write(c, t) for t in far)]
-
-    def relay(a, k, die, dst):
-        b = topo.chip(dst)
-        if (chips.index(a), chips.index(b)) not in FAR:
-            return []
-        return [[c for c in range(SIM) if topo.mates(topo.chip(c), b) and topo.die(c) == die
-                 and topo.may_write(c, dst)][k]]
-    groups, jobs, mate, helper = {}, {}, {}, {}
-    for a in chips:
-        for k in range(2):
-            me, hc = rk[a][k], hp[a][k]
-            mate[me], helper[me] = rk[a][1 - k], hc
-            own, oth, last = [], [], []
-            for o in NEXT[chips.index(a)]:
-                d0, d1 = rk[chips[o]][k], rk[chips[o]][1 - k]
-                own.append([me] + relay(a, k, topo.die(me), d0) + [d0])
-                oth.append([me, hc] + relay(a, k, topo.die(hc), d1) + [d1])
-                last = [me] + relay(a, k, topo.die(me), d1) + [d1]
-            m, h = [me, rk[a][1 - k]], CAP // 2
-            grp = [[(own[0], 0, h), (oth[0], 0, h)], [(own[0], h, CAP), (oth[0], h, CAP)]]
-            grp += [[(own[i], 0, CAP), (oth[i], 0, CAP)] for i in (1, 2, 3)]
-            grp += [[(own[4], 0, h), (oth[4], 0, h)], [(own[4], h, CAP), (m, 0, h)], [(last, h, CAP), (m, h, CAP)]]
-            groups[me] = grp
-            for pair in grp:
-                for piece in pair:
-                    for c in piece[0][1:-1]:
-                        jobs.setdefault(c, []).append(piece)
-    return groups, jobs, mate, helper
+        hp.append([c for c in range(SIM) if topo.chip(c) == h and T.rank_of(c) is None
+                   and topo.die(c) != topo.die(rk[i][0]) and all(topo.may_write(c, t) for t in far)][0:2])
+    return chips, rk, hp
 
 
-def _mask(topo, src, dst):
-    m = topo.mask(src, dst)
-    if topo.chip(src) == topo.chip(dst):
-        off = [topo.mask(src, c) for c in range(SIM) if topo.same_plane(topo.chip(src), topo.chip(c))][0]
-        return m & ~off
-    return m
+def _masks(topo, core, near, far):
+    lo = topo.mask(core, far)
+    hi = topo.mask(core, near) & ~lo
+    out = []
+    for m in (lo, hi):
+        bits = [1 << i for i in range(m.bit_length()) if m >> i & 1]
+        out.append((sum(bits[:len(bits) // 2]), sum(bits[len(bits) // 2:])))
+    return lo, hi, out[0], out[1]
 
 
 def _did(topo, c):
@@ -88,21 +72,8 @@ def _did(topo, c):
     return DstId(rid=rid, pnc=pid)
 
 
-def _hop(T, topo, jobs, piece, core, src):
-    path, c0, c1 = piece
-    nx = path[path.index(core) + 1]
-    if nx == path[-1]:
-        r = T.rank_of(path[0])
-        dst, sem = T.land[:, r * CAP + c0:r * CAP + c1], T.sem.arr
-    else:
-        j = jobs[nx].index(piece)
-        dst, sem = T.land[:, j * CAP:j * CAP + c1 - c0], T.sem["fw%d" % j]
-    return RemoteDMATransfer(srcs=[src], dsts=[dst], dst_ids=[_did(topo, nx)],
-                             dma_engine_mask=_mask(topo, core, nx), remote_sem=sem)
-
-
-def _n(topo, a, b):
-    return bin(_mask(topo, a, b)).count("1")
+def _tr(topo, src, dst, to, mask, sem):
+    return RemoteDMATransfer(srcs=[src], dsts=[dst], dst_ids=[_did(topo, to)], dma_engine_mask=mask, remote_sem=sem)
 
 
 def _tools(g, T):
@@ -136,250 +107,183 @@ def _tools(g, T):
             return inc(g.vector.tensor_scalar(out, in0, s1, None, op0), t)
         return inc(g.vector.tensor_scalar(out, in0, s1, s2, op0, op1), t)
 
+    def cp(out, in_, t):
+        return inc(g.vector.tensor_copy(out, in_), t)
+
+    def tt(out, a, b, op, t):
+        return inc(g.vector.tensor_tensor(out, a, b, op), t)
+
     def counters():
         i1 = inc(g.iota(B("pi"), [[0, 1]], 0, 1), new())
-        i2 = inc(g.iota(B("ci"), [[1, 128]], 0, 0), new())
+        i2 = inc(g.iota(B("ci"), [[1, 132]], 0, 0), new())
         c1 = new()
         need("v", [i1])
         ts(B("pk", 0, 1), B("pi"), 4, OP.arith_shift_right, c1)
         ts(B("pk", 1, 2), B("pi"), 15, OP.bitwise_and, c1)
-        inc(g.vector.tensor_copy(B("pf"), B("pi")), c1)
+        cp(B("pf"), B("pi"), c1)
         ts(B("p16"), B("pi"), 16, OP.mult, c1)
         need("v", [i2])
-        ts(B("c16"), B("ci"), 15, OP.bitwise_and, c1)
-        ts(B("kc"), B("ci"), 4, OP.arith_shift_right, c1)
+        ts(B("c16"), B("ci", 0, 128), 15, OP.bitwise_and, c1)
+        ts(B("kc"), B("ci", 0, 128), 4, OP.arith_shift_right, c1)
+        cp(B("cch"), B("ci"), c1)
         need("v", [c1])
         c2 = new()
         ts(B("kcol", 0, 1), B("pk", 0, 1), 0, OP.add, c2)
         ts(B("kcol", 1, 2), B("pk", 0, 1), 8, OP.add, c2)
-        inc(g.vector.tensor_copy(B("vcol"), B("pk", 1, 2)), c2)
+        cp(B("vcol"), B("pk", 1, 2), c2)
+        cp(B("c16h"), B("c16"), c2)
+        cp(B("kch"), B("kc"), c2)
         need("v", [c2])
+
+    def blocks(t):
+        ts(B("bo"), B("kch"), B("kcol", 0, 1), OP.is_equal, t)
+        ts(B("gt"), B("kch"), B("kcol", 0, 1), OP.is_gt, t)
+        ts(B("onh"), B("cch", 0, 128), 0.0, OP.is_ge, t)
+
+    def sums(t):
+        c12 = B("cch", 0, N)
+        for a, op, mul in ((0, OP.is_gt, 1.0), (12, OP.is_equal, 0.0), (24, OP.is_equal, 1.0),
+                           (36, OP.is_le, 1.0), (48, OP.is_equal, 1.0), (60, OP.is_equal, -1.0)):
+            ts(T.xt[:, a:a + N], c12, B("pf"), op, t, mul, OP.mult)
+        ts(T.xt[:, 72:200], B("cch", 0, 128), 0.0, OP.is_ge, t, 0.125, OP.mult)
+
+    def gather(n, deps, out, win, off):
+        need(n, deps)
+        src = win.indirect(off)
+        if n == "v":
+            return inc(g.vector.tensor_copy(out, src), new())
+        return inc(g.scalar.activation(out, src, AF.Copy), new())
 
     def close():
         for t in toks:
             if not t["w"]:
                 need("g", [t])
-    return B, new, need, inc, ts, counters, close
+    return B, new, need, inc, ts, cp, tt, counters, blocks, sums, gather, close
 
 
-def _pass_on(g, core, T, topo, jobs, helper):
-    mine = jobs.get(core, [])
-    B, new, need, inc, ts, counters, close = _tools(g, T)
-    own = [c for c in T.cores if helper[c] == core]
-    if own:
-        counters()
-        t = new()
-        for j in range(3):
-            for x in range(2):
-                ts(T.th[:, 36 * x + 12 * j:36 * x + 12 * j + 12], B("ci", 0, N), B("kcol", x, x + 1), OP.is_equal, t)
-        ts(T.th[:, 72:74], B("kcol"), float(CAP), OP.mult, t)
-        inc(g.vector.memset(T.th[:, 74:202], 1.0), t)
-        inc(g.vector.memset(T.th[:, 202:330], -1.0), t)
-        need("g", [t])
-        rid, pid, _e = topo.addr(own[0])
-        g.remote_dma(T.th[:], T.th[:], T.sem.tabh, T.sem.tsent, pid, rid,
-                     topo.mask(core, own[0]) & ~_mask(topo, core, own[0]))
-    sent = 0
-    for i, piece in enumerate(mine):
-        path, c0, c1 = piece
-        at = path.index(core)
-        g.wait_ge(T.sem["fw%d" % i], _n(topo, path[at - 1], core))
-        g.remote_dma_fused([_hop(T, topo, jobs, piece, core, T.land[:, i * CAP:i * CAP + c1 - c0])],
-                           local_sem=T.sem.sent)
-        sent += _n(topo, core, path[at + 1])
-    if own:
-        g.wait_ge(T.sem.tsent, 8)
-    if mine:
-        g.wait_ge(T.sem.sent, sent)
-    close()
-
-
-def rank_program(g, core, T, topo):
-    groups, jobs, mates, helper = _plan(T, topo)
-    r = T.rank_of(core)
-    if r is None:
-        return _pass_on(g, core, T, topo, jobs, helper)
-    mate = mates[core]
-    far = [c for c in T.cores if topo.chip(c) != topo.chip(core)]
-    lo = topo.mask(core, far[0])
-    hi = topo.mask(core, mate) & ~lo
-    mid, mpid, _e = topo.addr(mate)
-    first = T.rank_of(core) < T.rank_of(mate)
-
-    V, S, P, Y = g.vector, g.scalar, g.tensor, g.sync
-    B, new, need, inc, ts, counters, close = _tools(g, T)
-
-    tk, tx = new(), new()
-    inc(Y.dma_start(T.ki[0:16, :], T.key[:]), tk, 16)
-    inc(Y.dma_start(T.xin[:], T.x[:]), tx, 16)
-
-    counters()
-    tab = new()
-    if first:
-        ts(T.tq[:], B("ci"), 16.0, OP.mult, tab, B("vcol"), OP.add)
-        mytab = T.tq[:]
-    else:
-        c12 = B("ci", 0, N)
-        for a, op, mul in ((0, OP.is_gt, 1.0), (12, OP.is_equal, 0.0), (24, OP.is_equal, 1.0),
-                           (36, OP.is_le, 1.0), (48, OP.is_equal, 1.0), (60, OP.is_equal, -1.0)):
-            ts(T.tr[:, a:a + N], c12, B("pf"), op, tab, mul, OP.mult)
-        ts(T.tr[:, 72:200], B("ci"), 0.0, OP.is_ge, tab, 0.125, OP.mult)
-        ts(T.tr[:, 200:212], c12, float(W), OP.mult, tab)
-        mytab = T.tr[:]
-    need("g", [tab])
-    g.remote_dma(mytab, mytab, T.sem.tabm, T.sem.tsent, mpid, mid, topo.mask(core, mate))
-
-    c2 = new()
-    ts(B("selv"), B("c16"), B("vcol"), OP.is_equal, c2)
-    c3 = new()
-    for h, te in enumerate(("te0", "te1")):
-        ts(B(te, 0, 128), B("c16"), B("kcol", h, h + 1), OP.is_ge, c3)
-        ts(B(te, 128, 256), B("c16"), B("kcol", h, h + 1), OP.is_gt, c3)
-
-    need("v", [tk])
-    a1 = inc(V.tensor_copy(B("kh", p=16), T.ki[0:16, :]), new())
-    need("t", [c2, a1])
-    a2 = inc(P.matmul(T.b0[:, 0:128], B("selv", p=16), B("kh", p=16), True, True), new())
-    c5 = new()
-    ts(B("bo"), B("kc"), B("kcol", 0, 1), OP.is_equal, c5)
-    ts(B("gt"), B("kc"), B("kcol", 0, 1), OP.is_gt, c5)
-    ts(B("le"), B("ci"), B("pf"), OP.is_le, c5, -1.0, OP.mult)
-    need("v", [a2])
-    a3, a4 = new(), new()
-    for h in range(2):
-        ts(B("oh", h * 128, h * 128 + 128), T.b0[:, 0:128], B("kcol", h, h + 1), OP.is_equal, a3)
-    need("v", [a3])
-    for h in range(2):
-        o = B("oh", h * 128, h * 128 + 128)
-        inc(V.tensor_tensor_scan(B("fs", h * 128, h * 128 + 128), o, o, 0.0, OP.add, OP.max), a4)
-    cnt = [B("fs", 127, 128), B("fs", 255, 256)]
-    need("t", [a4, c3])
-    P.matmul(T.b5[0:1, 0:256], cnt[0], B("te0"), True, False)
-    a5 = inc(P.matmul(T.b5[0:1, 0:256], cnt[1], B("te1"), False, True), new())
-    need("v", [c5])
-    c6 = new()
-    inc(V.tensor_tensor(B("lb"), B("le"), B("bo"), OP.mult), c6)
-    ts(B("onh"), B("ci"), 0.0, OP.is_ge, c6)
-    need("v", [a5])
-    a6 = inc(V.tensor_copy(T.erow[0:1, :], T.b5[0:1, 0:256]), new())
-    need("y", [a6])
-    a7 = inc(Y.dma_start(T.ed[r], T.erow[0:1, :]), new(), 16)
-    need("g", [a7])
-    g.remote_dma_fused([
-        RemoteDMATransfer(srcs=[T.ed[r]], dsts=[T.ed[r] for _ in far], dst_ids=[_did(topo, c) for c in far],
-                          dma_engine_mask=lo, remote_sem=T.sem.earr),
-        RemoteDMATransfer(srcs=[T.ed[r]], dsts=[T.ed[r]], dst_ids=[_did(topo, mate)], dma_engine_mask=hi,
-                          remote_sem=T.sem.earr)], local_sem=T.sem.esent)
-    Y.wait_ge(T.sem.earr, 8 * (N - 1))
-    need("y", [a7])
-    e1 = inc(Y.dma_start(T.el[0:N, :], T.ed[:]), new(), 16)
-
-    need("t", [c6])
-    P.matmul(T.b1[:, 0:256], B("bo"), B("fs"), True, False)
-    d1 = inc(P.matmul(T.b1[:, 0:256], B("lb"), B("oh"), False, True), new())
-    P.matmul(T.b2[:, 0:1], B("gt"), cnt[0], True, True)
-    P.matmul(T.b2[:, 1:2], B("onh"), cnt[0], True, False)
-    d2 = inc(P.matmul(T.b2[:, 1:2], B("gt"), cnt[1], False, True), new())
-    need("v", [d1])
-    d3 = inc(V.tensor_tensor(B("mk"), T.b1[:, 0:256], B("oh"), OP.mult), new())
-    need("v", [d2])
-    s16 = B("selv", 0, 16)
-    for h in range(2):
-        ts(B("sbase", h * 16, h * 16 + 16), s16, T.b2[:, h:h + 1], OP.mult, d3)
-    need("t", [d3])
-    P.matmul(T.b3[:, 0:16], B("mk", 0, 128), s16, True, False)
-    P.matmul(T.b3[:, 0:16], B("mk", 128, 256), s16, False, False)
-    P.matmul(T.b3[:, 0:16], B("oh", 0, 128), B("sbase", 0, 16), False, False)
-    d4 = inc(P.matmul(T.b3[:, 0:16], B("oh", 128, 256), B("sbase", 16, 32), False, True), new())
-    c7 = new()
-    inc(V.tensor_copy(B("c16h"), B("c16")), c7)
-    inc(V.tensor_copy(B("cch"), B("ci")), c7)
-    ts(B("jcol"), B("ci", 0, 16), B("p16"), OP.add, c7)
-    inc(V.memset(T.xs[:, W:W + CAP], 0.0), c7)
-    need("v", [d4])
-    d5 = inc(V.tensor_copy(B("posi"), T.b3[:, 0:16]), new())
-    need("v", [d5])
-    d6 = new()
-    ts(B("lh", 0, 16), B("posi"), 15, OP.bitwise_and, d6)
-    ts(B("lh", 16, 32), B("posi"), 4, OP.arith_shift_right, d6)
-    need("v", [d6])
-    d7 = inc(V.tensor_copy(B("lhf"), B("lh")), new())
-    need("v", [d7, c7])
-    for b in range(4):
-        d8 = new()
-        for v in range(4 * b, 4 * b + 4):
-            ts(B("lq", v * 128, v * 128 + 128), B("c16h"), B("lhf", v, v + 1), OP.is_equal, d8)
-            ts(B("rq", v * 128, v * 128 + 128), B("cch"), B("lhf", 16 + v, 17 + v), OP.is_equal, d8,
-               B("jcol", v, v + 1), OP.mult)
-        need("t", [d8])
-        for v in range(4 * b, 4 * b + 4):
-            m = P.matmul(T.b4[:, 0:128], B("lq", v * 128, v * 128 + 128), B("rq", v * 128, v * 128 + 128), v == 0,
-                         v == 15)
-    d9 = inc(m, new())
-    need("v", [d9])
-    f1 = inc(V.tensor_copy(T.gl[:], T.b4[:, 0:128]), new())
-    f2 = new()
-    f3 = new()
-    need("v", [f1, tx])
-    inc(V.tensor_copy(T.xs[:, 0:W // 2], T.xin[:, 0:W].indirect(T.gl[:, 0:64])), f2)
-    need("s", [f1, tx])
-    inc(S.activation(T.xs[:, W // 2:W], T.xin[:, 0:W].indirect(T.gl[:, 64:128]), ActivationFunctionType.Copy), f3)
-
-    if first:
-        P.wait_ge(T.sem.tabm, 16)
-    else:
-        need("t", [tab])
-    V.wait_ge(T.sem.tabm, 16)
-    need("v", [tab])
-    need("t", [e1])
-    P.matmul(T.b5[:, 0:36], T.el[0:N, 0:128], T.tr[0:N, 0:36], True, False)
-    h1 = inc(P.matmul(T.b5[:, 0:36], T.el[0:N, 128:256], T.tr[0:N, 36:72], False, True), new())
+def _counts(g, T, tools, deps):
+    B, new, need, inc = tools[0:4]
+    need("t", deps)
+    g.tensor.matmul(T.b5[:, 0:36], T.el[0:N, 0:128], T.xt[0:N, 0:36], True, False)
+    h1 = inc(g.tensor.matmul(T.b5[:, 0:36], T.el[0:N, 128:256], T.xt[0:N, 36:72], False, True), new())
     need("v", [h1])
+
+
+def _xtables(g, T, tools):
+    B, new, need, inc, ts, cp, tt = tools[0:7]
+
+    def X(n, w=72):
+        return T.xt[:, _XT[n]:_XT[n] + w]
+    i4 = new()
+    inc(g.iota(B("cc"), [[0, 6], [1, 12]], 0, 0), i4)
+    inc(g.iota(B("cd"), [[1, 6], [0, 12]], 0, 0), i4)
+    for h in range(2):
+        inc(g.iota(B("wd", 12 * h, 12 * h + 12), [[W, 6], [6 * W, 2]], W * h, 0), i4)
+    need("v", [i4])
+    c8 = new()
+    tools[9](c8)
+    cp(X("cc"), B("cc"), c8)
+    cp(X("wd", 24), B("wd"), c8)
+    ts(B("df"), B("pf"), TW, OP.mult, c8, -HALF, OP.add)
+    ts(X("base"), B("cc"), 16.0, OP.mult, c8, B("vcol"), OP.add)
+    need("v", [c8])
+    c9 = cp(B("di"), B("df"), new())
+    need("v", [c9])
+    c10 = cp(B("dcol"), B("di"), new())
+    need("v", [c10])
+    c11 = new()
+    ts(B("sm"), B("dcol"), -12.0, OP.mult, c11, B("pf"), OP.add)
+    ts(X("xm"), B("cd"), B("dcol"), OP.is_equal, c11)
+    ts(B("xg"), B("cch", 0, 72), B("pf"), OP.is_gt, c11)
+    ts(B("xy"), B("cch", 0, 72), B("pf"), OP.subtract, c11, 1.0, OP.is_equal)
+    ts(X("xb"), B("cch", 0, 72), B("pf"), OP.is_equal, c11)
+    need("v", [c11])
+    c12 = new()
+    tt(X("xu"), B("xg"), X("xm"), OP.mult, c12)
+    tt(B("xz"), B("xy"), X("xm"), OP.mult, c12)
+    need("v", [c12])
+    c13 = new()
+    tt(X("xb"), X("xb"), B("xz"), OP.subtract, c13)
+    ts(X("xs"), B("xz"), -1.0, OP.mult, c13)
+    ts(X("s176", 8), B("cch", 0, 8), 0.0, OP.is_ge, c13, B("sm"), OP.mult)
+    need("v", [c13])
+    return ts(X("s176", 8), X("s176", 8), 0.0, OP.is_gt, new(), float(S1), OP.mult)
+
+
+def _xlist(g, T, tools):
+    B, new, need, inc, ts, cp, tt = tools[0:7]
+    P = g.tensor
+
+    def X(n, w=72, p=72):
+        return T.xt[0:p, _XT[n]:_XT[n] + w]
+    zb, zo, _w, _d = _AT["z1"]
     h2 = new()
-    ts(B("z1"), T.tr[:, 200:212], T.b5[:, r:r + 1], OP.subtract, h2, T.b5[:, 24 + r:25 + r], OP.min)
+    for s in range(N):
+        ts(T[zb][0:128, zo + s:zo + 288:12], X("wd", 24, 128), T.b5[:, s:s + 1], OP.subtract, h2,
+           T.b5[:, 24 + s:25 + s], OP.min)
     need("v", [h2])
-    h3 = new()
-    ts(B("z2"), B("z1"), 0.0, OP.max, h3)
+    h3 = ts(B("z2"), B("z1"), 0.0, OP.max, new())
     need("t", [h3])
-    h4 = inc(P.matmul(T.b6[:, 0:N], T.tr[:, 72:200], B("z2"), True, True), new())
+    for h in range(4):
+        m = P.matmul(T.b6[0:72, h:h + 1], B("z2", 72 * h, 72 * h + 72), T.xt[:, 72:73], True, True)
+    h4 = inc(m, new())
     need("v", [h4])
-    tl = {}
+    h5 = new()
+    ts(B("fq", 0, 2, 72), T.b6[0:72, 0:2], TW, OP.mult, h5, -HALF, OP.add)
+    ts(B("fq", 2, 4, 72), T.b6[0:72, 2:4], TW, OP.mult, h5, HALF, OP.add)
+    need("v", [h5])
+    h6 = cp(B("qx", p=72), B("fq", p=72), new())
+    need("v", [h6])
+    h7 = new()
+    cp(B("an", p=72), B("qx", 0, 2, 72), h7)
+    tt(B("nn", p=72), B("qx", 2, 4, 72), B("qx", 0, 2, 72), OP.subtract, h7)
+    need("t", [h7])
+    P.matmul(T.b0[0:72, 0:2], X("xu"), B("nn", p=72), True, True)
+    P.matmul(T.b0[0:72, 2:4], X("xb"), B("an", p=72), True, False)
+    h8 = inc(P.matmul(T.b0[0:72, 2:4], X("xs"), B("nn", p=72), False, True), new())
+    need("v", [h8])
+    h9 = new()
+    cp(B("oi", p=72), T.b0[0:72, 0:2], h9)
+    tt(B("xd", p=72), T.b0[0:72, 2:4], X("s176", 2), OP.add, h9)
+    need("v", [h9])
+    h10 = new()
+    ts(B("oh2", 0, 2, 72), B("oi", p=72), 4, OP.arith_shift_right, h10)
+    ts(B("oh2", 2, 4, 72), B("oi", p=72), 15, OP.bitwise_and, h10)
+    need("v", [h10])
+    h11 = cp(B("ohl", p=72), B("oh2", p=72), new())
+    need("v", [h11])
+    h12 = new()
+    for h in range(2):
+        hs, xd = B("ohl", h, h + 1, 72), B("xd", h, h + 1, 72)
+        o = 144 * h
+        ts(B("xr", o, o + 72, 72), X("cc"), hs, OP.is_gt, h12, xd, OP.mult)
+        ts(B("xr", o + 72, o + 144, 72), X("cc"), hs, OP.is_equal, h12, xd, OP.mult)
+        ts(B("xlg", 128 * h, 128 * h + 128, 72), B("c16h", p=72), B("ohl", 2 + h, 3 + h, 72), OP.is_ge, h12)
+    need("v", [h12])
+    h13 = new()
+    for o in range(0, 288, 72):
+        tt(B("xq", o, o + 72, 72), B("xr", o, o + 72, 72), X("xm"), OP.mult, h13)
+    need("t", [h13])
+    for h in range(2):
+        o = 144 * h
+        P.matmul(T.b1[:, 72 * h:72 * h + 72], B("onh", p=72), B("xq", o, o + 72, 72), True, False)
+        m = P.matmul(T.b1[:, 72 * h:72 * h + 72], B("xlg", 128 * h, 128 * h + 128, 72),
+                     B("xq", o + 72, o + 144, 72), False, True)
+    h14 = inc(m, new())
+    need("v", [h14])
+    h15 = new()
+    for h in range(2):
+        tt(B("xo", 72 * h, 72 * h + 72), T.b1[:, 72 * h:72 * h + 72], X("base", 72, 128), OP.add, h15)
+    need("v", [h15])
+    return ts(T.il[:], B("xo"), 0.0, OP.max, new(), float(N * S1 - 1), OP.min)
 
-    def mklist(d):
-        if d not in tl:
-            tl[d] = new()
-            ts(T.sl[:, d * 32:d * 32 + 32], T.tq[:, 0:32], T.b6[:, d:d + 1], OP.add, tl[d])
 
-    def gather(n, d, c0, c1, out):
-        need(n, [tl[d], f2, f3, c7])
-        src = T.xs[:, 0:W + CAP].indirect(T.sl[:, d * 32 + c0 // 16:d * 32 + c1 // 16])
-        if n == "v":
-            return inc(V.tensor_copy(out, src), new())
-        return inc(S.activation(out, src, ActivationFunctionType.Copy), new())
-
-    sent = 0
-    grp = groups[core]
-    for i, pair in enumerate(grp):
-        for piece in pair + grp[i + 1][0:1] if i + 1 < len(grp) else pair:
-            mklist(T.rank_of(piece[0][-1]))
-        done, tr = [], []
-        for n, piece in zip("sv", pair):
-            path, c0, c1 = piece
-            d = T.rank_of(path[-1])
-            out = T.slots[:, d * CAP + c0:d * CAP + c1]
-            done.append(gather(n, d, c0, c1, out))
-            tr.append(_hop(T, topo, jobs, piece, core, out))
-            sent += _n(topo, core, path[1])
-        need("g", done)
-        g.remote_dma_fused(tr, local_sem=T.sem.sent)
-    mklist(r)
-    town = gather("v", r, 0, CAP, T.land[:, r * CAP:(r + 1) * CAP])
-
-    V.wait_ge(T.sem.tabh, 8)
-    P.wait_ge(T.sem.tabh, 8)
+def _rlist(g, T, tools, r):
+    B, new, need, inc, ts, cp, tt = tools[0:7]
+    V, P = g.vector, g.tensor
     k2 = new()
-    inc(V.tensor_tensor(B("pa"), T.b5[:, 0:36], T.th[:, 0:36], OP.mult), k2)
-    inc(V.tensor_tensor(B("pb"), T.b5[:, 0:36], T.th[:, 36:72], OP.mult), k2)
+    tt(B("pa"), T.b5[:, 0:36], T.th[:, 0:36], OP.mult, k2)
+    tt(B("pb"), T.b5[:, 0:36], T.th[:, 36:72], OP.mult, k2)
     need("v", [k2])
     k3 = new()
     for j in range(3):
@@ -389,69 +293,370 @@ def rank_program(g, core, T, topo):
     need("v", [k3])
     k4 = new()
     ts(B("u"), B("cols", 0, 2), -1.0, OP.mult, k4, float(W * r), OP.add)
+    ts(B("u2"), B("cols", 0, 2), -1.0, OP.mult, k4, float(W * r + W), OP.add)
     need("v", [k4])
     k5 = new()
-    inc(V.tensor_tensor(B("zm"), B("u"), B("cols", 4, 6), OP.min), k5)
+    tt(B("zm", 0, 2), B("u"), B("cols", 4, 6), OP.min, k5)
+    tt(B("zm", 2, 4), B("u2"), B("cols", 4, 6), OP.min, k5)
     ts(B("lr", 0, 2), B("u"), -1.0, OP.mult, k5)
-    inc(V.tensor_tensor(B("lr", 2, 4), B("cols", 4, 6), B("u"), OP.subtract), k5)
-    inc(V.tensor_tensor(B("t1"), B("u"), B("cols", 2, 4), OP.add), k5)
+    tt(B("lr", 2, 4), B("cols", 4, 6), B("u"), OP.subtract, k5)
+    tt(B("t1"), B("u"), B("cols", 2, 4), OP.add, k5)
     need("v", [k5])
-    k6 = new()
-    ts(B("zd"), B("zm"), 0.0, OP.max, k6)
+    k6 = ts(B("zd"), B("zm"), 0.0, OP.max, new())
     need("t", [k6])
-    k7 = inc(P.matmul(T.b7[:, 0:2], B("bo"), B("zd"), True, True), new())
-    k8 = new()
-    ts(B("li"), B("lr"), 0.0, OP.max, k8, float(W), OP.min)
-    inc(V.tensor_tensor(B("t2"), B("t1"), T.th[:, 72:74], OP.add), k8)
+    k7 = inc(P.matmul(T.b7[:, 0:4], B("bo"), B("zd"), True, True), new())
+    k8 = ts(B("li"), B("lr"), 0.0, OP.max, new(), float(W), OP.min)
     need("v", [k8])
     k9 = new()
     ts(B("lx", 0, 4), B("li"), 4, OP.arith_shift_right, k9)
     ts(B("lx", 4, 8), B("li"), 15, OP.bitwise_and, k9)
     need("v", [k9])
-    k10 = inc(V.tensor_copy(B("lxf"), B("lx")), new())
+    k10 = cp(B("lxf"), B("lx"), new())
     need("v", [k7])
-    inc(V.tensor_tensor(B("dl"), B("t2"), T.b7[:, 0:2], OP.subtract), k10)
+    ts(B("rf", 0, 2), T.b7[:, 0:2], TW, OP.mult, k10, -HALF, OP.add)
+    ts(B("rf", 2, 4), T.b7[:, 2:4], TW, OP.mult, k10, HALF, OP.add)
     need("v", [k10])
+    k10b = cp(B("ri"), B("rf"), new())
+    need("v", [k10b])
+    k10c = new()
+    tt(B("rb"), B("ri", 2, 4), B("ri", 0, 2), OP.subtract, k10c)
+    ts(B("ra"), B("ri", 0, 2), -12.0, OP.mult, k10c)
+    need("v", [k10c])
+    k10d = ts(B("n16"), B("rb"), 0.0625, OP.mult, new())
+    tt(B("t2"), B("t1"), B("ra"), OP.add, k10d)
+    need("t", [k10d])
+    P.matmul(T.b7[:, 8:9], B("gt"), B("n16", 0, 1), True, True)
+    P.matmul(T.b7[:, 9:10], B("onh"), B("n16", 0, 1), True, False)
+    k10e = inc(P.matmul(T.b7[:, 9:10], B("gt"), B("n16", 1, 2), False, True), new())
+    need("v", [k10e, k10d])
+    k10f = ts(B("ov"), T.b7[:, 8:10], 12.0, OP.mult, new())
+    need("v", [k10f])
+    k10g = tt(B("dl"), B("t2"), B("ov"), OP.add, new())
+    need("v", [k10g])
     k11 = new()
     for x in range(2):
         dl = B("dl", x, x + 1)
         for e in range(2):
             o = x * 512 + e * 256
             hs, ls = 2 * e + x, 4 + 2 * e + x
-            ts(B("rg", o, o + 128), B("ci"), B("lxf", hs, hs + 1), OP.is_gt, k11, dl, OP.mult)
-            ts(B("rg", o + 128, o + 256), B("ci"), B("lxf", hs, hs + 1), OP.is_equal, k11, dl, OP.mult)
+            c = B("ci", 0, 128)
+            ts(B("rg", o, o + 128), c, B("lxf", hs, hs + 1), OP.is_gt, k11, dl, OP.mult)
+            ts(B("rg", o + 128, o + 256), c, B("lxf", hs, hs + 1), OP.is_equal, k11, dl, OP.mult)
             o = x * 256 + e * 128
             ts(B("lg", o, o + 128), B("c16"), B("lxf", ls, ls + 1), OP.is_ge, k11, 1.0 - 2.0 * e, OP.mult)
     need("t", [k11])
     for x in range(2):
         for e in range(2):
             o = x * 512 + e * 256
-            P.matmul(T.b7[:, 128:256], T.th[:, 74 + 128 * e:202 + 128 * e], B("rg", o, o + 128), x + e == 0, False)
+            P.matmul(T.b7[:, 128:256], T.th[:, 72 + 128 * e:200 + 128 * e], B("rg", o, o + 128), x + e == 0, False)
             m = P.matmul(T.b7[:, 128:256], B("lg", x * 256 + e * 128, x * 256 + e * 128 + 128),
                          B("rg", o + 128, o + 256), False, x + e == 2)
     k12 = inc(m, new())
     need("v", [k12])
-    k13 = inc(V.tensor_tensor(B("off"), T.b7[:, 128:256], T.tq[:], OP.add), new())
+    k13 = tt(B("off"), T.b7[:, 128:256], T.th[:, 328:456], OP.add, new())
     need("v", [k13])
-    k14 = inc(V.tensor_copy(T.ol[:], B("off")), new())
+    k14 = new()
+    ts(B("vq"), B("off"), TW, OP.mult, k14, -HALF, OP.add)
+    ts(B("v1"), B("off"), float(S2), OP.mult, k14)
+    need("v", [k14])
+    k15 = cp(B("vi"), B("vq"), new())
+    need("v", [k15])
+    k16 = ts(B("v2"), B("vi"), -(12.0 * S2 - 1), OP.mult, new())
+    need("v", [k16])
+    k17 = tt(B("v3"), B("v2"), B("v1"), OP.add, new())
+    need("v", [k17])
+    return cp(T.ol[:], B("v3"), new())
 
-    total = sum(_n(topo, p[0][-2], core) for c in T.cores for pair in groups[c] for p in pair if p[0][-1] == core)
+
+def _deal(T, topo, need, g, c, r, done, xl0, xl1, halves):
+    need("g", done)
+    tr = []
+    for x, to, m in ((0, xl0, halves[0]), (1, xl1, halves[1])):
+        if to is not None:
+            s = (2 * c + x) * S1
+            tr.append(_tr(topo, T.p1[:, s:s + S1], T.xl[:, r * S1:(r + 1) * S1], to, m, T.sem.a1))
+    g.remote_dma_fused(tr, local_sem=T.sem.sent)
+    return sum(bin(t).count("1") for t, to in zip(halves, (xl0, xl1)) if to is not None)
+
+
+def _meet(g, T, topo, core, m, ci, rk, sib, order, need, gather, deps, lo2, hi2):
+    def pack(n, c, k):
+        e = 2 * c + k
+        own = rk[c][k] == core
+        out = T.land[:, m * S2:(m + 1) * S2] if own else T.p2[:, e * S2:(e + 1) * S2]
+        return gather(n, deps, out, T.xl[:, 0:N * S1], T.il[:, 12 * e:12 * e + 12])
+    sent, home = 0, None
+    for i in range(3):
+        c = order[2 + i]
+        done = [pack("v", c, 0), pack("v", c, 1)]
+        o = order[i] if i < 2 else ci
+        near = [pack("s", o, 0), pack("s", o, 1)]
+        tr = []
+        for k in range(2):
+            e = 2 * c + k
+            tr.append(_tr(topo, T.p2[:, e * S2:(e + 1) * S2], T.land[:, m * S2:(m + 1) * S2], rk[c][k], lo2[k],
+                          T.sem.arr))
+            e = 2 * o + k
+            src = T.p2[:, e * S2:(e + 1) * S2]
+            if i < 2:
+                tr.append(_tr(topo, src, T.sb[:, (2 * i + k) * S2:(2 * i + k + 1) * S2], sib, hi2[k],
+                              T.sem["f%d" % i]))
+            elif rk[o][k] != core:
+                tr.append(_tr(topo, src, T.land[:, m * S2:(m + 1) * S2], rk[o][k], hi2[k], T.sem.arr))
+            else:
+                home = near[k]
+        need("g", done + near)
+        g.remote_dma_fused(tr, local_sem=T.sem.sent)
+        sent += 4 * len(tr)
+    return sent, home
+
+
+def _neighbour(g, T, topo, m, rk, order, lo2):
+    for i in range(2):
+        g.wait_ge(T.sem["f%d" % i], 8)
+        g.remote_dma_fused([_tr(topo, T.sb[:, (2 * i + k) * S2:(2 * i + k + 1) * S2],
+                                T.land[:, m * S2:(m + 1) * S2], rk[order[i]][k], lo2[k], T.sem.arr)
+                            for k in range(2)], local_sem=T.sem.sent)
+    return 16
+
+
+def _help(g, core, T, topo, chips, rk, hp):
+    ci = chips.index(topo.chip(core))
+    k = hp[ci].index(core)
+    owner = rk[ci][k]
+    r = T.rank_of(owner)
+    order = [(ci + 1 + i) % 6 for i in range(5)]
+    lo, hi, lo2, hi2 = _masks(topo, core, owner, rk[order[0]][0])
+    tools = _tools(g, T)
+    B, new, need, inc, ts, cp, tt, counters, blocks, sums, gather, close = tools
+    counters()
+    rid, pid, _e = topo.addr(owner)
+    t = new()
+    blocks(t)
+    if k == 0:
+        tab = _xtables(g, T, tools)
+        need("g", [tab])
+        g.remote_dma(T.xt[:], T.xt[:], T.sem.tabh, T.sem.tsent, pid, rid, hi)
+        deps = [t, tab]
+    else:
+        for j in range(3):
+            for x in range(2):
+                ts(T.th[:, 36 * x + 12 * j:36 * x + 12 * j + 12], B("cch", 0, N), B("kcol", x, x + 1), OP.is_equal, t)
+        inc(g.vector.memset(T.th[:, 72:200], 1.0), t)
+        inc(g.vector.memset(T.th[:, 200:328], -1.0), t)
+        ts(T.th[:, 328:456], B("ci", 0, 128), 16.0, OP.mult, t, B("vcol"), OP.add)
+        sums(t)
+        need("g", [t])
+        g.remote_dma(T.th[:], T.th[:], T.sem.tabh, T.sem.tsent, pid, rid, hi)
+        deps = [t]
+    need("v", deps)
+    g.sync.wait_ge(T.sem.earr, 4 * (N - 2) + 16)
+    e1 = inc(g.sync.dma_start(T.el[0:N, :], T.ed[:]), new(), 16)
+    for q in (g.vector, g.scalar):
+        q.wait_ge(T.sem.xa, 16 * XP)
+        q.wait_ge(T.sem.la, 16)
+    sent = 0
+    parts = [gather(n, [], T.p1[:, 2 * c * S1:(2 * c + 2) * S1], T.xin[:, 0:W], T.gl[:, 22 * c:22 * c + 22])
+             for n, c in zip("vs", order)]
+    for c, d in zip(order, parts):
+        sent += _deal(T, topo, need, g, c, r, [d], rk[c][0], hp[c][0], lo2)
+    _counts(g, T, tools, deps + [e1])
+    if k == 0:
+        il = _xlist(g, T, tools)
+        for q in (g.vector, g.scalar):
+            q.wait_ge(T.sem.a1, 4 * N)
+        sent += _meet(g, T, topo, core, 2 * ci + 1, ci, rk, hp[ci][1], order, need, gather, [il], lo2, hi2)[0]
+        g.wait_ge(T.sem.tsent, 8)
+    else:
+        ol = _rlist(g, T, tools, T.rank_of(rk[ci][0]))
+        need("g", [ol])
+        rid, pid, _e = topo.addr(rk[ci][0])
+        g.remote_dma(T.ol[:], T.ol[:], T.sem.ola, T.sem.tsent, pid, rid, hi)
+        sent += _neighbour(g, T, topo, 2 * ci + 1, rk, order, lo2)
+        g.wait_ge(T.sem.tsent, 16)
+    g.wait_ge(T.sem.sent, sent)
+    close()
+
+
+def rank_program(g, core, T, topo):
+    chips, rk, hp = _places(T, topo)
+    r = T.rank_of(core)
+    if r is None:
+        if any(core in h for h in hp):
+            _help(g, core, T, topo, chips, rk, hp)
+        return
+    ci = chips.index(topo.chip(core))
+    kk = rk[ci].index(core)
+    mate, hc = rk[ci][1 - kk], hp[ci][kk]
+    order = [(ci + 1 + i) % 6 for i in range(5)]
+    farr = [c for h in order for c in rk[h]]
+    farh = [c for h in order for c in hp[h]]
+    lo, hi, lo2, hi2 = _masks(topo, core, mate, farr[0])
+    every = topo.mask(core, mate)
+    hid, hpid, _e = topo.addr(hc)
+    first = kk == 0
+
+    V, S, P, Y = g.vector, g.scalar, g.tensor, g.sync
+    tools = _tools(g, T)
+    B, new, need, inc, ts, cp, tt, counters, blocks, sums, gather, close = tools
+
+    tk, txs = new(), [new() for _ in range(XP)]
+    inc(Y.dma_start(T.ki[0:16, :], T.key[:]), tk, 16)
+    for h in range(XP):
+        inc(Y.dma_start(T.xin[:, h * W // XP:(h + 1) * W // XP], T.x[:, h * W // XP:(h + 1) * W // XP]), txs[h], 16)
+
+    counters()
+    for h in range(XP):
+        need("g", [txs[h]])
+        xh = T.xin[:, h * W // XP:(h + 1) * W // XP]
+        g.remote_dma(xh, xh, T.sem.xa, T.sem.tsent, hpid, hid, every)
+    c2, c6 = new(), new()
+    ts(B("selv"), B("c16h"), B("vcol"), OP.is_equal, c2)
+    blocks(c6)
+    ts(B("le"), B("cch", 0, 128), B("pf"), OP.is_le, c6, -1.0, OP.mult)
+
+    need("v", [tk])
+    a1 = cp(B("kh", p=16), T.ki[0:16, :], new())
+    need("t", [c2, a1])
+    a2 = inc(P.matmul(T.b0[:, 0:128], B("selv", p=16), B("kh", p=16), True, True), new())
+    need("v", [c6])
+    c6b = tt(B("lb"), B("le"), B("bo"), OP.mult, new())
+    c3 = new()
+    for h, te in enumerate(("te0", "te1")):
+        ts(B(te, 0, 128), B("c16h"), B("kcol", h, h + 1), OP.is_ge, c3)
+        ts(B(te, 128, 256), B("c16h"), B("kcol", h, h + 1), OP.is_gt, c3)
+    need("v", [a2])
+    a3, a4 = new(), new()
+    for h in range(2):
+        ts(B("oh", h * 128, h * 128 + 128), T.b0[:, 0:128], B("kcol", h, h + 1), OP.is_equal, a3)
+    need("v", [a3])
+    for h in range(2):
+        o = B("oh", h * 128, h * 128 + 128)
+        inc(V.tensor_tensor_scan(B("fs", h * 128, h * 128 + 128), o, o, 0.0, OP.add, OP.max), a4)
+    cnt = [B("fs", 127, 128), B("fs", 255, 256)]
+
+    need("t", [a4, c6, c6b])
+    P.matmul(T.b1[:, 0:256], B("bo"), B("fs"), True, False)
+    d1 = inc(P.matmul(T.b1[:, 0:256], B("lb"), B("oh"), False, True), new())
+    P.matmul(T.b2[:, 0:1], B("gt"), cnt[0], True, True)
+    P.matmul(T.b2[:, 1:2], B("onh"), cnt[0], True, False)
+    d2 = inc(P.matmul(T.b2[:, 1:2], B("gt"), cnt[1], False, True), new())
+    need("t", [c3])
+    P.matmul(T.b5[0:1, 0:256], cnt[0], B("te0"), True, False)
+    a5 = inc(P.matmul(T.b5[0:1, 0:256], cnt[1], B("te1"), False, True), new())
+    c7 = new()
+    cp(B("c16b"), B("c16h"), c7)
+    ts(B("jcol"), B("ci", 0, 16), B("p16"), OP.add, c7)
+    need("v", [d1])
+    d3 = tt(B("mk"), T.b1[:, 0:256], B("oh"), OP.mult, new())
+    need("v", [d2])
+    s16 = B("selv", 0, 16)
+    for h in range(2):
+        ts(B("sbase", h * 16, h * 16 + 16), s16, T.b2[:, h:h + 1], OP.mult, d3)
+    need("t", [d3])
+    P.matmul(T.b3[:, 0:16], B("mk", 0, 128), s16, True, False)
+    P.matmul(T.b3[:, 0:16], B("mk", 128, 256), s16, False, False)
+    P.matmul(T.b3[:, 0:16], B("oh", 0, 128), B("sbase", 0, 16), False, False)
+    d4 = inc(P.matmul(T.b3[:, 0:16], B("oh", 128, 256), B("sbase", 16, 32), False, True), new())
+    need("v", [a5])
+    a6 = cp(T.erow[0:1, :], T.b5[0:1, 0:256], new())
+    need("y", [a6])
+    a7 = inc(Y.dma_start(T.ed[r], T.erow[0:1, :]), new(), 16)
+    need("g", [a7])
+    g.remote_dma_fused([
+        RemoteDMATransfer(srcs=[T.ed[r]], dsts=[T.ed[r] for _ in to], dst_ids=[_did(topo, c) for c in to],
+                          dma_engine_mask=m, remote_sem=T.sem.earr)
+        for to, m in ((farr, lo2[0]), (farh, lo2[1]), ([mate] + hp[ci], hi))], local_sem=T.sem.esent)
+    Y.wait_ge(T.sem.earr, 4 * (N - 2) + 8)
+    need("y", [a7])
+    e1 = inc(Y.dma_start(T.el[0:N, :], T.ed[:]), new(), 16)
+    need("v", [d4])
+    d5 = new()
+    ts(B("qf"), T.b3[:, 0:16], TW, OP.mult, d5, -HALF, OP.add)
+    ts(B("jf"), T.b3[:, 0:16], float(S1), OP.mult, d5)
+    need("v", [d5])
+    d5b = cp(B("qi"), B("qf"), new())
+    need("v", [d5b])
+    d5c = ts(B("pq"), B("qi"), -(12.0 * S1 - 1), OP.mult, new())
+    need("v", [d5c])
+    d5d = tt(B("posi"), B("pq"), B("jf"), OP.add, new())
+    need("v", [d5d])
+    d6 = new()
+    ts(B("lh", 0, 16), B("posi"), 15, OP.bitwise_and, d6)
+    ts(B("lh", 16, 32), B("posi"), 4, OP.arith_shift_right, d6)
+    need("v", [d6])
+    d7 = cp(B("lhf"), B("lh"), new())
+    need("v", [d7, c7])
+    need("s", [d7, c7])
+    n0 = 128 * (16 - VS)
+    w1 = new()
+    for v in range(VS, 16):
+        o = (v - VS) * 128
+        inc(S.activation(B("lab", o, o + 128), B("c16b"), AF.Abs, bias=B("lhf", v, v + 1), scale=-1.0), w1)
+    need("s", [w1])
+    w2 = inc(S.activation(B("lqs", 0, n0), B("lab", 0, n0), AF.Relu, bias=1.0, scale=-1.0), new())
+    for b in range(4):
+        d8 = new()
+        for v in range(4 * b, 4 * b + 4):
+            if v < VS:
+                ts(B("lq", v * 128, v * 128 + 128), B("c16h"), B("lhf", v, v + 1), OP.is_equal, d8)
+            ts(B("rq", v * 132, v * 132 + 132), B("cch"), B("lhf", 16 + v, 17 + v), OP.is_equal, d8,
+               B("jcol", v, v + 1), OP.mult)
+        need("t", [d8])
+        for v in range(4 * b, 4 * b + 4):
+            if v < VS:
+                lq = B("lq", v * 128, v * 128 + 128)
+            else:
+                need("t", [w2])
+                lq = B("lqs", (v - VS) * 128, (v - VS) * 128 + 128)
+            m = P.matmul(T.b4[:, 0:132], lq, B("rq", v * 132, v * 132 + 132), v == 0, v == 15)
+    d9 = inc(m, new())
+    need("v", [d9])
+    f1 = cp(T.gl[:], T.b4[:, 0:132], new())
+
+    need("g", [f1])
+    g.remote_dma(T.gl[:], T.gl[:], T.sem.la, T.sem.tsent, hpid, hid, every)
+    sent = 0
+    parts = []
+    for n, c in zip("vsvs", order[2:5] + [ci]):
+        parts.append(gather(n, [f1] + txs, T.p1[:, 2 * c * S1:(2 * c + 2) * S1], T.xin[:, 0:W],
+                            T.gl[:, 22 * c:22 * c + 22]))
+    for c, d in zip(order[2:5], parts):
+        sent += _deal(T, topo, need, g, c, r, [d], rk[c][0], hp[c][0], lo2)
+    sent += _deal(T, topo, need, g, ci, r, parts[3:], None if first else rk[ci][0], hp[ci][0], hi2)
+
+    if first:
+        mine = gather("v", [f1] + txs, T.xl[:, r * S1:(r + 1) * S1], T.xin[:, 0:W], T.gl[:, 22 * ci:22 * ci + 11])
+        for q in (V, P):
+            q.wait_ge(T.sem.tabh, 8)
+        _counts(g, T, tools, [e1, a6])
+        il = _xlist(g, T, tools)
+        for q in (V, S):
+            q.wait_ge(T.sem.a1, 4 * (N - 1))
+        s2, home = _meet(g, T, topo, core, 2 * ci, ci, rk, mate, order, need, gather, [mine, il], lo2, hi2)
+        sent += s2
+        deps = [home]
+        for q in (V, S):
+            q.wait_ge(T.sem.ola, 8)
+    else:
+        tab = new()
+        sums(tab)
+        for q in (V, P):
+            q.wait_ge(T.sem.tabh, 8)
+        _counts(g, T, tools, [e1, a6, tab])
+        deps = [_rlist(g, T, tools, r)]
+        sent += _neighbour(g, T, topo, 2 * ci, rk, order, lo2)
+
+    total = 4 * (N - 1) if first else 4 * N
     V.wait_ge(T.sem.arr, total)
     S.wait_ge(T.sem.arr, total)
     ty = new()
-    for b in range(4):
-        n = "s" if b % 2 else "v"
-        need(n, [k14, town])
-        src = T.land[:, 0:N * CAP].indirect(T.ol[:, b * 32:b * 32 + 32])
-        out = T.yb[:, b * 512:b * 512 + 512]
-        if n == "v":
-            t = inc(V.tensor_copy(out, src), new())
-        else:
-            t = inc(S.activation(out, src, ActivationFunctionType.Copy), new())
+    for n, a, b in (("v", 0, 640), ("s", 640, 1280), ("v", 1280, 1664), ("s", 1664, W)):
+        t = gather(n, deps, T.yb[:, a:b], T.land[:, 0:N * S2], T.ol[:, a // 16:b // 16])
         need("y", [t])
-        inc(Y.dma_start(T.y[:, b * 512:b * 512 + 512], out), ty, 16)
+        inc(Y.dma_start(T.y[:, a:b], T.yb[:, a:b]), ty, 16)
     need("y", [ty])
-    g.wait_ge(T.sem.tsent, 16)
+    g.wait_ge(T.sem.tsent, 16 * XP + 16)
     g.wait_ge(T.sem.esent, 16)
     g.wait_ge(T.sem.sent, sent)
     close()

@@ -2,36 +2,35 @@ from concourse.bass import DstId, RemoteDMATransfer
 from concourse.mybir import AluOpType as OP, AxisListType, ActivationFunctionType as AF
 
 N, W, SIM = 12, 2048, 112
-S1, S2 = 176, 192
-TW, HALF = 1.0 / 12, 11.0 / 24
+NU = 16
+S1, S2, G2 = 128, 152, 160
 VS = 11
-XP = 4
+XB = (0, 512, W)
 F32, F16, BF, I32, U16 = "float32", "float16", "bfloat16", "int32", "uint16"
 SCRATCH = {
-    "xin": ("sbuf", [128, W], F32), "p1": ("sbuf", [128, N * S1], F32), "xl": ("sbuf", [128, N * S1], F32),
-    "p2": ("sbuf", [128, N * S2], F32), "sb": ("sbuf", [128, 4 * S2], F32), "land": ("sbuf", [128, N * S2], F32),
-    "yb": ("sbuf", [128, W], F32),
+    "xin": ("sbuf", [128, W], F32), "p1": ("sbuf", [128, W], F32), "xl": ("sbuf", [128, N * S1], F32),
+    "p2": ("sbuf", [128, N * G2], F32), "sb": ("sbuf", [128, 4 * S2], F32),
+    "land": ("sbuf", [128, NU * S2 + G2 - S2], F32), "yb": ("sbuf", [128, W], F32),
     "ki": ("sbuf", [128, 128], I32), "erow": ("sbuf", [128, 256], F16), "el": ("sbuf", [128, 256], F16),
-    "gl": ("sbuf", [128, 132], U16), "il": ("sbuf", [128, 144], U16), "ol": ("sbuf", [128, 128], U16),
-    "xt": ("sbuf", [128, 664], F16), "th": ("sbuf", [128, 456], F32),
+    "gl": ("sbuf", [128, 128], U16), "il": ("sbuf", [128, 120], U16), "ol": ("sbuf", [128, 128], U16),
+    "xt": ("sbuf", [128, 816], F16), "th": ("sbuf", [128, 456], F32),
     "ed": ("dram", [N, 128, 2], F16),
 }
 for _i in range(8):
     SCRATCH["b%d" % _i] = ("psum", [128, 512], F32)
 _TILES = {
-    F16: (("kh", 128), ("oh", 256), ("fs", 256), ("mk", 256), ("sbase", 32), ("lq", 2048), ("rq", 16 * 132),
-          ("selv", 128), ("c16h", 128), ("kch", 128), ("cch", 132), ("bo", 128), ("gt", 128), ("le", 128),
-          ("lb", 128), ("te0", 256), ("te1", 256), ("onh", 128), ("zd", 4), ("n16", 2), ("z2", 288), ("xg", 72),
-          ("xy", 72), ("xz", 72), ("an", 2), ("nn", 2), ("xr", 288), ("xq", 288), ("xlg", 256)),
-    BF: (("c16b", 128), ("lab", 640), ("lqs", 640)),
-    F32: (("lhf", 32), ("qf", 16), ("jf", 16), ("pq", 16), ("pf", 1), ("p16", 1), ("vcol", 1), ("kcol", 2),
-          ("jcol", 16), ("pa", 36), ("pb", 36), ("cols", 6), ("u", 2), ("u2", 2), ("zm", 4), ("lr", 4), ("lxf", 8),
-          ("t1", 2), ("t2", 2), ("dl", 2), ("rf", 4), ("rb", 2), ("ra", 2), ("ov", 2), ("rg", 1024), ("lg", 512),
-          ("off", 128), ("vq", 128), ("v1", 128), ("v2", 128), ("v3", 128), ("z1", 288), ("df", 1), ("dcol", 1),
-          ("sm", 1), ("fq", 4), ("ohl", 4), ("xd", 2), ("xo", 144)),
-    I32: (("posi", 16), ("qi", 16), ("lh", 32), ("ci", 132), ("c16", 128), ("kc", 128), ("pi", 1), ("pk", 2),
-          ("li", 4), ("lx", 8), ("ri", 4), ("vi", 128), ("wd", 24), ("cc", 72), ("cd", 72), ("di", 1), ("qx", 4),
-          ("oi", 2), ("oh2", 4)),
+    F16: (("oh", 256), ("fs", 256), ("mk", 256), ("sbase", 32), ("lq", 2048), ("rq", 2048),
+          ("selv", 128), ("bo", 128), ("gt", 128), ("le", 128), ("lb", 128), ("te0", 256), ("te1", 256), ("onh", 128),
+          ("zd", 4), ("n16", 2), ("z2", 288), ("xg", 72), ("xy", 72), ("xz", 72), ("xn", 72), ("xm", 60), ("xc", 60),
+          ("xe", 60), ("an", 2), ("nn", 2), ("xr", 240), ("xlg", 512)),
+    BF: (("c16b", 128), ("kcb", 128), ("ccb", 128), ("lab", 640), ("lqs", 640)),
+    F32: (("lhf", 32), ("pf", 1), ("omp", 2), ("vcol", 1), ("kcol", 2), ("jcol", 16), ("pa", 36), ("pb", 36),
+          ("cols", 6), ("u", 2), ("u2", 2), ("zm", 4), ("lr", 4), ("lxf", 8), ("t1", 2), ("t2", 2), ("dl", 2),
+          ("rb", 2), ("ra", 2), ("ov", 2), ("rg", 1024), ("lg", 512), ("v2", 128), ("v3", 128), ("z1", 288),
+          ("df", 1), ("dcol", 1), ("sm", 1), ("ohl", 2), ("xd", 2)),
+    I32: (("posi", 16), ("lh", 32), ("pi", 1), ("pk", 2), ("li", 4), ("lx", 8), ("ri", 4), ("rj", 4), ("vi", 128),
+          ("vk", 128), ("vr", 128), ("vs", 128), ("wd", 24), ("cc", 60), ("cb", 60), ("cd", 60), ("ce", 72), ("di", 1),
+          ("qx", 4), ("qy", 4), ("oi", 2), ("oh2", 2)),
 }
 _AT = {}
 for _dt, _ts in _TILES.items():
@@ -40,21 +39,34 @@ for _dt, _ts in _TILES.items():
         _AT[_n] = ("m_" + _dt, _o, _w, _dt)
         _o += (_w + 31) // 32 * 32
     SCRATCH["m_" + _dt] = ("sbuf", [128, _o], _dt)
-_XT = {"tr": 0, "xu": 200, "xb": 272, "xs": 344, "xm": 416, "cc": 488, "base": 560, "wd": 632, "s176": 656}
-NSEM = 110
-SEMAPHORES = (["earr", "arr", "a1", "sent", "esent", "tabh", "tsent", "xa", "la", "ola", "f0", "f1"]
+XA, XC, XE = 200, 568, 816
+_XT = {"xu": (200, 72), "xb": (272, 72), "xs": (344, 72), "cm": (416, 60), "cn": (476, 60), "wd": (536, 24),
+       "s1": (560, 8), "l2": (568, 128), "r2": (696, 120)}
+NSEM = 100
+SEMAPHORES = (["earr", "elr", "arr", "a1", "sent", "esent", "tabh", "tsent", "xa", "la", "ila", "ola", "f0", "f1"]
               + ["s%d" % i for i in range(NSEM)])
 
 
 def _places(T, topo):
     chips = sorted(set(topo.chip(c) for c in T.cores))
     rk = [sorted(c for c in T.cores if topo.chip(c) == h) for h in chips]
-    hp = []
-    for i, h in enumerate(chips):
+    hp, ls, ex = [], [], []
+
+    def able(h, d):
         far = [t for t in T.cores if topo.chip(t) != h]
-        hp.append([c for c in range(SIM) if topo.chip(c) == h and T.rank_of(c) is None
-                   and topo.die(c) != topo.die(rk[i][0]) and all(topo.may_write(c, t) for t in far)][0:2])
-    return chips, rk, hp
+        return [c for c in range(SIM) if topo.chip(c) == h and topo.die(c) == d and T.rank_of(c) is None
+                and all(topo.may_write(c, t) for t in far)][0:2]
+    for i, h in enumerate(chips):
+        d = topo.die(rk[i][0])
+        hp.append(able(h, 1 - d))
+        ls.append([c for c in range(SIM) if topo.chip(c) == h and c not in rk[i] + hp[i]][0])
+    d = topo.die(rk[0][0])
+    nchips = topo.chip(SIM - 1) + 1
+    for h in chips:
+        for m in range(nchips):
+            if topo.mates(h, m) and m not in chips and len(ex) < 2:
+                ex.append([able(m, d), able(m, 1 - d)])
+    return chips, rk, hp, ls, ex
 
 
 def _masks(topo, core, near, far):
@@ -73,7 +85,8 @@ def _did(topo, c):
 
 
 def _tr(topo, src, dst, to, mask, sem):
-    return RemoteDMATransfer(srcs=[src], dsts=[dst], dst_ids=[_did(topo, to)], dma_engine_mask=mask, remote_sem=sem)
+    return RemoteDMATransfer(srcs=[src], dsts=[dst for _ in to], dst_ids=[_did(topo, c) for c in to],
+                             dma_engine_mask=mask, remote_sem=sem)
 
 
 def _tools(g, T):
@@ -113,39 +126,39 @@ def _tools(g, T):
     def tt(out, a, b, op, t):
         return inc(g.vector.tensor_tensor(out, a, b, op), t)
 
+    def iota(name, pattern, mult):
+        return inc(g.iota(B(name), pattern, 0, mult, allow_small_or_imprecise_dtypes=True), new())
+
     def counters():
         i1 = inc(g.iota(B("pi"), [[0, 1]], 0, 1), new())
-        i2 = inc(g.iota(B("ci"), [[1, 132]], 0, 0), new())
+        rows = [iota("c16b", [[0, 8], [1, 16]], 0), iota("kcb", [[1, 8], [0, 16]], 0), iota("ccb", [[1, 128]], 0),
+                iota("pf", [[0, 1]], 1)]
         c1 = new()
         need("v", [i1])
         ts(B("pk", 0, 1), B("pi"), 4, OP.arith_shift_right, c1)
         ts(B("pk", 1, 2), B("pi"), 15, OP.bitwise_and, c1)
-        cp(B("pf"), B("pi"), c1)
-        ts(B("p16"), B("pi"), 16, OP.mult, c1)
-        need("v", [i2])
-        ts(B("c16"), B("ci", 0, 128), 15, OP.bitwise_and, c1)
-        ts(B("kc"), B("ci", 0, 128), 4, OP.arith_shift_right, c1)
-        cp(B("cch"), B("ci"), c1)
         need("v", [c1])
         c2 = new()
         ts(B("kcol", 0, 1), B("pk", 0, 1), 0, OP.add, c2)
         ts(B("kcol", 1, 2), B("pk", 0, 1), 8, OP.add, c2)
         cp(B("vcol"), B("pk", 1, 2), c2)
-        cp(B("c16h"), B("c16"), c2)
-        cp(B("kch"), B("kc"), c2)
         need("v", [c2])
+        return rows
+
+    def ones(t):
+        return ts(B("onh"), B("ccb"), 0.0, OP.is_ge, t)
 
     def blocks(t):
-        ts(B("bo"), B("kch"), B("kcol", 0, 1), OP.is_equal, t)
-        ts(B("gt"), B("kch"), B("kcol", 0, 1), OP.is_gt, t)
-        ts(B("onh"), B("cch", 0, 128), 0.0, OP.is_ge, t)
+        ts(B("bo"), B("kcb"), B("kcol", 0, 1), OP.is_equal, t)
+        ts(B("gt"), B("kcb"), B("kcol", 0, 1), OP.is_gt, t)
+        ones(t)
 
     def sums(t):
-        c12 = B("cch", 0, N)
+        c12 = B("ccb", 0, N)
         for a, op, mul in ((0, OP.is_gt, 1.0), (12, OP.is_equal, 0.0), (24, OP.is_equal, 1.0),
                            (36, OP.is_le, 1.0), (48, OP.is_equal, 1.0), (60, OP.is_equal, -1.0)):
             ts(T.xt[:, a:a + N], c12, B("pf"), op, t, mul, OP.mult)
-        ts(T.xt[:, 72:200], B("cch", 0, 128), 0.0, OP.is_ge, t, 0.125, OP.mult)
+        return ts(T.xt[:, 72:XA], B("ccb"), 0.0, OP.is_ge, t, 0.125, OP.mult)
 
     def gather(n, deps, out, win, off):
         need(n, deps)
@@ -158,7 +171,7 @@ def _tools(g, T):
         for t in toks:
             if not t["w"]:
                 need("g", [t])
-    return B, new, need, inc, ts, cp, tt, counters, blocks, sums, gather, close
+    return B, new, need, inc, ts, cp, tt, counters, blocks, sums, gather, close, ones, iota
 
 
 def _counts(g, T, tools, deps):
@@ -169,23 +182,23 @@ def _counts(g, T, tools, deps):
     need("v", [h1])
 
 
+def _X(T, n, p=128):
+    return T.xt[0:p, _XT[n][0]:_XT[n][0] + _XT[n][1]]
+
+
 def _xtables(g, T, tools):
     B, new, need, inc, ts, cp, tt = tools[0:7]
-
-    def X(n, w=72):
-        return T.xt[:, _XT[n]:_XT[n] + w]
     i4 = new()
-    inc(g.iota(B("cc"), [[0, 6], [1, 12]], 0, 0), i4)
-    inc(g.iota(B("cd"), [[1, 6], [0, 12]], 0, 0), i4)
+    inc(g.iota(B("cc"), [[0, 6], [1, 10]], 0, 0), i4)
+    inc(g.iota(B("cd"), [[1, 6], [0, 10]], 0, 0), i4)
+    inc(g.iota(B("ce"), [[1, 6], [0, 12]], 0, 0), i4)
     for h in range(2):
         inc(g.iota(B("wd", 12 * h, 12 * h + 12), [[W, 6], [6 * W, 2]], W * h, 0), i4)
     need("v", [i4])
     c8 = new()
-    tools[9](c8)
-    cp(X("cc"), B("cc"), c8)
-    cp(X("wd", 24), B("wd"), c8)
-    ts(B("df"), B("pf"), TW, OP.mult, c8, -HALF, OP.add)
-    ts(X("base"), B("cc"), 16.0, OP.mult, c8, B("vcol"), OP.add)
+    cp(_X(T, "wd"), B("wd"), c8)
+    ts(B("df"), B("pf"), 1.0 / 12, OP.mult, c8, -11.0 / 24, OP.add)
+    ts(B("xc"), B("cc"), 16.0, OP.mult, c8, 64.0, OP.add)
     need("v", [c8])
     c9 = cp(B("di"), B("df"), new())
     need("v", [c9])
@@ -193,33 +206,47 @@ def _xtables(g, T, tools):
     need("v", [c10])
     c11 = new()
     ts(B("sm"), B("dcol"), -12.0, OP.mult, c11, B("pf"), OP.add)
-    ts(X("xm"), B("cd"), B("dcol"), OP.is_equal, c11)
-    ts(B("xg"), B("cch", 0, 72), B("pf"), OP.is_gt, c11)
-    ts(B("xy"), B("cch", 0, 72), B("pf"), OP.subtract, c11, 1.0, OP.is_equal)
-    ts(X("xb"), B("cch", 0, 72), B("pf"), OP.is_equal, c11)
+    ts(B("xm"), B("cd"), B("dcol"), OP.is_equal, c11)
+    ts(B("xn"), B("ce"), B("dcol"), OP.is_equal, c11)
+    ts(B("xg"), B("ccb", 0, 72), B("pf"), OP.is_gt, c11)
+    ts(B("xy"), B("ccb", 0, 72), B("pf"), OP.subtract, c11, 1.0, OP.is_equal)
+    ts(_X(T, "xb"), B("ccb", 0, 72), B("pf"), OP.is_equal, c11)
     need("v", [c11])
     c12 = new()
-    tt(X("xu"), B("xg"), X("xm"), OP.mult, c12)
-    tt(B("xz"), B("xy"), X("xm"), OP.mult, c12)
+    tt(_X(T, "xu"), B("xg"), B("xn"), OP.mult, c12)
+    tt(B("xz"), B("xy"), B("xn"), OP.mult, c12)
+    tt(B("xe"), B("xc"), B("xm"), OP.mult, c12)
     need("v", [c12])
     c13 = new()
-    tt(X("xb"), X("xb"), B("xz"), OP.subtract, c13)
-    ts(X("xs"), B("xz"), -1.0, OP.mult, c13)
-    ts(X("s176", 8), B("cch", 0, 8), 0.0, OP.is_ge, c13, B("sm"), OP.mult)
+    tt(_X(T, "xb"), _X(T, "xb"), B("xz"), OP.subtract, c13)
+    ts(_X(T, "xs"), B("xz"), -1.0, OP.mult, c13)
+    ts(_X(T, "cm"), B("xe"), -64.0, OP.add, c13)
+    ts(_X(T, "cn"), B("xe"), -48.0, OP.add, c13)
+    ts(_X(T, "s1"), B("ccb", 0, 8), 0.0, OP.is_ge, c13, B("sm"), OP.mult)
     need("v", [c13])
-    return ts(X("s176", 8), X("s176", 8), 0.0, OP.is_gt, new(), float(S1), OP.mult)
+    return ts(_X(T, "s1"), _X(T, "s1"), 0.0, OP.is_gt, new(), float(S1), OP.mult)
+
+
+def _base(g, T, tools):
+    B, new, need, inc, ts, cp, tt = tools[0:7]
+    i5 = inc(g.iota(B("cb"), [[0, 6], [1, 10]], 0, 0), new())
+    c14 = ts(B("omp", 0, 1), B("pf"), -1.0, OP.mult, new(), 1.0, OP.add)
+    ts(B("omp", 1, 2), B("pf"), -16.0, OP.mult, c14, 16.0, OP.add)
+    need("v", [c14, i5])
+    c15 = ts(_X(T, "l2"), B("c16b"), B("pf"), OP.mult, new(), B("omp", 0, 1), OP.add)
+    o = _XT["r2"][0]
+    for h in range(2):
+        ts(T.xt[:, o + 60 * h:o + 60 * h + 60], B("cb"), B("omp", 1, 2), OP.mult, c15, B("pf"), OP.add)
+    return c15
 
 
 def _xlist(g, T, tools):
     B, new, need, inc, ts, cp, tt = tools[0:7]
     P = g.tensor
-
-    def X(n, w=72, p=72):
-        return T.xt[0:p, _XT[n]:_XT[n] + w]
     zb, zo, _w, _d = _AT["z1"]
     h2 = new()
     for s in range(N):
-        ts(T[zb][0:128, zo + s:zo + 288:12], X("wd", 24, 128), T.b5[:, s:s + 1], OP.subtract, h2,
+        ts(T[zb][0:128, zo + s:zo + 288:12], _X(T, "wd"), T.b5[:, s:s + 1], OP.subtract, h2,
            T.b5[:, 24 + s:25 + s], OP.min)
     need("v", [h2])
     h3 = ts(B("z2"), B("z1"), 0.0, OP.max, new())
@@ -229,56 +256,49 @@ def _xlist(g, T, tools):
     h4 = inc(m, new())
     need("v", [h4])
     h5 = new()
-    ts(B("fq", 0, 2, 72), T.b6[0:72, 0:2], TW, OP.mult, h5, -HALF, OP.add)
-    ts(B("fq", 2, 4, 72), T.b6[0:72, 2:4], TW, OP.mult, h5, HALF, OP.add)
+    ts(B("qx", 0, 2, 72), T.b6[0:72, 0:2], 0.0, OP.add, h5)
+    ts(B("qx", 2, 4, 72), T.b6[0:72, 2:4], 15.0, OP.add, h5)
     need("v", [h5])
-    h6 = cp(B("qx", p=72), B("fq", p=72), new())
+    h6 = ts(B("qy", p=72), B("qx", p=72), 4, OP.arith_shift_right, new())
     need("v", [h6])
     h7 = new()
-    cp(B("an", p=72), B("qx", 0, 2, 72), h7)
-    tt(B("nn", p=72), B("qx", 2, 4, 72), B("qx", 0, 2, 72), OP.subtract, h7)
+    cp(B("an", p=72), B("qy", 0, 2, 72), h7)
+    tt(B("nn", p=72), B("qy", 2, 4, 72), B("qy", 0, 2, 72), OP.subtract, h7)
     need("t", [h7])
-    P.matmul(T.b0[0:72, 0:2], X("xu"), B("nn", p=72), True, True)
-    P.matmul(T.b0[0:72, 2:4], X("xb"), B("an", p=72), True, False)
-    h8 = inc(P.matmul(T.b0[0:72, 2:4], X("xs"), B("nn", p=72), False, True), new())
+    P.matmul(T.b0[0:72, 0:2], _X(T, "xu", 72), B("nn", p=72), True, True)
+    P.matmul(T.b0[0:72, 2:4], _X(T, "xb", 72), B("an", p=72), True, False)
+    h8 = inc(P.matmul(T.b0[0:72, 2:4], _X(T, "xs", 72), B("nn", p=72), False, True), new())
     need("v", [h8])
-    h9 = new()
-    cp(B("oi", p=72), T.b0[0:72, 0:2], h9)
-    tt(B("xd", p=72), T.b0[0:72, 2:4], X("s176", 2), OP.add, h9)
+    h9 = cp(B("oi", p=72), T.b0[0:72, 0:2], new())
+    h9b = tt(B("xd", p=72), T.b0[0:72, 2:4], T.xt[0:72, _XT["s1"][0]:_XT["s1"][0] + 2], OP.add, new())
     need("v", [h9])
-    h10 = new()
-    ts(B("oh2", 0, 2, 72), B("oi", p=72), 4, OP.arith_shift_right, h10)
-    ts(B("oh2", 2, 4, 72), B("oi", p=72), 15, OP.bitwise_and, h10)
+    h10 = ts(B("oh2", p=72), B("oi", p=72), 15, OP.bitwise_and, new())
+    need("v", [h9b])
+    h12 = new()
+    for h in range(2):
+        for o, n in ((0, "cm"), (60, "cn")):
+            ts(B("xr", 120 * h + o, 120 * h + o + 60, 72), _X(T, n, 72), T.b0[0:72, h:h + 1], OP.is_gt, h12,
+               B("xd", h, h + 1, 72), OP.mult)
     need("v", [h10])
     h11 = cp(B("ohl", p=72), B("oh2", p=72), new())
     need("v", [h11])
-    h12 = new()
     for h in range(2):
-        hs, xd = B("ohl", h, h + 1, 72), B("xd", h, h + 1, 72)
-        o = 144 * h
-        ts(B("xr", o, o + 72, 72), X("cc"), hs, OP.is_gt, h12, xd, OP.mult)
-        ts(B("xr", o + 72, o + 144, 72), X("cc"), hs, OP.is_equal, h12, xd, OP.mult)
-        ts(B("xlg", 128 * h, 128 * h + 128, 72), B("c16h", p=72), B("ohl", 2 + h, 3 + h, 72), OP.is_ge, h12)
-    need("v", [h12])
-    h13 = new()
-    for o in range(0, 288, 72):
-        tt(B("xq", o, o + 72, 72), B("xr", o, o + 72, 72), X("xm"), OP.mult, h13)
-    need("t", [h13])
+        for o, op in ((0, OP.is_lt), (128, OP.is_ge)):
+            ts(B("xlg", 256 * h + o, 256 * h + o + 128, 72), B("c16b", p=72), B("ohl", h, h + 1, 72), op, h12)
+    o = _XT["r2"][0]
+    need("t", [h12])
     for h in range(2):
-        o = 144 * h
-        P.matmul(T.b1[:, 72 * h:72 * h + 72], B("onh", p=72), B("xq", o, o + 72, 72), True, False)
-        m = P.matmul(T.b1[:, 72 * h:72 * h + 72], B("xlg", 128 * h, 128 * h + 128, 72),
-                     B("xq", o + 72, o + 144, 72), False, True)
+        out = T.b1[:, 60 * h:60 * h + 60]
+        P.matmul(out, _X(T, "l2", 2), T.xt[0:2, o + 60 * h:o + 60 * h + 60], True, False)
+        P.matmul(out, B("xlg", 256 * h, 256 * h + 128, 72), B("xr", 120 * h, 120 * h + 60, 72), False, False)
+        m = P.matmul(out, B("xlg", 256 * h + 128, 256 * h + 256, 72), B("xr", 120 * h + 60, 120 * h + 120, 72),
+                     False, True)
     h14 = inc(m, new())
     need("v", [h14])
-    h15 = new()
-    for h in range(2):
-        tt(B("xo", 72 * h, 72 * h + 72), T.b1[:, 72 * h:72 * h + 72], X("base", 72, 128), OP.add, h15)
-    need("v", [h15])
-    return ts(T.il[:], B("xo"), 0.0, OP.max, new(), float(N * S1 - 1), OP.min)
+    return ts(T.il[:], T.b1[:, 0:120], 0.0, OP.max, new(), float(N * S1 - 1), OP.min)
 
 
-def _rlist(g, T, tools, r):
+def _rlist(g, T, tools, r, first):
     B, new, need, inc, ts, cp, tt = tools[0:7]
     V, P = g.vector, g.tensor
     k2 = new()
@@ -313,14 +333,14 @@ def _rlist(g, T, tools, r):
     need("v", [k9])
     k10 = cp(B("lxf"), B("lx"), new())
     need("v", [k7])
-    ts(B("rf", 0, 2), T.b7[:, 0:2], TW, OP.mult, k10, -HALF, OP.add)
-    ts(B("rf", 2, 4), T.b7[:, 2:4], TW, OP.mult, k10, HALF, OP.add)
+    ts(B("ri", 0, 2), T.b7[:, 0:2], 0.0, OP.add, k10)
+    ts(B("ri", 2, 4), T.b7[:, 2:4], 15.0, OP.add, k10)
     need("v", [k10])
-    k10b = cp(B("ri"), B("rf"), new())
+    k10b = ts(B("rj"), B("ri"), 4, OP.arith_shift_right, new())
     need("v", [k10b])
     k10c = new()
-    tt(B("rb"), B("ri", 2, 4), B("ri", 0, 2), OP.subtract, k10c)
-    ts(B("ra"), B("ri", 0, 2), -12.0, OP.mult, k10c)
+    tt(B("rb"), B("rj", 2, 4), B("rj", 0, 2), OP.subtract, k10c)
+    ts(B("ra"), B("rj", 0, 2), -16.0, OP.mult, k10c)
     need("v", [k10c])
     k10d = ts(B("n16"), B("rb"), 0.0625, OP.mult, new())
     tt(B("t2"), B("t1"), B("ra"), OP.add, k10d)
@@ -329,7 +349,7 @@ def _rlist(g, T, tools, r):
     P.matmul(T.b7[:, 9:10], B("onh"), B("n16", 0, 1), True, False)
     k10e = inc(P.matmul(T.b7[:, 9:10], B("gt"), B("n16", 1, 2), False, True), new())
     need("v", [k10e, k10d])
-    k10f = ts(B("ov"), T.b7[:, 8:10], 12.0, OP.mult, new())
+    k10f = ts(B("ov"), T.b7[:, 8:10], 16.0, OP.mult, new())
     need("v", [k10f])
     k10g = tt(B("dl"), B("t2"), B("ov"), OP.add, new())
     need("v", [k10g])
@@ -339,11 +359,10 @@ def _rlist(g, T, tools, r):
         for e in range(2):
             o = x * 512 + e * 256
             hs, ls = 2 * e + x, 4 + 2 * e + x
-            c = B("ci", 0, 128)
-            ts(B("rg", o, o + 128), c, B("lxf", hs, hs + 1), OP.is_gt, k11, dl, OP.mult)
-            ts(B("rg", o + 128, o + 256), c, B("lxf", hs, hs + 1), OP.is_equal, k11, dl, OP.mult)
+            ts(B("rg", o, o + 128), B("ccb"), B("lxf", hs, hs + 1), OP.is_gt, k11, dl, OP.mult)
+            ts(B("rg", o + 128, o + 256), B("ccb"), B("lxf", hs, hs + 1), OP.is_equal, k11, dl, OP.mult)
             o = x * 256 + e * 128
-            ts(B("lg", o, o + 128), B("c16"), B("lxf", ls, ls + 1), OP.is_ge, k11, 1.0 - 2.0 * e, OP.mult)
+            ts(B("lg", o, o + 128), B("c16b"), B("lxf", ls, ls + 1), OP.is_ge, k11, 1.0 - 2.0 * e, OP.mult)
     need("t", [k11])
     for x in range(2):
         for e in range(2):
@@ -353,56 +372,79 @@ def _rlist(g, T, tools, r):
                          B("rg", o + 128, o + 256), False, x + e == 2)
     k12 = inc(m, new())
     need("v", [k12])
-    k13 = tt(B("off"), T.b7[:, 128:256], T.th[:, 328:456], OP.add, new())
+    k13 = tt(B("vi"), T.b7[:, 128:256], T.th[:, 328:456], OP.add, new())
     need("v", [k13])
-    k14 = new()
-    ts(B("vq"), B("off"), TW, OP.mult, k14, -HALF, OP.add)
-    ts(B("v1"), B("off"), float(S2), OP.mult, k14)
+    k14 = ts(B("vk"), B("vi"), float(NU - first), OP.add, new())
+    ts(B("vr"), B("vi"), 4, OP.arith_shift_right, k14)
     need("v", [k14])
-    k15 = cp(B("vi"), B("vq"), new())
+    k15 = ts(B("vs"), B("vk"), 15, OP.bitwise_and, new())
     need("v", [k15])
-    k16 = ts(B("v2"), B("vi"), -(12.0 * S2 - 1), OP.mult, new())
+    k16 = ts(B("v2"), B("vs"), float(S2), OP.mult, new())
     need("v", [k16])
-    k17 = tt(B("v3"), B("v2"), B("v1"), OP.add, new())
+    k17 = tt(B("v3"), B("v2"), B("vr"), OP.add, new())
     need("v", [k17])
     return cp(T.ol[:], B("v3"), new())
 
 
-def _deal(T, topo, need, g, c, r, done, xl0, xl1, halves):
-    need("g", done)
-    tr = []
-    for x, to, m in ((0, xl0, halves[0]), (1, xl1, halves[1])):
-        if to is not None:
-            s = (2 * c + x) * S1
-            tr.append(_tr(topo, T.p1[:, s:s + S1], T.xl[:, r * S1:(r + 1) * S1], to, m, T.sem.a1))
-    g.remote_dma_fused(tr, local_sem=T.sem.sent)
-    return sum(bin(t).count("1") for t, to in zip(halves, (xl0, xl1)) if to is not None)
+def _legs(ci):
+    o = [(ci + 1 + i) % 6 for i in range(5)]
+    far = o[0:2] + [6 + ci % 2] + o[2:4] + [7 - ci % 2] + o[4:]
+    a = [(far[i], 0) for i in range(6)] + [(far[6], 0), (far[6], 1)]
+    b = [(far[(2 + i) % 6], 1) for i in range(6)]
+    return [a[i:i + 2] for i in range(0, 8, 2)], [b[i:i + 2] for i in range(0, 6, 2)]
 
 
-def _meet(g, T, topo, core, m, ci, rk, sib, order, need, gather, deps, lo2, hi2):
+def _deal(g, T, topo, r, legs, main, tools, deps, lo2):
+    need, gather = tools[2], tools[10]
+    parts = []
+    for pair in legs:
+        for n, (e, x) in zip("vs", pair):
+            u = 2 * e + x
+            parts.append(gather(n, deps, T.p1[:, u * S1:(u + 1) * S1], T.xin[:, 0:W], T.gl[:, 8 * u:8 * u + 8]))
+    for i, pair in enumerate(legs):
+        need("g", parts[2 * i:2 * i + 2])
+        tr = []
+        for (e, x), m in zip(pair, lo2):
+            u = 2 * e + x
+            tr.append(_tr(topo, T.p1[:, u * S1:(u + 1) * S1], T.xl[:, r * S1:(r + 1) * S1], [main[e][x]], m, T.sem.a1))
+        g.remote_dma_fused(tr, local_sem=T.sem.sent)
+    return 8 * len(legs)
+
+
+def _slot(T, u, ci):
+    s = (u - 2 * ci - 1) % NU * S2
+    return T.land[:, s:s + S2]
+
+
+def _meet(g, T, topo, core, u, ci, rk, sib, fwd, own, tools, deps, lo2, hi2):
+    need, gather = tools[2], tools[10]
+
     def pack(n, c, k):
         e = 2 * c + k
-        own = rk[c][k] == core
-        out = T.land[:, m * S2:(m + 1) * S2] if own else T.p2[:, e * S2:(e + 1) * S2]
-        return gather(n, deps, out, T.xl[:, 0:N * S1], T.il[:, 12 * e:12 * e + 12])
+        if rk[c][k] == core:
+            out = T.land[:, (NU - 1) * S2:(NU - 1) * S2 + G2]
+        else:
+            out = T.p2[:, e * G2:(e + 1) * G2]
+        return gather(n, deps, out, T.xl[:, 0:N * S1], T.il[:, 10 * e:10 * e + 10])
     sent, home = 0, None
-    for i in range(3):
-        c = order[2 + i]
-        done = [pack("v", c, 0), pack("v", c, 1)]
-        o = order[i] if i < 2 else ci
-        near = [pack("s", o, 0), pack("s", o, 1)]
+    also = fwd + [ci] * (ci is not None) + [None] * len(own)
+    for i, c in enumerate(own):
+        o = also[i]
+        done = [pack("v", c, 0), pack("v" if o is not None else "s", c, 1)]
+        near = [] if o is None else [pack("s", o, 0), pack("s", o, 1)]
         tr = []
         for k in range(2):
             e = 2 * c + k
-            tr.append(_tr(topo, T.p2[:, e * S2:(e + 1) * S2], T.land[:, m * S2:(m + 1) * S2], rk[c][k], lo2[k],
-                          T.sem.arr))
+            tr.append(_tr(topo, T.p2[:, e * G2:e * G2 + S2], _slot(T, u, c), [rk[c][k]], lo2[k], T.sem.arr))
+            if o is None:
+                continue
             e = 2 * o + k
-            src = T.p2[:, e * S2:(e + 1) * S2]
-            if i < 2:
-                tr.append(_tr(topo, src, T.sb[:, (2 * i + k) * S2:(2 * i + k + 1) * S2], sib, hi2[k],
+            src = T.p2[:, e * G2:e * G2 + S2]
+            if i < len(fwd):
+                tr.append(_tr(topo, src, T.sb[:, (2 * i + k) * S2:(2 * i + k + 1) * S2], [sib], hi2[k],
                               T.sem["f%d" % i]))
             elif rk[o][k] != core:
-                tr.append(_tr(topo, src, T.land[:, m * S2:(m + 1) * S2], rk[o][k], hi2[k], T.sem.arr))
+                tr.append(_tr(topo, src, _slot(T, u, o), [rk[o][k]], hi2[k], T.sem.arr))
             else:
                 home = near[k]
         need("g", done + near)
@@ -411,131 +453,225 @@ def _meet(g, T, topo, core, m, ci, rk, sib, order, need, gather, deps, lo2, hi2)
     return sent, home
 
 
-def _neighbour(g, T, topo, m, rk, order, lo2):
-    for i in range(2):
+def _neighbour(g, T, topo, u, rk, fwd, lo2):
+    for i, c in enumerate(fwd):
         g.wait_ge(T.sem["f%d" % i], 8)
-        g.remote_dma_fused([_tr(topo, T.sb[:, (2 * i + k) * S2:(2 * i + k + 1) * S2],
-                                T.land[:, m * S2:(m + 1) * S2], rk[order[i]][k], lo2[k], T.sem.arr)
-                            for k in range(2)], local_sem=T.sem.sent)
-    return 16
+        g.remote_dma_fused([_tr(topo, T.sb[:, (2 * i + k) * S2:(2 * i + k + 1) * S2], _slot(T, u, c), [rk[c][k]],
+                                lo2[k], T.sem.arr) for k in range(2)], local_sem=T.sem.sent)
+    return 8 * len(fwd)
 
 
-def _help(g, core, T, topo, chips, rk, hp):
+def _send(g, topo, buf, to, mask, sem, lsem):
+    rid, pid, _e = topo.addr(to)
+    g.remote_dma(buf, buf, sem, lsem, pid, rid, mask)
+
+
+def _far(ci):
+    o = [(ci + 1 + i) % 6 for i in range(5)]
+    return o[0:1], o[1:5]
+
+
+def _allcounts(g, T, topo, tools, z, to, every):
+    new, need, inc = tools[1:4]
+    need("y", [z])
+    g.sync.wait_ge(T.sem.earr, 8 * N)
+    e1 = inc(g.sync.dma_start(T.el[0:N, :], T.ed[:]), new(), 16)
+    need("g", [z, e1])
+    g.remote_dma_fused([_tr(topo, T.el[:], T.el[:], to, every, T.sem.elr)], local_sem=T.sem.tsent)
+    return e1
+
+
+def _zero(T, tools):
+    B, new, ts = tools[0], tools[1], tools[4]
+    z = new()
+    for h in range(2):
+        ts(T.el[:, 128 * h:128 * h + 128], B("ccb"), 0.0, OP.mult, z)
+    return z
+
+
+def _help(g, core, T, topo, chips, rk, hp, ls, main):
     ci = chips.index(topo.chip(core))
     k = hp[ci].index(core)
     owner = rk[ci][k]
     r = T.rank_of(owner)
-    order = [(ci + 1 + i) % 6 for i in range(5)]
-    lo, hi, lo2, hi2 = _masks(topo, core, owner, rk[order[0]][0])
+    fwd, own = _far(ci)
+    lo, hi, lo2, hi2 = _masks(topo, core, owner, rk[own[0]][0])
+    every = topo.mask(core, owner)
     tools = _tools(g, T)
-    B, new, need, inc, ts, cp, tt, counters, blocks, sums, gather, close = tools
-    counters()
-    rid, pid, _e = topo.addr(owner)
-    t = new()
-    blocks(t)
+    B, new, need, inc, ts, cp, tt, counters, blocks, sums, gather, close, ones, iota = tools
+    need("v", counters())
     if k == 0:
-        tab = _xtables(g, T, tools)
-        need("g", [tab])
-        g.remote_dma(T.xt[:], T.xt[:], T.sem.tabh, T.sem.tsent, pid, rid, hi)
-        deps = [t, tab]
+        tab = [_xtables(g, T, tools), _base(g, T, tools)]
+        need("g", tab)
+        _send(g, topo, T.xt[:, XA:XE], ls[ci], every, T.sem.tabh, T.sem.tsent)
     else:
+        t = new()
         for j in range(3):
             for x in range(2):
-                ts(T.th[:, 36 * x + 12 * j:36 * x + 12 * j + 12], B("cch", 0, N), B("kcol", x, x + 1), OP.is_equal, t)
+                ts(T.th[:, 36 * x + 12 * j:36 * x + 12 * j + 12], B("ccb", 0, N), B("kcol", x, x + 1), OP.is_equal, t)
         inc(g.vector.memset(T.th[:, 72:200], 1.0), t)
         inc(g.vector.memset(T.th[:, 200:328], -1.0), t)
-        ts(T.th[:, 328:456], B("ci", 0, 128), 16.0, OP.mult, t, B("vcol"), OP.add)
-        sums(t)
+        ts(T.th[:, 328:456], B("ccb"), 16.0, OP.mult, t, B("vcol"), OP.add)
         need("g", [t])
-        g.remote_dma(T.th[:], T.th[:], T.sem.tabh, T.sem.tsent, pid, rid, hi)
-        deps = [t]
-    need("v", deps)
-    g.sync.wait_ge(T.sem.earr, 4 * (N - 2) + 16)
-    e1 = inc(g.sync.dma_start(T.el[0:N, :], T.ed[:]), new(), 16)
+        _send(g, topo, T.th[:], owner, every, T.sem.tabh, T.sem.tsent)
+        blocks(t)
+        sums(t)
+        need("v", [t])
     for q in (g.vector, g.scalar):
-        q.wait_ge(T.sem.xa, 16 * XP)
+        q.wait_ge(T.sem.xa, 16 * (len(XB) - 1))
         q.wait_ge(T.sem.la, 16)
-    sent = 0
-    parts = [gather(n, [], T.p1[:, 2 * c * S1:(2 * c + 2) * S1], T.xin[:, 0:W], T.gl[:, 22 * c:22 * c + 22])
-             for n, c in zip("vs", order)]
-    for c, d in zip(order, parts):
-        sent += _deal(T, topo, need, g, c, r, [d], rk[c][0], hp[c][0], lo2)
-    _counts(g, T, tools, deps + [e1])
+    sent = _deal(g, T, topo, r, _legs(ci)[1], main, tools, [], lo2)
     if k == 0:
-        il = _xlist(g, T, tools)
         for q in (g.vector, g.scalar):
+            q.wait_ge(T.sem.ila, 16)
             q.wait_ge(T.sem.a1, 4 * N)
-        sent += _meet(g, T, topo, core, 2 * ci + 1, ci, rk, hp[ci][1], order, need, gather, [il], lo2, hi2)[0]
-        g.wait_ge(T.sem.tsent, 8)
-    else:
-        ol = _rlist(g, T, tools, T.rank_of(rk[ci][0]))
-        need("g", [ol])
-        rid, pid, _e = topo.addr(rk[ci][0])
-        g.remote_dma(T.ol[:], T.ol[:], T.sem.ola, T.sem.tsent, pid, rid, hi)
-        sent += _neighbour(g, T, topo, 2 * ci + 1, rk, order, lo2)
+        sent += _meet(g, T, topo, core, 2 * ci + 1, ci, rk, hp[ci][1], fwd, own, tools, [], lo2, hi2)[0]
         g.wait_ge(T.sem.tsent, 16)
+    else:
+        g.tensor.wait_ge(T.sem.elr, 16)
+        _counts(g, T, tools, [t])
+        ol = _rlist(g, T, tools, T.rank_of(rk[ci][0]), 2 * ci + 1)
+        need("g", [ol])
+        _send(g, topo, T.ol[:], rk[ci][0], hi, T.sem.ola, T.sem.tsent)
+        sent += _neighbour(g, T, topo, 2 * ci + 1, rk, fwd, lo2)
+        g.wait_ge(T.sem.tsent, 24)
+    g.wait_ge(T.sem.sent, sent)
+    close()
+
+
+def _list(g, core, T, topo, ci, rk, hp):
+    every = topo.mask(core, rk[ci][1])
+    tools = _tools(g, T)
+    B, new, need, inc, ts, cp, tt, counters, blocks, sums, gather, close, ones, iota = tools
+    need("v", counters())
+    tab = new()
+    sums(tab)
+    need("g", [tab])
+    _send(g, topo, T.xt[:, 0:72], rk[ci][1], every, T.sem.tabh, T.sem.tsent)
+    z = _zero(T, tools)
+    need("v", [tab])
+    for q in (g.vector, g.tensor):
+        q.wait_ge(T.sem.tabh, 16)
+    e1 = _allcounts(g, T, topo, tools, z, [rk[ci][1], hp[ci][1]], every)
+    _counts(g, T, tools, [tab, e1])
+    il = _xlist(g, T, tools)
+    need("g", [il])
+    g.remote_dma_fused([_tr(topo, T.il[:], T.il[:], [rk[ci][0], hp[ci][0]], every, T.sem.ila)], local_sem=T.sem.tsent)
+    g.wait_ge(T.sem.tsent, 48)
+    close()
+
+
+def _extra(g, core, T, topo, q, x, k, rk, ex):
+    u = 12 + 2 * q + x
+    o = [(3 * q + i) % 6 for i in range(6)]
+    fwd, own = o[0:2], o[2:6]
+    sib, other = ex[q][x][1 - k], ex[q][1 - x][0]
+    lo, hi, lo2, hi2 = _masks(topo, core, sib, rk[0][0])
+    every = topo.mask(core, sib)
+    tools = _tools(g, T)
+    B, new, need, inc, ts, cp, tt, counters, blocks, sums, gather, close, ones, iota = tools
+    need("v", counters())
+    tables = 16
+    if k == 1:
+        tab = _xtables(g, T, tools)
+        need("g", [tab])
+        _send(g, topo, T.xt[:, XA:XC], sib, every, T.sem.tabh, T.sem.tsent)
+        sent = _neighbour(g, T, topo, u, rk, fwd, lo2)
+    else:
+        if x == 0:
+            t = new()
+            sums(t)
+            part = T.xt[:, 0:XA]
+        else:
+            t = _base(g, T, tools)
+            part = T.xt[:, XC:XE]
+        need("g", [t])
+        _send(g, topo, part, other, every, T.sem.tabh, T.sem.tsent)
+        need("v", [t])
+        for n in (g.vector, g.tensor):
+            n.wait_ge(T.sem.tabh, 32)
+        if x == 0:
+            deps = [t, _allcounts(g, T, topo, tools, _zero(T, tools), [other], every)]
+            tables = 32
+        else:
+            g.tensor.wait_ge(T.sem.elr, 16)
+            deps = [t]
+        _counts(g, T, tools, deps)
+        il = _xlist(g, T, tools)
+        for n in (g.vector, g.scalar):
+            n.wait_ge(T.sem.a1, 4 * N)
+        sent = _meet(g, T, topo, core, u, None, rk, sib, fwd, own, tools, [il], lo2, hi2)[0]
+    g.wait_ge(T.sem.tsent, tables)
     g.wait_ge(T.sem.sent, sent)
     close()
 
 
 def rank_program(g, core, T, topo):
-    chips, rk, hp = _places(T, topo)
+    chips, rk, hp, ls, ex = _places(T, topo)
+    main = [[rk[i][0], hp[i][0]] for i in range(6)] + [[e[0][0], e[1][0]] for e in ex]
     r = T.rank_of(core)
     if r is None:
         if any(core in h for h in hp):
-            _help(g, core, T, topo, chips, rk, hp)
+            _help(g, core, T, topo, chips, rk, hp, ls, main)
+        elif core in ls:
+            _list(g, core, T, topo, ls.index(core), rk, hp)
+        for q in range(2):
+            for x in range(2):
+                if core in ex[q][x]:
+                    _extra(g, core, T, topo, q, x, ex[q][x].index(core), rk, ex)
         return
     ci = chips.index(topo.chip(core))
     kk = rk[ci].index(core)
     mate, hc = rk[ci][1 - kk], hp[ci][kk]
-    order = [(ci + 1 + i) % 6 for i in range(5)]
-    farr = [c for h in order for c in rk[h]]
-    farh = [c for h in order for c in hp[h]]
-    lo, hi, lo2, hi2 = _masks(topo, core, mate, farr[0])
+    fwd, own = _far(ci)
+    fars = [ls[i] for i in fwd + own] + [e[0][0] for e in ex]
+    lo, hi, lo2, hi2 = _masks(topo, core, mate, rk[own[0]][0])
     every = topo.mask(core, mate)
-    hid, hpid, _e = topo.addr(hc)
     first = kk == 0
 
     V, S, P, Y = g.vector, g.scalar, g.tensor, g.sync
     tools = _tools(g, T)
-    B, new, need, inc, ts, cp, tt, counters, blocks, sums, gather, close = tools
+    B, new, need, inc, ts, cp, tt, counters, blocks, sums, gather, close, ones, iota = tools
 
-    tk, txs = new(), [new() for _ in range(XP)]
-    inc(Y.dma_start(T.ki[0:16, :], T.key[:]), tk, 16)
-    for h in range(XP):
-        inc(Y.dma_start(T.xin[:, h * W // XP:(h + 1) * W // XP], T.x[:, h * W // XP:(h + 1) * W // XP]), txs[h], 16)
+    tk, txs = new(), [new() for _ in XB[1:]]
+    for q, a in ((Y, 0), (S, 64)):
+        for h in range(a, a + 64, 16):
+            inc(q.dma_start(T.ki[h:h + 16, :], T.key[:]), tk, 16)
+    for a, b, t in zip(XB, XB[1:], txs):
+        inc(Y.dma_start(T.xin[:, a:b], T.x[:, a:b]), t, 16)
 
-    counters()
-    for h in range(XP):
-        need("g", [txs[h]])
-        xh = T.xin[:, h * W // XP:(h + 1) * W // XP]
-        g.remote_dma(xh, xh, T.sem.xa, T.sem.tsent, hpid, hid, every)
+    def copy(i):
+        need("g", [txs[i]])
+        _send(g, topo, T.xin[:, XB[i]:XB[i + 1]], hc, every, T.sem.xa, T.sem.tsent)
+
+    r16, rkk, rcc, rp = counters()
+    ij = iota("jcol", [[1, 16]], 16)
+    copy(0)
     c2, c6 = new(), new()
-    ts(B("selv"), B("c16h"), B("vcol"), OP.is_equal, c2)
+    need("v", [r16])
+    ts(B("selv"), B("c16b"), B("vcol"), OP.is_equal, c2)
+    need("v", [rkk, rcc])
     blocks(c6)
-    ts(B("le"), B("cch", 0, 128), B("pf"), OP.is_le, c6, -1.0, OP.mult)
+    need("v", [rp])
+    ts(B("le"), B("ccb"), B("pf"), OP.is_le, c6, -1.0, OP.mult)
 
     need("v", [tk])
-    a1 = cp(B("kh", p=16), T.ki[0:16, :], new())
-    need("t", [c2, a1])
-    a2 = inc(P.matmul(T.b0[:, 0:128], B("selv", p=16), B("kh", p=16), True, True), new())
-    need("v", [c6])
-    c6b = tt(B("lb"), B("le"), B("bo"), OP.mult, new())
-    c3 = new()
-    for h, te in enumerate(("te0", "te1")):
-        ts(B(te, 0, 128), B("c16h"), B("kcol", h, h + 1), OP.is_ge, c3)
-        ts(B(te, 128, 256), B("c16h"), B("kcol", h, h + 1), OP.is_gt, c3)
-    need("v", [a2])
     a3, a4 = new(), new()
     for h in range(2):
-        ts(B("oh", h * 128, h * 128 + 128), T.b0[:, 0:128], B("kcol", h, h + 1), OP.is_equal, a3)
+        ts(B("oh", h * 128, h * 128 + 128), T.ki[:], B("kcol", h, h + 1), OP.is_equal, a3)
+    need("v", [c6])
+    c6b = tt(B("lb"), B("le"), B("bo"), OP.mult, new())
     need("v", [a3])
     for h in range(2):
         o = B("oh", h * 128, h * 128 + 128)
         inc(V.tensor_tensor_scan(B("fs", h * 128, h * 128 + 128), o, o, 0.0, OP.add, OP.max), a4)
+    c3 = new()
+    for h, te in enumerate(("te0", "te1")):
+        ts(B(te, 0, 128), B("c16b"), B("kcol", h, h + 1), OP.is_ge, c3)
+        ts(B(te, 128, 256), B("c16b"), B("kcol", h, h + 1), OP.is_gt, c3)
     cnt = [B("fs", 127, 128), B("fs", 255, 256)]
 
-    need("t", [a4, c6, c6b])
+    need("t", [a4, c6, c6b, c2])
     P.matmul(T.b1[:, 0:256], B("bo"), B("fs"), True, False)
     d1 = inc(P.matmul(T.b1[:, 0:256], B("lb"), B("oh"), False, True), new())
     P.matmul(T.b2[:, 0:1], B("gt"), cnt[0], True, True)
@@ -544,12 +680,9 @@ def rank_program(g, core, T, topo):
     need("t", [c3])
     P.matmul(T.b5[0:1, 0:256], cnt[0], B("te0"), True, False)
     a5 = inc(P.matmul(T.b5[0:1, 0:256], cnt[1], B("te1"), False, True), new())
-    c7 = new()
-    cp(B("c16b"), B("c16h"), c7)
-    ts(B("jcol"), B("ci", 0, 16), B("p16"), OP.add, c7)
     need("v", [d1])
     d3 = tt(B("mk"), T.b1[:, 0:256], B("oh"), OP.mult, new())
-    need("v", [d2])
+    need("v", [d2, c2])
     s16 = B("selv", 0, 16)
     for h in range(2):
         ts(B("sbase", h * 16, h * 16 + 16), s16, T.b2[:, h:h + 1], OP.mult, d3)
@@ -563,31 +696,19 @@ def rank_program(g, core, T, topo):
     need("y", [a6])
     a7 = inc(Y.dma_start(T.ed[r], T.erow[0:1, :]), new(), 16)
     need("g", [a7])
-    g.remote_dma_fused([
-        RemoteDMATransfer(srcs=[T.ed[r]], dsts=[T.ed[r] for _ in to], dst_ids=[_did(topo, c) for c in to],
-                          dma_engine_mask=m, remote_sem=T.sem.earr)
-        for to, m in ((farr, lo2[0]), (farh, lo2[1]), ([mate] + hp[ci], hi))], local_sem=T.sem.esent)
-    Y.wait_ge(T.sem.earr, 4 * (N - 2) + 8)
-    need("y", [a7])
-    e1 = inc(Y.dma_start(T.el[0:N, :], T.ed[:]), new(), 16)
+    g.remote_dma_fused([_tr(topo, T.ed[r], T.ed[r], fars, lo, T.sem.earr),
+                        _tr(topo, T.ed[r], T.ed[r], [ls[ci]], hi, T.sem.earr)], local_sem=T.sem.esent)
+    copy(1)
     need("v", [d4])
-    d5 = new()
-    ts(B("qf"), T.b3[:, 0:16], TW, OP.mult, d5, -HALF, OP.add)
-    ts(B("jf"), T.b3[:, 0:16], float(S1), OP.mult, d5)
+    d5 = ts(B("posi"), T.b3[:, 0:16], float(W + 1), OP.mult, new())
     need("v", [d5])
-    d5b = cp(B("qi"), B("qf"), new())
-    need("v", [d5b])
-    d5c = ts(B("pq"), B("qi"), -(12.0 * S1 - 1), OP.mult, new())
-    need("v", [d5c])
-    d5d = tt(B("posi"), B("pq"), B("jf"), OP.add, new())
-    need("v", [d5d])
     d6 = new()
-    ts(B("lh", 0, 16), B("posi"), 15, OP.bitwise_and, d6)
-    ts(B("lh", 16, 32), B("posi"), 4, OP.arith_shift_right, d6)
+    ts(B("lh", 0, 16), B("posi"), 4, OP.arith_shift_right, d6, 15, OP.bitwise_and)
+    ts(B("lh", 16, 32), B("posi"), 8, OP.arith_shift_right, d6, 127, OP.bitwise_and)
     need("v", [d6])
     d7 = cp(B("lhf"), B("lh"), new())
-    need("v", [d7, c7])
-    need("s", [d7, c7])
+    need("v", [d7, ij])
+    need("s", [d7, r16])
     n0 = 128 * (16 - VS)
     w1 = new()
     for v in range(VS, 16):
@@ -599,8 +720,8 @@ def rank_program(g, core, T, topo):
         d8 = new()
         for v in range(4 * b, 4 * b + 4):
             if v < VS:
-                ts(B("lq", v * 128, v * 128 + 128), B("c16h"), B("lhf", v, v + 1), OP.is_equal, d8)
-            ts(B("rq", v * 132, v * 132 + 132), B("cch"), B("lhf", 16 + v, 17 + v), OP.is_equal, d8,
+                ts(B("lq", v * 128, v * 128 + 128), B("c16b"), B("lhf", v, v + 1), OP.is_equal, d8)
+            ts(B("rq", v * 128, v * 128 + 128), B("ccb"), B("lhf", 16 + v, 17 + v), OP.is_equal, d8,
                B("jcol", v, v + 1), OP.mult)
         need("t", [d8])
         for v in range(4 * b, 4 * b + 4):
@@ -609,54 +730,52 @@ def rank_program(g, core, T, topo):
             else:
                 need("t", [w2])
                 lq = B("lqs", (v - VS) * 128, (v - VS) * 128 + 128)
-            m = P.matmul(T.b4[:, 0:132], lq, B("rq", v * 132, v * 132 + 132), v == 0, v == 15)
+            m = P.matmul(T.b4[:, 0:128], lq, B("rq", v * 128, v * 128 + 128), v == 0, v == 15)
     d9 = inc(m, new())
     need("v", [d9])
-    f1 = cp(T.gl[:], T.b4[:, 0:132], new())
+    f1 = cp(T.gl[:], T.b4[:, 0:128], new())
 
     need("g", [f1])
-    g.remote_dma(T.gl[:], T.gl[:], T.sem.la, T.sem.tsent, hpid, hid, every)
-    sent = 0
-    parts = []
-    for n, c in zip("vsvs", order[2:5] + [ci]):
-        parts.append(gather(n, [f1] + txs, T.p1[:, 2 * c * S1:(2 * c + 2) * S1], T.xin[:, 0:W],
-                            T.gl[:, 22 * c:22 * c + 22]))
-    for c, d in zip(order[2:5], parts):
-        sent += _deal(T, topo, need, g, c, r, [d], rk[c][0], hp[c][0], lo2)
-    sent += _deal(T, topo, need, g, ci, r, parts[3:], None if first else rk[ci][0], hp[ci][0], hi2)
+    _send(g, topo, T.gl[:], hc, every, T.sem.la, T.sem.tsent)
+    sent = _deal(g, T, topo, r, _legs(ci)[0], main, tools, [f1] + txs, lo2)
+    u = 2 * ci
+    part = gather("s", [], T.p1[:, u * S1:(u + 2) * S1], T.xin[:, 0:W], T.gl[:, 8 * u:8 * u + 16])
+    if first:
+        mine = gather("v", [], T.xl[:, r * S1:(r + 1) * S1], T.xin[:, 0:W], T.gl[:, 8 * u:8 * u + 8])
+    need("g", [part])
+    tr = [_tr(topo, T.p1[:, (u + x) * S1:(u + x + 1) * S1], T.xl[:, r * S1:(r + 1) * S1], [main[ci][x]], hi2[x],
+              T.sem.a1) for x in range(2) if main[ci][x] != core]
+    g.remote_dma_fused(tr, local_sem=T.sem.sent)
+    sent += 4 * len(tr)
 
     if first:
-        mine = gather("v", [f1] + txs, T.xl[:, r * S1:(r + 1) * S1], T.xin[:, 0:W], T.gl[:, 22 * ci:22 * ci + 11])
-        for q in (V, P):
-            q.wait_ge(T.sem.tabh, 8)
-        _counts(g, T, tools, [e1, a6])
-        il = _xlist(g, T, tools)
         for q in (V, S):
+            q.wait_ge(T.sem.ila, 16)
             q.wait_ge(T.sem.a1, 4 * (N - 1))
-        s2, home = _meet(g, T, topo, core, 2 * ci, ci, rk, mate, order, need, gather, [mine, il], lo2, hi2)
+        s2, home = _meet(g, T, topo, core, u, ci, rk, mate, fwd, own, tools, [mine], lo2, hi2)
         sent += s2
         deps = [home]
         for q in (V, S):
             q.wait_ge(T.sem.ola, 8)
     else:
-        tab = new()
-        sums(tab)
         for q in (V, P):
-            q.wait_ge(T.sem.tabh, 8)
-        _counts(g, T, tools, [e1, a6, tab])
-        deps = [_rlist(g, T, tools, r)]
-        sent += _neighbour(g, T, topo, 2 * ci, rk, order, lo2)
+            q.wait_ge(T.sem.tabh, 32)
+        P.wait_ge(T.sem.elr, 16)
+        _counts(g, T, tools, [a6])
+        deps = [_rlist(g, T, tools, r, u + 1)]
+        sent += _neighbour(g, T, topo, u, rk, fwd, lo2)
 
-    total = 4 * (N - 1) if first else 4 * N
+    total = 4 * (NU - 1) if first else 4 * NU
     V.wait_ge(T.sem.arr, total)
     S.wait_ge(T.sem.arr, total)
     ty = new()
-    for n, a, b in (("v", 0, 640), ("s", 640, 1280), ("v", 1280, 1664), ("s", 1664, W)):
-        t = gather(n, deps, T.yb[:, a:b], T.land[:, 0:N * S2], T.ol[:, a // 16:b // 16])
+    for n, a, b in (("v", 0, 384), ("s", 384, 768), ("v", 768, 1280), ("s", 1280, 1664), ("v", 1664, 1856),
+                    ("s", 1856, W)):
+        t = gather(n, deps, T.yb[:, a:b], T.land[:, 0:NU * S2], T.ol[:, a // 16:b // 16])
         need("y", [t])
         inc(Y.dma_start(T.y[:, a:b], T.yb[:, a:b]), ty, 16)
     need("y", [ty])
-    g.wait_ge(T.sem.tsent, 16 * XP + 16)
+    g.wait_ge(T.sem.tsent, 16 * len(XB))
     g.wait_ge(T.sem.esent, 16)
     g.wait_ge(T.sem.sent, sent)
     close()

from concourse.bass import DstId, RemoteDMATransfer
from concourse.mybir import AluOpType as OP, AxisListType, ActivationFunctionType as AF

N, W, SIM = 12, 2048, 112
NU = 16
S1, S2, G2 = 128, 152, 160
VS = 11
XB = (0, 512, W)
F32, F16, BF, I32, U16 = "float32", "float16", "bfloat16", "int32", "uint16"
SCRATCH = {
    "xin": ("sbuf", [128, W], F32), "p1": ("sbuf", [128, W], F32), "xl": ("sbuf", [128, N * S1], F32),
    "p2": ("sbuf", [128, N * G2], F32), "sb": ("sbuf", [128, 4 * S2], F32),
    "land": ("sbuf", [128, NU * S2 + G2 - S2], F32), "yb": ("sbuf", [128, W], F32),
    "ki": ("sbuf", [128, 128], I32), "erow": ("sbuf", [128, 256], F16), "el": ("sbuf", [128, 256], F16),
    "gl": ("sbuf", [128, 128], U16), "il": ("sbuf", [128, 120], U16), "ol": ("sbuf", [128, 128], U16),
    "xt": ("sbuf", [128, 816], F16), "th": ("sbuf", [128, 456], F32),
    "ed": ("dram", [N, 128, 2], F16),
}
for _i in range(8):
    SCRATCH["b%d" % _i] = ("psum", [128, 512], F32)
_TILES = {
    F16: (("oh", 256), ("fs", 256), ("mk", 256), ("sbase", 32), ("lq", 2048), ("rq", 2048),
          ("selv", 128), ("bo", 128), ("gt", 128), ("le", 128), ("lb", 128), ("te0", 256), ("te1", 256), ("onh", 128),
          ("zd", 4), ("n16", 2), ("z2", 288), ("xg", 72), ("xy", 72), ("xz", 72), ("xn", 72), ("xm", 60), ("xc", 60),
          ("xe", 60), ("an", 2), ("nn", 2), ("xr", 240), ("xlg", 512)),
    BF: (("c16b", 128), ("kcb", 128), ("ccb", 128), ("lab", 640), ("lqs", 640)),
    F32: (("lhf", 32), ("pf", 1), ("omp", 2), ("vcol", 1), ("kcol", 2), ("jcol", 16), ("pa", 36), ("pb", 36),
          ("cols", 6), ("u", 2), ("u2", 2), ("zm", 4), ("lr", 4), ("lxf", 8), ("t1", 2), ("t2", 2), ("dl", 2),
          ("rb", 2), ("ra", 2), ("ov", 2), ("rg", 1024), ("lg", 512), ("v2", 128), ("v3", 128), ("z1", 288),
          ("df", 1), ("dcol", 1), ("sm", 1), ("ohl", 2), ("xd", 2)),
    I32: (("posi", 16), ("lh", 32), ("pi", 1), ("pk", 2), ("li", 4), ("lx", 8), ("ri", 4), ("rj", 4), ("vi", 128),
          ("vk", 128), ("vr", 128), ("vs", 128), ("wd", 24), ("cc", 60), ("cb", 60), ("cd", 60), ("ce", 72), ("di", 1),
          ("qx", 4), ("qy", 4), ("oi", 2), ("oh2", 2)),
}
_AT = {}
for _dt, _ts in _TILES.items():
    _o = 0
    for _n, _w in _ts:
        _AT[_n] = ("m_" + _dt, _o, _w, _dt)
        _o += (_w + 31) // 32 * 32
    SCRATCH["m_" + _dt] = ("sbuf", [128, _o], _dt)
XA, XC, XE = 200, 568, 816
_XT = {"xu": (200, 72), "xb": (272, 72), "xs": (344, 72), "cm": (416, 60), "cn": (476, 60), "wd": (536, 24),
       "s1": (560, 8), "l2": (568, 128), "r2": (696, 120)}
NSEM = 100
SEMAPHORES = (["earr", "elr", "arr", "a1", "sent", "esent", "tabh", "tsent", "xa", "la", "ila", "ola", "f0", "f1"]
              + ["s%d" % i for i in range(NSEM)])


def _places(T, topo):
    chips = sorted(set(topo.chip(c) for c in T.cores))
    rk = [sorted(c for c in T.cores if topo.chip(c) == h) for h in chips]
    hp, ls, ex = [], [], []

    def able(h, d):
        far = [t for t in T.cores if topo.chip(t) != h]
        return [c for c in range(SIM) if topo.chip(c) == h and topo.die(c) == d and T.rank_of(c) is None
                and all(topo.may_write(c, t) for t in far)][0:2]
    for i, h in enumerate(chips):
        d = topo.die(rk[i][0])
        hp.append(able(h, 1 - d))
        ls.append([c for c in range(SIM) if topo.chip(c) == h and c not in rk[i] + hp[i]][0])
    d = topo.die(rk[0][0])
    nchips = topo.chip(SIM - 1) + 1
    for h in chips:
        for m in range(nchips):
            if topo.mates(h, m) and m not in chips and len(ex) < 2:
                ex.append([able(m, d), able(m, 1 - d)])
    return chips, rk, hp, ls, ex


def _masks(topo, core, near, far):
    lo = topo.mask(core, far)
    hi = topo.mask(core, near) & ~lo
    out = []
    for m in (lo, hi):
        bits = [1 << i for i in range(m.bit_length()) if m >> i & 1]
        out.append((sum(bits[:len(bits) // 2]), sum(bits[len(bits) // 2:])))
    return lo, hi, out[0], out[1]


def _did(topo, c):
    rid, pid, _e = topo.addr(c)
    return DstId(rid=rid, pnc=pid)


def _tr(topo, src, dst, to, mask, sem):
    return RemoteDMATransfer(srcs=[src], dsts=[dst for _ in to], dst_ids=[_did(topo, c) for c in to],
                             dma_engine_mask=mask, remote_sem=sem)


def _tools(g, T):
    q = {"v": g.vector, "s": g.scalar, "t": g.tensor, "g": g, "y": g.sync}
    seen = dict((n, {}) for n in q)
    toks = []

    def B(name, a=0, b=None, p=128):
        buf, o, w, _ = _AT[name]
        return T[buf][0:p, o + a:o + (w if b is None else b)]

    def new():
        t = {"s": "s%d" % len(toks), "n": 0, "w": False}
        toks.append(t)
        return t

    def need(n, deps):
        for t in deps:
            if seen[n].get(t["s"], 0) < t["n"]:
                q[n].wait_ge(T.sem[t["s"]], t["n"])
                seen[n][t["s"]] = t["n"]
                t["w"] = True

    def inc(inst, t, k=1):
        inst.then_inc(T.sem[t["s"]], k)
        t["n"] += k
        return t

    def ts(out, in0, s1, op0, t, s2=None, op1=None):
        if op1 is None:
            return inc(g.vector.tensor_scalar(out, in0, s1, None, op0), t)
        return inc(g.vector.tensor_scalar(out, in0, s1, s2, op0, op1), t)

    def cp(out, in_, t):
        return inc(g.vector.tensor_copy(out, in_), t)

    def tt(out, a, b, op, t):
        return inc(g.vector.tensor_tensor(out, a, b, op), t)

    def iota(name, pattern, mult):
        return inc(g.iota(B(name), pattern, 0, mult, allow_small_or_imprecise_dtypes=True), new())

    def counters():
        i1 = inc(g.iota(B("pi"), [[0, 1]], 0, 1), new())
        rows = [iota("c16b", [[0, 8], [1, 16]], 0), iota("kcb", [[1, 8], [0, 16]], 0), iota("ccb", [[1, 128]], 0),
                iota("pf", [[0, 1]], 1)]
        c1 = new()
        need("v", [i1])
        ts(B("pk", 0, 1), B("pi"), 4, OP.arith_shift_right, c1)
        ts(B("pk", 1, 2), B("pi"), 15, OP.bitwise_and, c1)
        need("v", [c1])
        c2 = new()
        ts(B("kcol", 0, 1), B("pk", 0, 1), 0, OP.add, c2)
        ts(B("kcol", 1, 2), B("pk", 0, 1), 8, OP.add, c2)
        cp(B("vcol"), B("pk", 1, 2), c2)
        need("v", [c2])
        return rows

    def ones(t):
        return ts(B("onh"), B("ccb"), 0.0, OP.is_ge, t)

    def blocks(t):
        ts(B("bo"), B("kcb"), B("kcol", 0, 1), OP.is_equal, t)
        ts(B("gt"), B("kcb"), B("kcol", 0, 1), OP.is_gt, t)
        ones(t)

    def sums(t):
        c12 = B("ccb", 0, N)
        for a, op, mul in ((0, OP.is_gt, 1.0), (12, OP.is_equal, 0.0), (24, OP.is_equal, 1.0),
                           (36, OP.is_le, 1.0), (48, OP.is_equal, 1.0), (60, OP.is_equal, -1.0)):
            ts(T.xt[:, a:a + N], c12, B("pf"), op, t, mul, OP.mult)
        return ts(T.xt[:, 72:XA], B("ccb"), 0.0, OP.is_ge, t, 0.125, OP.mult)

    def gather(n, deps, out, win, off):
        need(n, deps)
        src = win.indirect(off)
        if n == "v":
            return inc(g.vector.tensor_copy(out, src), new())
        return inc(g.scalar.activation(out, src, AF.Copy), new())

    def close():
        for t in toks:
            if not t["w"]:
                need("g", [t])
    return B, new, need, inc, ts, cp, tt, counters, blocks, sums, gather, close, ones, iota


def _counts(g, T, tools, deps):
    B, new, need, inc = tools[0:4]
    need("t", deps)
    g.tensor.matmul(T.b5[:, 0:36], T.el[0:N, 0:128], T.xt[0:N, 0:36], True, False)
    h1 = inc(g.tensor.matmul(T.b5[:, 0:36], T.el[0:N, 128:256], T.xt[0:N, 36:72], False, True), new())
    need("v", [h1])


def _X(T, n, p=128):
    return T.xt[0:p, _XT[n][0]:_XT[n][0] + _XT[n][1]]


def _xtables(g, T, tools):
    B, new, need, inc, ts, cp, tt = tools[0:7]
    i4 = new()
    inc(g.iota(B("cc"), [[0, 6], [1, 10]], 0, 0), i4)
    inc(g.iota(B("cd"), [[1, 6], [0, 10]], 0, 0), i4)
    inc(g.iota(B("ce"), [[1, 6], [0, 12]], 0, 0), i4)
    for h in range(2):
        inc(g.iota(B("wd", 12 * h, 12 * h + 12), [[W, 6], [6 * W, 2]], W * h, 0), i4)
    need("v", [i4])
    c8 = new()
    cp(_X(T, "wd"), B("wd"), c8)
    ts(B("df"), B("pf"), 1.0 / 12, OP.mult, c8, -11.0 / 24, OP.add)
    ts(B("xc"), B("cc"), 16.0, OP.mult, c8, 64.0, OP.add)
    need("v", [c8])
    c9 = cp(B("di"), B("df"), new())
    need("v", [c9])
    c10 = cp(B("dcol"), B("di"), new())
    need("v", [c10])
    c11 = new()
    ts(B("sm"), B("dcol"), -12.0, OP.mult, c11, B("pf"), OP.add)
    ts(B("xm"), B("cd"), B("dcol"), OP.is_equal, c11)
    ts(B("xn"), B("ce"), B("dcol"), OP.is_equal, c11)
    ts(B("xg"), B("ccb", 0, 72), B("pf"), OP.is_gt, c11)
    ts(B("xy"), B("ccb", 0, 72), B("pf"), OP.subtract, c11, 1.0, OP.is_equal)
    ts(_X(T, "xb"), B("ccb", 0, 72), B("pf"), OP.is_equal, c11)
    need("v", [c11])
    c12 = new()
    tt(_X(T, "xu"), B("xg"), B("xn"), OP.mult, c12)
    tt(B("xz"), B("xy"), B("xn"), OP.mult, c12)
    tt(B("xe"), B("xc"), B("xm"), OP.mult, c12)
    need("v", [c12])
    c13 = new()
    tt(_X(T, "xb"), _X(T, "xb"), B("xz"), OP.subtract, c13)
    ts(_X(T, "xs"), B("xz"), -1.0, OP.mult, c13)
    ts(_X(T, "cm"), B("xe"), -64.0, OP.add, c13)
    ts(_X(T, "cn"), B("xe"), -48.0, OP.add, c13)
    ts(_X(T, "s1"), B("ccb", 0, 8), 0.0, OP.is_ge, c13, B("sm"), OP.mult)
    need("v", [c13])
    return ts(_X(T, "s1"), _X(T, "s1"), 0.0, OP.is_gt, new(), float(S1), OP.mult)


def _base(g, T, tools):
    B, new, need, inc, ts, cp, tt = tools[0:7]
    i5 = inc(g.iota(B("cb"), [[0, 6], [1, 10]], 0, 0), new())
    c14 = ts(B("omp", 0, 1), B("pf"), -1.0, OP.mult, new(), 1.0, OP.add)
    ts(B("omp", 1, 2), B("pf"), -16.0, OP.mult, c14, 16.0, OP.add)
    need("v", [c14, i5])
    c15 = ts(_X(T, "l2"), B("c16b"), B("pf"), OP.mult, new(), B("omp", 0, 1), OP.add)
    o = _XT["r2"][0]
    for h in range(2):
        ts(T.xt[:, o + 60 * h:o + 60 * h + 60], B("cb"), B("omp", 1, 2), OP.mult, c15, B("pf"), OP.add)
    return c15


def _xlist(g, T, tools):
    B, new, need, inc, ts, cp, tt = tools[0:7]
    P = g.tensor
    zb, zo, _w, _d = _AT["z1"]
    h2 = new()
    for s in range(N):
        ts(T[zb][0:128, zo + s:zo + 288:12], _X(T, "wd"), T.b5[:, s:s + 1], OP.subtract, h2,
           T.b5[:, 24 + s:25 + s], OP.min)
    need("v", [h2])
    h3 = ts(B("z2"), B("z1"), 0.0, OP.max, new())
    need("t", [h3])
    for h in range(4):
        m = P.matmul(T.b6[0:72, h:h + 1], B("z2", 72 * h, 72 * h + 72), T.xt[:, 72:73], True, True)
    h4 = inc(m, new())
    need("v", [h4])
    h5 = new()
    ts(B("qx", 0, 2, 72), T.b6[0:72, 0:2], 0.0, OP.add, h5)
    ts(B("qx", 2, 4, 72), T.b6[0:72, 2:4], 15.0, OP.add, h5)
    need("v", [h5])
    h6 = ts(B("qy", p=72), B("qx", p=72), 4, OP.arith_shift_right, new())
    need("v", [h6])
    h7 = new()
    cp(B("an", p=72), B("qy", 0, 2, 72), h7)
    tt(B("nn", p=72), B("qy", 2, 4, 72), B("qy", 0, 2, 72), OP.subtract, h7)
    need("t", [h7])
    P.matmul(T.b0[0:72, 0:2], _X(T, "xu", 72), B("nn", p=72), True, True)
    P.matmul(T.b0[0:72, 2:4], _X(T, "xb", 72), B("an", p=72), True, False)
    h8 = inc(P.matmul(T.b0[0:72, 2:4], _X(T, "xs", 72), B("nn", p=72), False, True), new())
    need("v", [h8])
    h9 = cp(B("oi", p=72), T.b0[0:72, 0:2], new())
    h9b = tt(B("xd", p=72), T.b0[0:72, 2:4], T.xt[0:72, _XT["s1"][0]:_XT["s1"][0] + 2], OP.add, new())
    need("v", [h9])
    h10 = ts(B("oh2", p=72), B("oi", p=72), 15, OP.bitwise_and, new())
    need("v", [h9b])
    h12 = new()
    for h in range(2):
        for o, n in ((0, "cm"), (60, "cn")):
            ts(B("xr", 120 * h + o, 120 * h + o + 60, 72), _X(T, n, 72), T.b0[0:72, h:h + 1], OP.is_gt, h12,
               B("xd", h, h + 1, 72), OP.mult)
    need("v", [h10])
    h11 = cp(B("ohl", p=72), B("oh2", p=72), new())
    need("v", [h11])
    for h in range(2):
        for o, op in ((0, OP.is_lt), (128, OP.is_ge)):
            ts(B("xlg", 256 * h + o, 256 * h + o + 128, 72), B("c16b", p=72), B("ohl", h, h + 1, 72), op, h12)
    o = _XT["r2"][0]
    need("t", [h12])
    for h in range(2):
        out = T.b1[:, 60 * h:60 * h + 60]
        P.matmul(out, _X(T, "l2", 2), T.xt[0:2, o + 60 * h:o + 60 * h + 60], True, False)
        P.matmul(out, B("xlg", 256 * h, 256 * h + 128, 72), B("xr", 120 * h, 120 * h + 60, 72), False, False)
        m = P.matmul(out, B("xlg", 256 * h + 128, 256 * h + 256, 72), B("xr", 120 * h + 60, 120 * h + 120, 72),
                     False, True)
    h14 = inc(m, new())
    need("v", [h14])
    return ts(T.il[:], T.b1[:, 0:120], 0.0, OP.max, new(), float(N * S1 - 1), OP.min)


def _rlist(g, T, tools, r, first):
    B, new, need, inc, ts, cp, tt = tools[0:7]
    V, P = g.vector, g.tensor
    k2 = new()
    tt(B("pa"), T.b5[:, 0:36], T.th[:, 0:36], OP.mult, k2)
    tt(B("pb"), T.b5[:, 0:36], T.th[:, 36:72], OP.mult, k2)
    need("v", [k2])
    k3 = new()
    for j in range(3):
        for x, p in enumerate(("pa", "pb")):
            inc(V.tensor_reduce(B("cols", 2 * j + x, 2 * j + x + 1), B(p, 12 * j, 12 * j + 12), AxisListType.X, OP.add),
                k3)
    need("v", [k3])
    k4 = new()
    ts(B("u"), B("cols", 0, 2), -1.0, OP.mult, k4, float(W * r), OP.add)
    ts(B("u2"), B("cols", 0, 2), -1.0, OP.mult, k4, float(W * r + W), OP.add)
    need("v", [k4])
    k5 = new()
    tt(B("zm", 0, 2), B("u"), B("cols", 4, 6), OP.min, k5)
    tt(B("zm", 2, 4), B("u2"), B("cols", 4, 6), OP.min, k5)
    ts(B("lr", 0, 2), B("u"), -1.0, OP.mult, k5)
    tt(B("lr", 2, 4), B("cols", 4, 6), B("u"), OP.subtract, k5)
    tt(B("t1"), B("u"), B("cols", 2, 4), OP.add, k5)
    need("v", [k5])
    k6 = ts(B("zd"), B("zm"), 0.0, OP.max, new())
    need("t", [k6])
    k7 = inc(P.matmul(T.b7[:, 0:4], B("bo"), B("zd"), True, True), new())
    k8 = ts(B("li"), B("lr"), 0.0, OP.max, new(), float(W), OP.min)
    need("v", [k8])
    k9 = new()
    ts(B("lx", 0, 4), B("li"), 4, OP.arith_shift_right, k9)
    ts(B("lx", 4, 8), B("li"), 15, OP.bitwise_and, k9)
    need("v", [k9])
    k10 = cp(B("lxf"), B("lx"), new())
    need("v", [k7])
    ts(B("ri", 0, 2), T.b7[:, 0:2], 0.0, OP.add, k10)
    ts(B("ri", 2, 4), T.b7[:, 2:4], 15.0, OP.add, k10)
    need("v", [k10])
    k10b = ts(B("rj"), B("ri"), 4, OP.arith_shift_right, new())
    need("v", [k10b])
    k10c = new()
    tt(B("rb"), B("rj", 2, 4), B("rj", 0, 2), OP.subtract, k10c)
    ts(B("ra"), B("rj", 0, 2), -16.0, OP.mult, k10c)
    need("v", [k10c])
    k10d = ts(B("n16"), B("rb"), 0.0625, OP.mult, new())
    tt(B("t2"), B("t1"), B("ra"), OP.add, k10d)
    need("t", [k10d])
    P.matmul(T.b7[:, 8:9], B("gt"), B("n16", 0, 1), True, True)
    P.matmul(T.b7[:, 9:10], B("onh"), B("n16", 0, 1), True, False)
    k10e = inc(P.matmul(T.b7[:, 9:10], B("gt"), B("n16", 1, 2), False, True), new())
    need("v", [k10e, k10d])
    k10f = ts(B("ov"), T.b7[:, 8:10], 16.0, OP.mult, new())
    need("v", [k10f])
    k10g = tt(B("dl"), B("t2"), B("ov"), OP.add, new())
    need("v", [k10g])
    k11 = new()
    for x in range(2):
        dl = B("dl", x, x + 1)
        for e in range(2):
            o = x * 512 + e * 256
            hs, ls = 2 * e + x, 4 + 2 * e + x
            ts(B("rg", o, o + 128), B("ccb"), B("lxf", hs, hs + 1), OP.is_gt, k11, dl, OP.mult)
            ts(B("rg", o + 128, o + 256), B("ccb"), B("lxf", hs, hs + 1), OP.is_equal, k11, dl, OP.mult)
            o = x * 256 + e * 128
            ts(B("lg", o, o + 128), B("c16b"), B("lxf", ls, ls + 1), OP.is_ge, k11, 1.0 - 2.0 * e, OP.mult)
    need("t", [k11])
    for x in range(2):
        for e in range(2):
            o = x * 512 + e * 256
            P.matmul(T.b7[:, 128:256], T.th[:, 72 + 128 * e:200 + 128 * e], B("rg", o, o + 128), x + e == 0, False)
            m = P.matmul(T.b7[:, 128:256], B("lg", x * 256 + e * 128, x * 256 + e * 128 + 128),
                         B("rg", o + 128, o + 256), False, x + e == 2)
    k12 = inc(m, new())
    need("v", [k12])
    k13 = tt(B("vi"), T.b7[:, 128:256], T.th[:, 328:456], OP.add, new())
    need("v", [k13])
    k14 = ts(B("vk"), B("vi"), float(NU - first), OP.add, new())
    ts(B("vr"), B("vi"), 4, OP.arith_shift_right, k14)
    need("v", [k14])
    k15 = ts(B("vs"), B("vk"), 15, OP.bitwise_and, new())
    need("v", [k15])
    k16 = ts(B("v2"), B("vs"), float(S2), OP.mult, new())
    need("v", [k16])
    k17 = tt(B("v3"), B("v2"), B("vr"), OP.add, new())
    need("v", [k17])
    return cp(T.ol[:], B("v3"), new())


def _legs(ci):
    o = [(ci + 1 + i) % 6 for i in range(5)]
    far = o[0:2] + [6 + ci % 2] + o[2:4] + [7 - ci % 2] + o[4:]
    a = [(far[i], 0) for i in range(6)] + [(far[6], 0), (far[6], 1)]
    b = [(far[(2 + i) % 6], 1) for i in range(6)]
    return [a[i:i + 2] for i in range(0, 8, 2)], [b[i:i + 2] for i in range(0, 6, 2)]


def _deal(g, T, topo, r, legs, main, tools, deps, lo2):
    need, gather = tools[2], tools[10]
    parts = []
    for pair in legs:
        for n, (e, x) in zip("vs", pair):
            u = 2 * e + x
            parts.append(gather(n, deps, T.p1[:, u * S1:(u + 1) * S1], T.xin[:, 0:W], T.gl[:, 8 * u:8 * u + 8]))
    for i, pair in enumerate(legs):
        need("g", parts[2 * i:2 * i + 2])
        tr = []
        for (e, x), m in zip(pair, lo2):
            u = 2 * e + x
            tr.append(_tr(topo, T.p1[:, u * S1:(u + 1) * S1], T.xl[:, r * S1:(r + 1) * S1], [main[e][x]], m, T.sem.a1))
        g.remote_dma_fused(tr, local_sem=T.sem.sent)
    return 8 * len(legs)


def _slot(T, u, ci):
    s = (u - 2 * ci - 1) % NU * S2
    return T.land[:, s:s + S2]


def _meet(g, T, topo, core, u, ci, rk, sib, fwd, own, tools, deps, lo2, hi2):
    need, gather = tools[2], tools[10]

    def pack(n, c, k):
        e = 2 * c + k
        if rk[c][k] == core:
            out = T.land[:, (NU - 1) * S2:(NU - 1) * S2 + G2]
        else:
            out = T.p2[:, e * G2:(e + 1) * G2]
        return gather(n, deps, out, T.xl[:, 0:N * S1], T.il[:, 10 * e:10 * e + 10])
    sent, home = 0, None
    also = fwd + [ci] * (ci is not None) + [None] * len(own)
    for i, c in enumerate(own):
        o = also[i]
        done = [pack("v", c, 0), pack("v" if o is not None else "s", c, 1)]
        near = [] if o is None else [pack("s", o, 0), pack("s", o, 1)]
        tr = []
        for k in range(2):
            e = 2 * c + k
            tr.append(_tr(topo, T.p2[:, e * G2:e * G2 + S2], _slot(T, u, c), [rk[c][k]], lo2[k], T.sem.arr))
            if o is None:
                continue
            e = 2 * o + k
            src = T.p2[:, e * G2:e * G2 + S2]
            if i < len(fwd):
                tr.append(_tr(topo, src, T.sb[:, (2 * i + k) * S2:(2 * i + k + 1) * S2], [sib], hi2[k],
                              T.sem["f%d" % i]))
            elif rk[o][k] != core:
                tr.append(_tr(topo, src, _slot(T, u, o), [rk[o][k]], hi2[k], T.sem.arr))
            else:
                home = near[k]
        need("g", done + near)
        g.remote_dma_fused(tr, local_sem=T.sem.sent)
        sent += 4 * len(tr)
    return sent, home


def _neighbour(g, T, topo, u, rk, fwd, lo2):
    for i, c in enumerate(fwd):
        g.wait_ge(T.sem["f%d" % i], 8)
        g.remote_dma_fused([_tr(topo, T.sb[:, (2 * i + k) * S2:(2 * i + k + 1) * S2], _slot(T, u, c), [rk[c][k]],
                                lo2[k], T.sem.arr) for k in range(2)], local_sem=T.sem.sent)
    return 8 * len(fwd)


def _send(g, topo, buf, to, mask, sem, lsem):
    rid, pid, _e = topo.addr(to)
    g.remote_dma(buf, buf, sem, lsem, pid, rid, mask)


def _far(ci):
    o = [(ci + 1 + i) % 6 for i in range(5)]
    return o[0:1], o[1:5]


def _allcounts(g, T, topo, tools, z, to, every):
    new, need, inc = tools[1:4]
    need("y", [z])
    g.sync.wait_ge(T.sem.earr, 8 * N)
    e1 = inc(g.sync.dma_start(T.el[0:N, :], T.ed[:]), new(), 16)
    need("g", [z, e1])
    g.remote_dma_fused([_tr(topo, T.el[:], T.el[:], to, every, T.sem.elr)], local_sem=T.sem.tsent)
    return e1


def _zero(T, tools):
    B, new, ts = tools[0], tools[1], tools[4]
    z = new()
    for h in range(2):
        ts(T.el[:, 128 * h:128 * h + 128], B("ccb"), 0.0, OP.mult, z)
    return z


def _help(g, core, T, topo, chips, rk, hp, ls, main):
    ci = chips.index(topo.chip(core))
    k = hp[ci].index(core)
    owner = rk[ci][k]
    r = T.rank_of(owner)
    fwd, own = _far(ci)
    lo, hi, lo2, hi2 = _masks(topo, core, owner, rk[own[0]][0])
    every = topo.mask(core, owner)
    tools = _tools(g, T)
    B, new, need, inc, ts, cp, tt, counters, blocks, sums, gather, close, ones, iota = tools
    need("v", counters())
    if k == 0:
        tab = [_xtables(g, T, tools), _base(g, T, tools)]
        need("g", tab)
        _send(g, topo, T.xt[:, XA:XE], ls[ci], every, T.sem.tabh, T.sem.tsent)
    else:
        t = new()
        for j in range(3):
            for x in range(2):
                ts(T.th[:, 36 * x + 12 * j:36 * x + 12 * j + 12], B("ccb", 0, N), B("kcol", x, x + 1), OP.is_equal, t)
        inc(g.vector.memset(T.th[:, 72:200], 1.0), t)
        inc(g.vector.memset(T.th[:, 200:328], -1.0), t)
        ts(T.th[:, 328:456], B("ccb"), 16.0, OP.mult, t, B("vcol"), OP.add)
        need("g", [t])
        _send(g, topo, T.th[:], owner, every, T.sem.tabh, T.sem.tsent)
        blocks(t)
        sums(t)
        need("v", [t])
    for q in (g.vector, g.scalar):
        q.wait_ge(T.sem.xa, 16 * (len(XB) - 1))
        q.wait_ge(T.sem.la, 16)
    sent = _deal(g, T, topo, r, _legs(ci)[1], main, tools, [], lo2)
    if k == 0:
        for q in (g.vector, g.scalar):
            q.wait_ge(T.sem.ila, 16)
            q.wait_ge(T.sem.a1, 4 * N)
        sent += _meet(g, T, topo, core, 2 * ci + 1, ci, rk, hp[ci][1], fwd, own, tools, [], lo2, hi2)[0]
        g.wait_ge(T.sem.tsent, 16)
    else:
        g.tensor.wait_ge(T.sem.elr, 16)
        _counts(g, T, tools, [t])
        ol = _rlist(g, T, tools, T.rank_of(rk[ci][0]), 2 * ci + 1)
        need("g", [ol])
        _send(g, topo, T.ol[:], rk[ci][0], hi, T.sem.ola, T.sem.tsent)
        sent += _neighbour(g, T, topo, 2 * ci + 1, rk, fwd, lo2)
        g.wait_ge(T.sem.tsent, 24)
    g.wait_ge(T.sem.sent, sent)
    close()


def _list(g, core, T, topo, ci, rk, hp):
    every = topo.mask(core, rk[ci][1])
    tools = _tools(g, T)
    B, new, need, inc, ts, cp, tt, counters, blocks, sums, gather, close, ones, iota = tools
    need("v", counters())
    tab = new()
    sums(tab)
    need("g", [tab])
    _send(g, topo, T.xt[:, 0:72], rk[ci][1], every, T.sem.tabh, T.sem.tsent)
    z = _zero(T, tools)
    need("v", [tab])
    for q in (g.vector, g.tensor):
        q.wait_ge(T.sem.tabh, 16)
    e1 = _allcounts(g, T, topo, tools, z, [rk[ci][1], hp[ci][1]], every)
    _counts(g, T, tools, [tab, e1])
    il = _xlist(g, T, tools)
    need("g", [il])
    g.remote_dma_fused([_tr(topo, T.il[:], T.il[:], [rk[ci][0], hp[ci][0]], every, T.sem.ila)], local_sem=T.sem.tsent)
    g.wait_ge(T.sem.tsent, 48)
    close()


def _extra(g, core, T, topo, q, x, k, rk, ex):
    u = 12 + 2 * q + x
    o = [(3 * q + i) % 6 for i in range(6)]
    fwd, own = o[0:2], o[2:6]
    sib, other = ex[q][x][1 - k], ex[q][1 - x][0]
    lo, hi, lo2, hi2 = _masks(topo, core, sib, rk[0][0])
    every = topo.mask(core, sib)
    tools = _tools(g, T)
    B, new, need, inc, ts, cp, tt, counters, blocks, sums, gather, close, ones, iota = tools
    need("v", counters())
    tables = 16
    if k == 1:
        tab = _xtables(g, T, tools)
        need("g", [tab])
        _send(g, topo, T.xt[:, XA:XC], sib, every, T.sem.tabh, T.sem.tsent)
        sent = _neighbour(g, T, topo, u, rk, fwd, lo2)
    else:
        if x == 0:
            t = new()
            sums(t)
            part = T.xt[:, 0:XA]
        else:
            t = _base(g, T, tools)
            part = T.xt[:, XC:XE]
        need("g", [t])
        _send(g, topo, part, other, every, T.sem.tabh, T.sem.tsent)
        need("v", [t])
        for n in (g.vector, g.tensor):
            n.wait_ge(T.sem.tabh, 32)
        if x == 0:
            deps = [t, _allcounts(g, T, topo, tools, _zero(T, tools), [other], every)]
            tables = 32
        else:
            g.tensor.wait_ge(T.sem.elr, 16)
            deps = [t]
        _counts(g, T, tools, deps)
        il = _xlist(g, T, tools)
        for n in (g.vector, g.scalar):
            n.wait_ge(T.sem.a1, 4 * N)
        sent = _meet(g, T, topo, core, u, None, rk, sib, fwd, own, tools, [il], lo2, hi2)[0]
    g.wait_ge(T.sem.tsent, tables)
    g.wait_ge(T.sem.sent, sent)
    close()


def rank_program(g, core, T, topo):
    chips, rk, hp, ls, ex = _places(T, topo)
    main = [[rk[i][0], hp[i][0]] for i in range(6)] + [[e[0][0], e[1][0]] for e in ex]
    r = T.rank_of(core)
    if r is None:
        if any(core in h for h in hp):
            _help(g, core, T, topo, chips, rk, hp, ls, main)
        elif core in ls:
            _list(g, core, T, topo, ls.index(core), rk, hp)
        for q in range(2):
            for x in range(2):
                if core in ex[q][x]:
                    _extra(g, core, T, topo, q, x, ex[q][x].index(core), rk, ex)
        return
    ci = chips.index(topo.chip(core))
    kk = rk[ci].index(core)
    mate, hc = rk[ci][1 - kk], hp[ci][kk]
    fwd, own = _far(ci)
    fars = [ls[i] for i in fwd + own] + [e[0][0] for e in ex]
    lo, hi, lo2, hi2 = _masks(topo, core, mate, rk[own[0]][0])
    every = topo.mask(core, mate)
    first = kk == 0

    V, S, P, Y = g.vector, g.scalar, g.tensor, g.sync
    tools = _tools(g, T)
    B, new, need, inc, ts, cp, tt, counters, blocks, sums, gather, close, ones, iota = tools

    tk, txs = new(), [new() for _ in XB[1:]]
    for q, a in ((Y, 0), (S, 64)):
        for h in range(a, a + 64, 16):
            inc(q.dma_start(T.ki[h:h + 16, :], T.key[:]), tk, 16)
    for a, b, t in zip(XB, XB[1:], txs):
        inc(Y.dma_start(T.xin[:, a:b], T.x[:, a:b]), t, 16)

    def copy(i):
        need("g", [txs[i]])
        _send(g, topo, T.xin[:, XB[i]:XB[i + 1]], hc, every, T.sem.xa, T.sem.tsent)

    r16, rkk, rcc, rp = counters()
    ij = iota("jcol", [[1, 16]], 16)
    copy(0)
    c2, c6 = new(), new()
    need("v", [r16])
    ts(B("selv"), B("c16b"), B("vcol"), OP.is_equal, c2)
    need("v", [rkk, rcc])
    blocks(c6)
    need("v", [rp])
    ts(B("le"), B("ccb"), B("pf"), OP.is_le, c6, -1.0, OP.mult)

    need("v", [tk])
    a3, a4 = new(), new()
    for h in range(2):
        ts(B("oh", h * 128, h * 128 + 128), T.ki[:], B("kcol", h, h + 1), OP.is_equal, a3)
    need("v", [c6])
    c6b = tt(B("lb"), B("le"), B("bo"), OP.mult, new())
    need("v", [a3])
    for h in range(2):
        o = B("oh", h * 128, h * 128 + 128)
        inc(V.tensor_tensor_scan(B("fs", h * 128, h * 128 + 128), o, o, 0.0, OP.add, OP.max), a4)
    c3 = new()
    for h, te in enumerate(("te0", "te1")):
        ts(B(te, 0, 128), B("c16b"), B("kcol", h, h + 1), OP.is_ge, c3)
        ts(B(te, 128, 256), B("c16b"), B("kcol", h, h + 1), OP.is_gt, c3)
    cnt = [B("fs", 127, 128), B("fs", 255, 256)]

    need("t", [a4, c6, c6b, c2])
    P.matmul(T.b1[:, 0:256], B("bo"), B("fs"), True, False)
    d1 = inc(P.matmul(T.b1[:, 0:256], B("lb"), B("oh"), False, True), new())
    P.matmul(T.b2[:, 0:1], B("gt"), cnt[0], True, True)
    P.matmul(T.b2[:, 1:2], B("onh"), cnt[0], True, False)
    d2 = inc(P.matmul(T.b2[:, 1:2], B("gt"), cnt[1], False, True), new())
    need("t", [c3])
    P.matmul(T.b5[0:1, 0:256], cnt[0], B("te0"), True, False)
    a5 = inc(P.matmul(T.b5[0:1, 0:256], cnt[1], B("te1"), False, True), new())
    need("v", [d1])
    d3 = tt(B("mk"), T.b1[:, 0:256], B("oh"), OP.mult, new())
    need("v", [d2, c2])
    s16 = B("selv", 0, 16)
    for h in range(2):
        ts(B("sbase", h * 16, h * 16 + 16), s16, T.b2[:, h:h + 1], OP.mult, d3)
    need("t", [d3])
    P.matmul(T.b3[:, 0:16], B("mk", 0, 128), s16, True, False)
    P.matmul(T.b3[:, 0:16], B("mk", 128, 256), s16, False, False)
    P.matmul(T.b3[:, 0:16], B("oh", 0, 128), B("sbase", 0, 16), False, False)
    d4 = inc(P.matmul(T.b3[:, 0:16], B("oh", 128, 256), B("sbase", 16, 32), False, True), new())
    need("v", [a5])
    a6 = cp(T.erow[0:1, :], T.b5[0:1, 0:256], new())
    need("y", [a6])
    a7 = inc(Y.dma_start(T.ed[r], T.erow[0:1, :]), new(), 16)
    need("g", [a7])
    g.remote_dma_fused([_tr(topo, T.ed[r], T.ed[r], fars, lo, T.sem.earr),
                        _tr(topo, T.ed[r], T.ed[r], [ls[ci]], hi, T.sem.earr)], local_sem=T.sem.esent)
    copy(1)
    need("v", [d4])
    d5 = ts(B("posi"), T.b3[:, 0:16], float(W + 1), OP.mult, new())
    need("v", [d5])
    d6 = new()
    ts(B("lh", 0, 16), B("posi"), 4, OP.arith_shift_right, d6, 15, OP.bitwise_and)
    ts(B("lh", 16, 32), B("posi"), 8, OP.arith_shift_right, d6, 127, OP.bitwise_and)
    need("v", [d6])
    d7 = cp(B("lhf"), B("lh"), new())
    need("v", [d7, ij])
    need("s", [d7, r16])
    n0 = 128 * (16 - VS)
    w1 = new()
    for v in range(VS, 16):
        o = (v - VS) * 128
        inc(S.activation(B("lab", o, o + 128), B("c16b"), AF.Abs, bias=B("lhf", v, v + 1), scale=-1.0), w1)
    need("s", [w1])
    w2 = inc(S.activation(B("lqs", 0, n0), B("lab", 0, n0), AF.Relu, bias=1.0, scale=-1.0), new())
    for b in range(4):
        d8 = new()
        for v in range(4 * b, 4 * b + 4):
            if v < VS:
                ts(B("lq", v * 128, v * 128 + 128), B("c16b"), B("lhf", v, v + 1), OP.is_equal, d8)
            ts(B("rq", v * 128, v * 128 + 128), B("ccb"), B("lhf", 16 + v, 17 + v), OP.is_equal, d8,
               B("jcol", v, v + 1), OP.mult)
        need("t", [d8])
        for v in range(4 * b, 4 * b + 4):
            if v < VS:
                lq = B("lq", v * 128, v * 128 + 128)
            else:
                need("t", [w2])
                lq = B("lqs", (v - VS) * 128, (v - VS) * 128 + 128)
            m = P.matmul(T.b4[:, 0:128], lq, B("rq", v * 128, v * 128 + 128), v == 0, v == 15)
    d9 = inc(m, new())
    need("v", [d9])
    f1 = cp(T.gl[:], T.b4[:, 0:128], new())

    need("g", [f1])
    _send(g, topo, T.gl[:], hc, every, T.sem.la, T.sem.tsent)
    sent = _deal(g, T, topo, r, _legs(ci)[0], main, tools, [f1] + txs, lo2)
    u = 2 * ci
    part = gather("s", [], T.p1[:, u * S1:(u + 2) * S1], T.xin[:, 0:W], T.gl[:, 8 * u:8 * u + 16])
    if first:
        mine = gather("v", [], T.xl[:, r * S1:(r + 1) * S1], T.xin[:, 0:W], T.gl[:, 8 * u:8 * u + 8])
    need("g", [part])
    tr = [_tr(topo, T.p1[:, (u + x) * S1:(u + x + 1) * S1], T.xl[:, r * S1:(r + 1) * S1], [main[ci][x]], hi2[x],
              T.sem.a1) for x in range(2) if main[ci][x] != core]
    g.remote_dma_fused(tr, local_sem=T.sem.sent)
    sent += 4 * len(tr)

    if first:
        for q in (V, S):
            q.wait_ge(T.sem.ila, 16)
            q.wait_ge(T.sem.a1, 4 * (N - 1))
        s2, home = _meet(g, T, topo, core, u, ci, rk, mate, fwd, own, tools, [mine], lo2, hi2)
        sent += s2
        deps = [home]
        for q in (V, S):
            q.wait_ge(T.sem.ola, 8)
    else:
        for q in (V, P):
            q.wait_ge(T.sem.tabh, 32)
        P.wait_ge(T.sem.elr, 16)
        _counts(g, T, tools, [a6])
        deps = [_rlist(g, T, tools, r, u + 1)]
        sent += _neighbour(g, T, topo, u, rk, fwd, lo2)

    total = 4 * (NU - 1) if first else 4 * NU
    V.wait_ge(T.sem.arr, total)
    S.wait_ge(T.sem.arr, total)
    ty = new()
    for n, a, b in (("v", 0, 384), ("s", 384, 768), ("v", 768, 1280), ("s", 1280, 1664), ("v", 1664, 1856),
                    ("s", 1856, W)):
        t = gather(n, deps, T.yb[:, a:b], T.land[:, 0:NU * S2], T.ol[:, a // 16:b // 16])
        need("y", [t])
        inc(Y.dma_start(T.y[:, a:b], T.yb[:, a:b]), ty, 16)
    need("y", [ty])
    g.wait_ge(T.sem.tsent, 16 * len(XB))
    g.wait_ge(T.sem.esent, 16)
    g.wait_ge(T.sem.sent, sent)
    close()
